import numpy as np, ml_dtypes
CORES = [2,6,10,14,18,22,26,30]
N = 8
BF = ml_dtypes.bfloat16
def gentries(a):
    return np.ascontiguousarray(a.reshape(8, 16, -1).transpose(0, 2, 1)).reshape(8, -1)
def gtable(e):
    e = np.asarray(e); return np.ascontiguousarray(e.reshape(8, -1, 16).transpose(0, 2, 1)).reshape(128, -1).astype(np.int32)
W, K, NK, RO = 2048, 512, 2, 3
def sign(rng, *shape):
    return (2 * rng.integers(0, 2, shape) - 1).astype(np.float32)
def unit(rng, *shape):
    return rng.random(shape, dtype=np.float32)
def parts(rng, lo=-1, hi=0, gap=0.3):
    col = np.exp2(rng.integers(lo, hi + 1, (N, 8, 1, W))).astype(np.float32) * (unit(rng, N, 8, 1, W) >= gap)
    b = sign(rng, N, 8, 16, W) * (np.float32(0.75) + np.float32(0.5) * unit(rng, N, 8, 16, W)) * col
    w = sign(rng, N, 8, 16, W) * (np.float32(0.25) + np.float32(0.25) * unit(rng, N, 8, 16, W))
    rec = np.float32(0.25) + np.float32(0.75) * unit(rng, N, 8, 16, W)
    t = np.exp2(rng.integers(-8, -3, (N, 8, 1, 1))) * (0.7 + 0.6 * rng.random((N, 8, 16, 1)))
    p = np.argsort(rng.random((N, 8, NK + 2, W)), axis=-1)
    d = np.ascontiguousarray(np.argsort(rng.random((N, 8, W)), axis=-1)[..., :K])
    return b, w, rec, t, p, d
def pack(b, w, rec, t, p, d):
    return {"b0": b.reshape(N, 128, W).astype(BF), "w": w.reshape(N, 128, W).astype(BF), "rec": rec.reshape(N, 128, W).astype(BF), "th": t.reshape(N, 128, 1).astype(np.float32),
            "hop": np.ascontiguousarray(p[:, :, :NK].reshape(N, 8, NK * W)).astype(np.int32), "up": np.ascontiguousarray(p[:, :, NK]).astype(np.int32),
            "dn": np.ascontiguousarray(p[:, :, NK + 1]).astype(np.int32), "wk": np.stack([gtable(a) for a in d])}
def rest(rng, d):
    m = np.ones(W, bool); m[d] = False
    return rng.permutation(np.flatnonzero(m))
def goal(q, g, i):
    return (q, g) if i < NK else ((q + 1) % N, (g + 1) % 8) if i == NK else ((q - 1) % N, g)
def route(rng, d, y, shut, src=(), dst=()):
    y = y.copy(); f = y < 0; ok = ~shut; ok[y[~f]] = False
    y[f] = rng.permutation(np.flatnonzero(ok))[:np.count_nonzero(f)]
    d = np.concatenate([d, np.asarray(src, np.int64)]); y = np.concatenate([y, np.asarray(dst, np.int64)])
    p = np.zeros(W, np.int64); p[d] = y; a = np.ones(W, bool); a[d] = False; v = np.ones(W, bool); v[y] = False
    p[a] = rng.permutation(np.flatnonzero(v))
    return p
def odd(rng, *shape):
    return (2 * rng.integers(65, 127, shape) + 1).astype(np.float32)
def choose(ok, *v):
    i = np.argmax(ok, axis=0)[None]
    return [np.take_along_axis(a, i, 0)[0] for a in v]
def setup_inputs(rng):
    return pack(*parts(rng))
def setup_inputs_spread(rng):
    b, w, rec, t, p, d = parts(rng, -1, 1)
    w = sign(rng, N, 8, 16, W) * np.exp2(-4 + 3 * unit(rng, N, 8, 16, W)); rec = 0.0625 + 0.9375 * unit(rng, N, 8, 16, W)
    t = np.exp2(-11 + 9 * rng.random((N, 8, 16, 1)))
    return pack(b, w, rec, t, p, d)
def setup_inputs_ends(rng):
    M = K // 4; h = K // 2; s = sign(rng, 16)[:, None]; j = np.arange(M)
    size = rng.choice(np.array([64.0, 64.0, 2.0 ** -20, 0.0]), (N, 8, 1, W)).astype(np.float32)
    b = sign(rng, N, 8, 16, W) * size
    w = sign(rng, N, 8, 16, W) * rng.choice(np.array([0.5, 0.0625]), (N, 8, 1, W)).astype(np.float32)
    rec = np.where(unit(rng, N, 8, 16, W) < 0.5, np.float32(1), np.float32(0.0625))
    t = np.zeros((N, 8, 16, 1)); p = np.zeros((N, 8, NK + 2, W), np.int64); d = np.zeros((N, 8, K), np.int64); x = np.zeros((N, 8, 3, M), np.int64)
    for q in range(N):
        for g in range(8):
            d[q, g] = rng.permutation(np.concatenate([np.arange(h), W - h - g % 2 + np.arange(h)]))
            r = rest(rng, d[q, g]); r = r[np.argsort(r != W - 1, kind="stable")][:3 * M].reshape(3, M)
            x[q, g] = r if g % 4 == 3 else r[::-1]
            a = d[q, g, K - M:]; b[q, g][:, a] = 64 * s; w[q, g][:, a] = 0.5; rec[q, g][:, a] = 1
            b[q, g][:, x[q, g, 0]] = s * np.array([-64.0, 0.0, 64.0])[j % 3]
            b[q, g][:, x[q, g, 1]] = s * np.array([64.0, 0.0, 64.0])[j % 3]
            b[q, g][:, x[q, g, 2]] = -s * np.array([64.0, 0.0, 64.0, 63.75, 0.0, 64.0])[j % 6]
            xx = x[q, g].reshape(-1); w[q, g][:, xx] = 0.5; rec[q, g][:, xx] = 1
            n = (9, 16, 8, 10, 9, 12, 9, 16)[(g + q) % 8]
            t[q, g, :, 0] = np.where(rng.permutation(16) < n, 2.0 ** -20, 64.0)
    for q in range(N):
        for g in range(8):
            for i in range(NK + 2):
                xx = x[goal(q, g, i)]; y = np.full(K, -1); y[K - M:] = xx[0]; shut = np.zeros(W, bool); shut[xx.reshape(-1)] = True
                p[q, g, i] = route(rng, d[q, g], y, shut, x[q, g, :2].reshape(-1), xx[1:].reshape(-1))
    return pack(b, w, rec, t, p, d)
def setup_inputs_corners(rng):
    b, w, rec, t, p, d = parts(rng, 0, 0, 0.1); M = K // 2; L = K // 8; U = K // 16; e = np.float32(2.0 ** -9); e1 = np.float32(2.0 ** -8)
    x = np.zeros((N, 8, NK, M), np.int64); z = np.zeros((N, 8, 3, L), np.int64); xn = np.zeros((N, 8, 2, U), np.int64); shut = np.zeros((N, 8, W), bool)
    kind = (np.arange(N)[:, None] + np.arange(8)[None, :]) % 8; need = np.array([8, 9, 8, 9, 7, 10, 0, 16])[kind]
    late = (kind == 2) | (kind == 3); low = (need < 9)[:, :, None]
    tb = odd(rng, 64, N, 8, 16) * e1; tr = odd(rng, 64, N, 8, 16) * e1; tw = odd(rng, 64, N, 8, 16) * e; xw = odd(rng, 64, N, 8, 16) * e
    h = (tb * tr) * tw; top = h.astype(BF).astype(np.float32); h2 = top + (h - top).astype(BF).astype(np.float32)
    tb, tr, tw, xw = choose(np.where(low, h2 * xw > h * xw, h2 * xw < h * xw), tb, tr, tw, xw)
    gm = ((tb * tr) * tw) * xw
    yv = odd(rng, 256, N, 8, 16) * e1; yr = odd(rng, 256, N, 8, 16) * e1; zw = odd(rng, 256, N, 8, 16) * e; b2 = yv
    for k in range(NK): b2 = b2 + gm
    dl = b2 * yr; g2 = (xw * dl) * zw; g3 = dl * (xw * zw); g4 = (b2 * (yr * xw)) * zw
    yv, yr, zw, g2 = choose(np.where(low, (g3 > g2) & (g4 > g2), (g3 < g2) & (g4 < g2)), yv, yr, zw, g2)
    for q in range(N):
        for g in range(8):
            r = rest(rng, d[q, g]); xn[q, g] = r[:2 * U].reshape(2, U); r = r[2 * U:]
            for i in range(2):
                to = goal(q, g, NK + i); a = d[q, g, 8 + i * U:8 + (i + 1) * U]
                b[q, g][:, a] = tb[to][:, None] * sign(rng, 16, U); rec[q, g][:, a] = tr[to][:, None]; w[q, g][:, a] = tw[to][:, None] * sign(rng, 16, U)
            xx = xn[q, g].reshape(-1); b[q, g][:, xx] = 0; w[q, g][:, xx] = xw[q, g][:, None] * sign(rng, 16, 2 * U); shut[q, g, xx] = True
            n = int(need[q, g]); o = rng.permutation(16); gl = g2[q, g] if late[q, g] else gm[q, g]
            t[q, g, :, 0] = gl; t[q, g, o[:n], 0] = np.nextafter(gl[o[:n]], np.float32(0))
            if late[q, g]:
                z[q, g] = r[:3 * L].reshape(3, L); shut[q, g, r[:3 * L]] = True; sb = sign(rng, 16, L); sw = sign(rng, 16, L); sy = sign(rng, 16, L)
                a = d[q, g, K - L:]; b[q, g][:, a] = tb[q, g][:, None] * sb; rec[q, g][:, a] = tr[q, g][:, None]; w[q, g][:, a] = tw[q, g][:, None] * sw
                a = z[q, g, 0]; b[q, g][:, a] = -sb * sw * sy * yv[q, g][:, None]; rec[q, g][:, a] = yr[q, g][:, None]; w[q, g][:, a] = xw[q, g][:, None] * sy
                a = z[q, g, 1]; b[q, g][:, a] = 0; w[q, g][:, a] = zw[q, g][:, None] * sign(rng, 16, L)
                v = zw[q, g][:, None] * sign(rng, 16, L); ab = odd(rng, 16, L) * np.float32(2.0 ** -22) * sign(rng, 16, L); ar = odd(rng, 16, L) * e1; aw = odd(rng, 16, L) * e * sign(rng, 16, L)
                a = d[q, g, K - 2 * L:K - L]; b[q, g][:, a] = ab; rec[q, g][:, a] = ar; w[q, g][:, a] = aw
                a = z[q, g, 2]; w[q, g][:, a] = v; b[q, g][:, a] = (((ab * ar) * aw) * v).astype(BF).astype(np.float32)
                continue
            x[q, g] = r[:NK * M].reshape(NK, M); a = d[q, g, K - M:]
            b[q, g][:, a] = tb[q, g][:, None] * sign(rng, 16, M); rec[q, g][:, a] = tr[q, g][:, None]; w[q, g][:, a] = tw[q, g][:, None] * sign(rng, 16, M)
            xx = x[q, g].reshape(-1); v = np.repeat(xw[q, g][:, None], xx.size, axis=1); u = rng.integers(0, 5, xx.size); b[q, g][:, xx] = 0; shut[q, g, xx] = True
            if n > 0:
                j = np.flatnonzero(u == 1); v[o[rng.integers(0, n, j.size)], j] -= e
            if n < 16:
                j = np.flatnonzero(u == 2); v[o[rng.integers(n, 16, j.size)], j] += e
            j = np.flatnonzero(u == 3); b[q, g][rng.integers(0, 16, j.size), xx[j]] = np.float32(2.0 ** -20) * sign(rng, j.size)
            w[q, g][:, xx] = v * sign(rng, 16, xx.size)
    for q in range(N):
        for g in range(8):
            for i in range(NK + 2):
                y = np.full(K, -1); to = goal(q, g, i); src = np.zeros(0, np.int64); dst = src
                if i >= NK: y[8 + (i - NK) * U:8 + (i - NK + 1) * U] = xn[to][i - NK]
                elif late[q, g]:
                    y[K - L:] = z[q, g, 0]
                    if i == 0: y[K - 2 * L:K - L] = z[q, g, 2]
                    if i < 2: src = z[q, g, 0]; dst = z[q, g, 1 + i]
                else: y[K - M:] = x[q, g, i]
                if i == 0: y[:8] = d[q, g, :8]
                p[q, g, i] = route(rng, d[q, g], y, shut[to], src, dst)
    return pack(b, w, rec, t, p, d)
def setup_inputs_crowd(rng):
    b, w, rec, t, p, d = parts(rng, -1, -1); T = K // (2 * NK); M = K // 4
    x = np.zeros((N, 8, NK, M), np.int64); c = np.zeros((N, 8, T), np.int64); e = np.float32(2.0 ** -9)
    for q in range(N):
        for g in range(8):
            r = rest(rng, d[q, g]); c[q, g] = r[:T]; x[q, g] = r[T:T + NK * M].reshape(NK, M)
            m = d[q, g, :NK * T]; b[q, g][:, m] = sign(rng, 16, NK * T) * (0.75 + 0.5 * unit(rng, 16, NK * T))
            b[q, g][:, c[q, g]] = 2 * sign(rng, 16, T); rec[q, g][:, c[q, g]] = 0.5 + 0.25 * unit(rng, 16, T)
            j = np.arange(2, T, 3); b[q, g][rng.integers(0, 16, j.size), c[q, g, j]] = 0
            a = d[q, g, K - M:]; sb = sign(rng, 16, M); sw = sign(rng, 16, M)
            b[q, g][:, a] = sb * odd(rng, 16, M) * np.float32(2.0 ** -17); w[q, g][:, a] = sw * odd(rng, 16, M) * e; rec[q, g][:, a] = 0.5 + 0.5 * unit(rng, 16, M)
            o = np.argsort(rng.random((NK, 16, M)), axis=0)
            for k in range(NK):
                sx = sign(rng, 16, M); b[q, g][:, x[q, g, k]] = sx
                w[q, g][:, x[q, g, k]] = -sb * sw * sx * (200 + o[k]).astype(np.float32) * e
    for q in range(N):
        for g in range(8):
            for i in range(NK + 2):
                y = np.full(K, -1); shut = np.zeros(W, bool); z = goal(q, g, i); shut[x[z].reshape(-1)] = True; shut[c[z]] = True
                if i < NK:
                    y[i * T:(i + 1) * T] = np.where((np.arange(T) % 3 == 1) & (i == 0), -1, c[q, g]); y[K - M:] = x[q, g, i]
                p[q, g, i] = route(rng, d[q, g], y, shut)
    return pack(b, w, rec, t, p, d)
def setup_inputs_level(rng):
    b, w, rec, t, p, d = parts(rng)
    s = np.where(unit(rng, N, 8, 1, W) < 0.25, sign(rng, N, 8, 16, W), sign(rng, 1, 1, 16, 1) * sign(rng, N, 8, 1, W))
    b = s * np.exp2(rng.integers(-1, 1, (N, 8, 1, W))) * (unit(rng, N, 8, 1, W) >= 0.3)
    w = sign(rng, N, 8, 1, W) * np.exp2(rng.integers(-2, 0, (N, 8, 1, W))) + np.zeros((N, 8, 16, W))
    rec = np.exp2(rng.integers(-1, 1, (N, 8, 1, W))) + np.zeros((N, 8, 16, W))
    e = rng.integers(-6, -2, (N, 8, 1, 1)).astype(np.float64); n = rng.integers(8, 10, (N, 8, 1, 1))
    t = np.where(np.argsort(rng.random((N, 8, 16, 1)), axis=2) < n, np.exp2(e - 1), np.exp2(e))
    return pack(b, w, rec, t, p, d)
def check_ranges(d):
    bad = []
    for k in ("hop", "up", "dn", "wk"):
        if np.min(d[k]) < 0 or np.max(d[k]) > W - 1: bad.append("range of " + k)
    for k in ("hop", "up", "dn"):
        if np.any(np.sort(np.asarray(d[k]).reshape(N, 8, -1, W), axis=-1) != np.arange(W)): bad.append(k + " is no permutation")
    e = np.sort(np.stack([gentries(np.asarray(a)) for a in d["wk"]]), axis=-1)
    if np.any(e[..., 1:] == e[..., :-1]): bad.append("wk names a place twice in a group")
    a = np.abs(np.asarray(d["b0"]).astype(np.float32))
    if not np.all((a == 0) | ((a >= 2.0 ** -20) & (a <= 64))): bad.append("range of b0")
    a = np.abs(np.asarray(d["w"]).astype(np.float32))
    if not np.all((a >= 0.0625) & (a <= 0.5)): bad.append("range of w")
    a = np.asarray(d["rec"]).astype(np.float32)
    if not np.all((a >= 0.0625) & (a <= 1)): bad.append("range of rec")
    a = np.asarray(d["th"]).astype(np.float32)
    if not np.all((a >= 2.0 ** -20) & (a <= 64)): bad.append("range of th")
    return bad
def pick(a, ix):
    return np.take_along_axis(a, ix[:, :, None, :], 3)
def place(a, ix, v):
    np.put_along_axis(a, ix[:, :, None, :], v, 3)
def arrive(b, wf, t, x, h):
    g = h * pick(wf, x); o = pick(b, x)
    new = np.all(o == 0, axis=2, keepdims=True); few = np.sum(np.abs(g) > t, axis=2, keepdims=True) < 9
    place(b, x, np.where(new & few, o, o + g))
def reference(b0, w, rec, th, hop, up, dn, wk):
    b = b0.astype(np.float32).reshape(N, 8, 16, W).copy(); wf = w.astype(np.float32).reshape(N, 8, 16, W); rf = rec.astype(np.float32).reshape(N, 8, 16, W)
    t = th.astype(np.float32).reshape(N, 8, 16, 1); hp = hop.astype(np.int64).reshape(N, 8, NK, W); ul = up.astype(np.int64); dl = dn.astype(np.int64)
    d = np.stack([gentries(a) for a in wk]).astype(np.int64); c = np.zeros((N, 8, 16, W), np.float32)
    for s in range(RO):
        delta = -(pick(b, d) * pick(rf, d))
        place(c, d, pick(c, d) + delta); place(b, d, np.float32(0))
        h = pick(wf, d) * delta
        xs = [np.take_along_axis(hp[:, :, k], d, 2) for k in range(NK)]
        for x in xs: arrive(b, wf, t, x, h)
        x = np.take_along_axis(ul, d, 2); arrive(b, wf, t, np.roll(x, (1, 1), (0, 1)), np.roll(h, (1, 1), (0, 1)))
        x = np.take_along_axis(dl, d, 2); arrive(b, wf, t, np.roll(x, -1, 0), np.roll(h, -1, 0))
        if s == RO - 1: break
        m = np.stack([np.abs(pick(b, x)) for x in xs])
        votes = np.sum(m == np.max(m, axis=0), axis=3)
        ch = np.argmax(votes, axis=0)
        to = np.take_along_axis(np.stack(xs), ch[None], 0)[0]
        held = np.zeros((N, 8, W), bool); np.put_along_axis(held, d, True, 2)
        first = np.full((N, 8, W), NK)
        for k in range(NK - 1, -1, -1):
            qq, gg, jj = np.nonzero(ch == k); first[qq, gg, to[qq, gg, jj]] = k
        go = ~np.take_along_axis(held, to, 2) & (np.take_along_axis(first, to, 2) == ch)
        d = np.where(go, to, d)
    return {"yb": b.reshape(N, 128, W), "yc": c.reshape(N, 128, W)}

def check_inputs(d):
    bad = list(check_ranges(d))
    if not bad:
        for name, y in reference(**d).items():
            for q in range(N):
                v = np.abs(np.asarray(y[q], np.float64)); s = np.sqrt(np.mean(v * v))
                if v.max() > 9 * s or s < 2.0 ** -3: bad.append('%s of rank %d is uneven or too small' % (name, q))
    return bad

@@ -1,0 +1,322 @@
+from concourse.mybir import AluOpType as ALU, ActivationFunctionType as AF
+
+W, K, RO = 2048, 512, 3
+F32, BF, F16, I32, U16 = "float32", "bfloat16", "float16", "int32", "uint16"
+SCRATCH = {
+    "b": ("sbuf", [128, W], F32), "c": ("sbuf", [128, W], F32), "m0": ("sbuf", [128, W], F32), "m1": ("sbuf", [128, W], F32),
+    "tw": ("sbuf", [128, W], I32), "bh": ("sbuf", [128, W], BF), "wb": ("sbuf", [128, W], BF), "rb": ("sbuf", [128, W], BF),
+    "nth": ("sbuf", [128, 1], F32), "ths": ("sbuf", [128, 1], F32), "wki": ("sbuf", [128, 32], I32),
+    "zero": ("sbuf", [128, K], F32), "held": ("sbuf", [128, K], F32), "jc": ("sbuf", [128, K], F32), "jlo": ("sbuf", [128, 32], F32),
+    "zc": ("sbuf", [128, 176], BF),
+    "zi": ("sbuf", [128, 32], I32), "zj": ("sbuf", [128, 32], I32), "za": ("sbuf", [128, 16], F32),
+    "bi": ("sbuf", [128, 128], I32), "bj": ("sbuf", [128, 128], I32),
+    "zt": ("sbuf", [128, 528], F16), "zb": ("sbuf", [128, 144], BF), "ones": ("sbuf", [128, 128], BF),
+    "nb": ("sbuf", [128, K], F32), "dl": ("sbuf", [128, K], F32), "cd": ("sbuf", [128, K], F32), "tg": ("sbuf", [128, K], F16),
+    "ab0": ("sbuf", [128, K], F32), "ab1": ("sbuf", [128, K], F32), "big0": ("sbuf", [128, K], BF), "big1": ("sbuf", [128, K], BF),
+    "rl": ("sbuf", [128, K], BF), "ao": ("sbuf", [128, K], BF), "acc": ("sbuf", [128, K], F32), "tt": ("sbuf", [128, K], F32),
+    "mg": ("sbuf", [128, 2 * K], BF), "wv": ("sbuf", [128, 560], BF), "wg": ("sbuf", [128, K], BF), "sg": ("sbuf", [128, K], BF),
+    "ee": ("sbuf", [128, 64], F32), "sm": ("sbuf", [128, 256], F32), "lk": ("sbuf", [128, 32], U16),
+    "land": ("dram", [RO, 128, K], F32),
+    "pc0": ("psum", [128, K], F32), "pc1": ("psum", [128, K], F32), "ps": ("psum", [128, K], F32), "px0": ("psum", [128, K], F32),
+    "px1": ("psum", [128, K], F32), "pxu": ("psum", [128, K], F32), "pl": ("psum", [128, K], F32), "pa": ("psum", [128, K], F32),
+}
+for _k in range(4):
+    SCRATCH["g%d" % _k] = ("sbuf", [128, K], F32)
+for _s in range(RO):
+    for _n in ("h", "hu", "hd"):
+        SCRATCH["%s%d" % (_n, _s)] = ("sbuf", [128, K], F32)
+    SCRATCH["xl%d" % _s] = ("sbuf", [128, 128], U16)
+    SCRATCH["df%d" % _s] = ("sbuf", [128, 32], F32)
+    for _n in ("dq", "ul", "nl"):
+        SCRATCH["%s%d" % (_n, _s)] = ("sbuf", [128, 32], U16)
+LOADS = ["wki", "bh", "rb", "wb", "tw", "ths", "jc", "yb", "yc"]
+SEMAPHORES = (["qv", "qa", "qp", "qg", "sent"] + ["d_" + n for n in LOADS] + ["d_hd%d" % s for s in range(RO)]
+              + ["r_%s%d" % (n, s) for n in ("hu", "ul", "land", "nl") for s in range(RO)])
+OPT = dict(ld=1, cw=1408, cb=1152, half=(0, 3), half3=(0, 3), act=(), act3=(), tb0=1, m1=22, m2=44, lead=1, s1=0, c3=2, p4=1)
+PSUM = ("pc0", "pc1", "ps", "px0", "px1", "pxu", "pl", "pa")
+
+
+def emit(g, T, ops):
+    Q = {"v": g.vector, "a": g.scalar, "p": g.tensor, "g": g, "s": g.sync}
+    lastw = {}; readers = {}
+    for i, o in enumerate(ops):
+        dep = set()
+        for r in o["r"]:
+            if r in lastw: dep.add(lastw[r])
+            if r in PSUM: dep.update(j for j in readers.get(r, ()) if ops[j]["q"] != o["q"])
+        for r in o["w"]:
+            for j in ([lastw[r]] if r in lastw else []) + list(readers.get(r, ())):
+                if ops[j]["q"] != o["q"] or ops[j]["sem"] or o["q"] != "p": dep.add(j)
+        twins = [j for j in dep if ops[j]["sem"] and ops[j]["sem"] == o["sem"]]
+        o["dep"] = [j for j in dep if j not in twins] + [x for j in twins for x in ops[j]["dep"]]
+        for r in o["r"]: readers.setdefault(r, []).append(i)
+        for r in o["w"]:
+            same = r in lastw and o["sem"] and ops[lastw[r]]["sem"] == o["sem"]
+            lastw[r] = i
+            if not same: readers[r] = []
+    known = {}; need = set(); final = {}
+    for i, o in enumerate(ops):
+        if o["sem"]: final[o["sem"]] = i
+    for i, o in enumerate(ops):
+        kn = known.setdefault(o["q"], {}); o["wait"] = []
+        for j in sorted(o["dep"], reverse=True):
+            key = ops[j]["sem"] or "q" + ops[j]["q"]
+            if kn.get(key, -1) >= j: continue
+            o["wait"].append(j); need.add(j)
+            for x, v in ops[j]["kn"].items(): kn[x] = max(kn.get(x, -1), v)
+            kn[key] = max(kn.get(key, -1), final[key] if ops[j]["sem"] else j)
+        o["kn"] = dict(kn)
+    total = {}; count = {}
+    for i, o in enumerate(ops):
+        if o["sem"]: total[o["sem"]] = total.get(o["sem"], 0) + o["n"]
+        elif i in need:
+            count[o["q"]] = count.get(o["q"], 0) + 1; o["at"] = count[o["q"]]
+    waited = {}
+    for i, o in enumerate(ops):
+        for j in o["wait"]:
+            p = ops[j]; s, v = (p["sem"], total[p["sem"]]) if p["sem"] else ("q" + p["q"], p["at"])
+            Q[o["q"]].wait_ge(T.sem[s], v); waited[s] = max(waited.get(s, 0), v)
+        if not o["f"]: continue
+        ins = o["f"]()
+        if o["sem"] and o["inc"]: ins.then_inc(T.sem[o["sem"]], o["n"])
+        elif "at" in o: ins.then_inc(T.sem["q" + o["q"]], 1)
+    for s, v in sorted(total.items()):
+        if waited.get(s, 0) < v: (g if s == "sent" else g.sync).wait_ge(T.sem[s], v)
+
+
+def rank_program(g, core, T, topo):
+    rank = T.rank_of(core)
+    if rank is None:
+        return
+    n = len(T.cores); up = T.cores[(rank + 1) % n]; dn = T.cores[(rank - 1) % n]
+    V, A, P = g.vector, g.scalar, g.tensor
+    ops = []
+
+    def op(q, f, r=(), w=(), sem=None, cnt=16, inc=True):
+        r, w = ([y for x in z for y in ([x + "h0", x + "h1"] if x in ("ab0", "big0", "rl") else [x])] for z in (r, w))
+        ops.append({"q": q, "f": f, "r": r, "w": w, "sem": sem, "n": cnt, "inc": inc})
+
+    def engines(src, dst):
+        rk = T.rank_of(src); both = [T.cores[(rk + 1) % n], T.cores[(rk - 1) % n]]
+        far = [e for c in both if topo.chip(c) != topo.chip(src) for e in topo.engines(src, c)]
+        e = topo.engines(src, dst)
+        return e if topo.chip(src) != topo.chip(dst) else [x for x in e if x not in far]
+
+    def send(dst, name, out, src, r):
+        e = engines(core, dst); rid, pid = topo.addr(dst)[:2]; m = sum(1 << x for x in e)
+        op("g", lambda: g.remote_dma(out, src, T.sem["r_" + name], T.sem.sent, pid, rid, m), r=r, sem="sent", cnt=len(e), inc=False)
+
+    def arrives(src, name):
+        op("r", None, w=[name], sem="r_" + name, cnt=len(engines(src, core)))
+
+    cut = 128 - 16 * rank
+
+    def dma(q, out, in_, sem, r=(), w=()):
+        op(q, lambda: (g.sync if q == "s" else g.scalar).dma_start(out, in_), r=r, w=w, sem="d_" + sem)
+
+    def load(q, name, src):
+        dma(q, T[name][0:cut, :], src[128 - cut:128, :], name, w=[name])
+        if rank: dma(q, T[name][cut:128, :], src[0:128 - cut, :], name, w=[name])
+
+    def store(q, name, dst, a=0, e=W):
+        dma(q, T[dst][128 - cut:128, a:e], T[name][0:cut, a:e], dst, r=[name])
+        if rank: dma(q, T[dst][0:128 - cut, a:e], T[name][cut:128, a:e], dst, r=[name])
+
+    def ind(win, lst):
+        return T[win][:, :].indirect(lst)
+
+    def tt(out, a, b, o, r, w): op("v", lambda: V.tensor_tensor(out, a, b, o), r, w)
+    def ts(out, a, s, o, r, w): op("v", lambda: V.tensor_scalar(out, a, s, None, o), r, w)
+    def cp(out, a, r, w): op("v", lambda: V.tensor_copy(out, a), r, w)
+    def ms(out, v, w): op("v", lambda: V.memset(out, v), (), w)
+    def act(out, a, f, r, w, **kw): op("a", lambda: A.activation(out, a, f, **kw), r, w)
+    def iota(out, pat, base, cm, w, **kw): op("g", lambda: g.iota(out, pat, base, cm, **kw), (), w)
+    def mm(out, l, x, st, sp, r, w): op("p", lambda: P.matmul(out, l, x, st, sp), r, w)
+
+    def tolist(bank, col, z, zoff, src, cols, lift=False):
+        def f():
+            for i in range(16):
+                o = zoff + 15 - i
+                ins = P.matmul(T[bank][:, col:col + cols // 16], T[z][:, o:o + 128], T[src][:, i:cols:16], i == 0 and not lift, i == 15)
+            return ins
+        if lift: mm(T[bank][:, col:col + 32], T.ones[:, :], T.zc[:, 144:176], True, False, ["ones", "zc1"], [bank])
+        op("p", f, [z, src], [bank])
+
+    fl = {"allow_small_or_imprecise_dtypes": True}
+    cw = OPT["cw"]
+    ms(T.tw[:, 0:cw], 0, ["tw"])
+    iota(T.zi[:, :], [[-4, 4], [-16, 8]], 132, 1, ["zi"])
+    if cw < W: iota(T.tw[:, cw:W], [[0, W - cw]], 0, 0, ["tw1"])
+    load("a", "wki", T.wk); load("s", "bh", T.b0); load("s", "rb", T.rec)
+    if not OPT["ld"]: load("s", "wb", T.w)
+    load("a", "ths", T.th)
+    for lo, hi, a, e in ((0, cut, rank, 8), (cut, 128, 0, rank)):
+        if a < e:
+            dma("a", T.tw[lo:hi:8, :], T.hop[a:e, :], "tw", w=["tw", "tw1"])
+            dma("s", T.tw[lo + 4:hi:16, :], T.up[a:e, :], "tw", w=["tw", "tw1"])
+            dma("s", T.tw[lo + 12:hi:16, :], T.dn[a:e, :], "tw", w=["tw", "tw1"])
+    if OPT["ld"]: load("s", "wb", T.w)
+    iota(T.bi[:, :], [[-16, 8], [0, 16]], 128, 1, ["bi"])
+    iota(T.jlo[:, :], [[0, 2], [1, 16]], 32, 0, ["jlo"], **fl); iota(T.jc[:, :], [[1, 32], [0, 16]], 32, 0, ["jc"], **fl)
+    dma("s", T.jc[1:128:16, :], T.jlo[:, :], "jc", r=["jlo"], w=["jc"])
+    iota(T.m0[:, K:W], [[0, W - K]], 63, 0, ["m0"], **fl)
+    ms(T.zero[:, :], 0.0, ["zero"]); ms(T.m0[:, 0:K], 63.0, ["m0v"])
+    act(T.held[:, :], T.zero[:, :], AF.Silu, ["zero"], ["held"], bias=64.0)
+    cp(T.zt[:, 0:K], T.zero[:, :], ["zero"], ["zt"]); cp(T.zt[:, K:528], T.zero[:, 0:16], ["zero"], ["zt1"])
+    ts(T.zj[:, :], T.zi[:, :], 127, ALU.bitwise_and, ["zi"], ["zj"])
+    cp(T.dq0[:, :], T.wki[:, :], ["wki"], ["dq0"])
+    ts(T.zt[:, 15:K:16], T.zj[:, :], 0.0, ALU.is_equal, ["zj", "zt", "zt1"], ["zt"])
+    ts(T.bj[:, :], T.bi[:, :], 4, ALU.arith_shift_right, ["bi"], ["bj"])
+    cp(T.df0[:, :], T.wki[:, :], ["wki"], ["df0"])
+    ts(T.ones[:, :], T.bj[:, :], 8.0, ALU.is_equal, ["bj"], ["ones"])
+    cb = OPT["cb"]
+    cp(T.b[:, cb:W], T.bh[:, cb:W], ["bh"], ["b1"])
+
+    def late_constants():
+        ms(T.zb[:, :], 0.0, ["zb"]); ms(T.wv[:, K:544], 1.0, ["wv1"]); ms(T.wv[:, 544:560], -1.0, ["wv2"])
+        ms(T.zc[:, 0:144], 0.0, ["zc"]); ms(T.zc[:, 144:176], 1.0 / 32, ["zc1"])
+        op("v", lambda: V.tensor_scalar(T.zc[:, 15:128:16], T.zi[:, 8:16], 128.0, 0.5, ALU.is_equal, ALU.mult), ["zi", "zc"], ["zc"])
+        op("v", lambda: V.tensor_scalar(T.za[:, 0:8], T.zi[:, 8:16], 128.0, 16.0, ALU.is_equal, ALU.mult), ["zi"], ["za0"])
+        ts(T.za[:, 8:16], T.zi[:, 8:16], 129.0, ALU.is_equal, ["zi"], ["za1"])
+        tt(T.zb[:, 15:128:16], T.za[:, 0:8], T.za[:, 8:16], ALU.add, ["za0", "za1", "zb"], ["zb"])
+
+    H = K // 2
+    for s in range(RO):
+        last = s == RO - 1
+        dq, xl, h, hu, hd, ul, nl, df, m = ("%s%d" % (x, s) for x in ("dq", "xl", "h", "hu", "hd", "ul", "nl", "df", "m"))
+        D = T[dq][:, :]
+        X = [(xl, 0, xl + "a", h), (xl, 32, xl + "b", h), (ul, 0, ul, hu), (nl, 0, nl, hd)]
+        halves = OPT["half3" if last else "half"]; acts = OPT["act3"] if last else OPT["act"]
+
+        def lst(k, a=0, e=K): return T[X[k][0]][:, X[k][1] + a // 16:X[k][1] + e // 16]
+        def parts(k): return ((0, H, "ps", "0"), (H, K, "pa", "1")) if k in halves else ((0, K, "ps", ""),)
+        def names(x, p): return [x + p] if p else [x + "0", x + "1"]
+        def grad(k):
+            tt(T["g%d" % k][:, :], ind("wb", lst(k)), T[X[k][3]][:, :], ALU.mult, ["wb", X[k][2], X[k][3]], ["g%d" % k])
+        def size(k):
+            j = k % 2; ab = "ab%d" % j
+            act(T[ab][:, :], T["g%d" % k][:, :], AF.Abs, ["g%d" % k], [ab])
+        def over(k):
+            j = k % 2; ab = "ab%d" % j; big = "big%d" % j
+            if k in acts:
+                act(T[ab][:, :], T[ab][:, :], AF.Relu, [ab, "nth"], [ab], bias=T.nth[:, :])
+                act(T[big][:, :], T[ab][:, :], AF.Sign, [ab], [big])
+            else: ts(T[big][:, :], T[ab][:, :], T.ths[:, :], ALU.is_gt, [ab, "ths"], [big])
+            mm(T["pc%d" % j][:, :], T.ones[:, :], T[big][:, :], True, True, ["ones", big], ["pc%d" % j])
+        def many(k, first=True):
+            act(T.rl[:, :], T["pc%d" % (k % 2)][:, :], AF.Relu, ["pc%d" % (k % 2)], ["rl"], bias=-8.0)
+            for a, e, bank, p in parts(k): mm(T[bank][:, a:e], T.ones[:, :], T.rl[:, a:e], first, not first, ["ones", "rl"], [bank])
+        def old(k, first=False):
+            act(T.ao[:, :], ind("b", lst(k)), AF.Abs, ["b", X[k][2]], ["ao"])
+            for a, e, bank, p in parts(k): mm(T[bank][:, a:e], T.ones[:, :], T.ao[:, a:e], first, not first, ["ones", "ao"], [bank])
+        def accept(k):
+            for a, e, bank, p in parts(k): act(T.acc[:, a:e], T[bank][:, a:e], AF.Sign, [bank], names("acc", p))
+        def total(k): tt(T.tt[:, :], ind("b", lst(k)), T["g%d" % k][:, :], ALU.add, ["b", X[k][2], "g%d" % k], ["tt0", "tt1"])
+        def put(k, between=None):
+            for a, e, bank, p in parts(k):
+                tt(ind("b", lst(k, a, e)), T.tt[:, a:e], T.acc[:, a:e], ALU.mult, names("tt", p) + names("acc", p) + [X[k][2]], ["b"])
+                if between and not a: between()
+        def mark(a, e):
+            if last: return
+            if a < 32: z = min(e, 32); act(ind(m, T[xl][:, a:z]), T.jc[:, 16 * a:16 * z], AF.Silu, [xl + "a", "jc", m, "m0v"], [m])
+            if e > 32: z = max(a, 32) - 32; act(ind(m, T[dq][:, z:e - 32]), T.held[:, 16 * z:16 * (e - 32)], AF.Silu, [dq, "held", m], [m])
+        def oldc():
+            if s: act(T.cd[:, :], ind("c", D), AF.Copy, ["c", dq], ["cd"])
+        def putc():
+            if s: tt(ind("c", D), T.cd[:, :], T.dl[:, :], ALU.add, ["cd", "dl", dq], ["c"])
+            else: cp(ind("c", D), T.dl[:, :], ["dl", dq, "c"], ["c"])
+            if last: store("s", "c", "yc")
+        def tables():
+            cp(T.tg[:, :], ind("tw", D), ["tw", dq], ["tg"])
+            tolist("pxu", 0, "zt", 256, "tg", K); tolist("px0", 0, "zt", 128, "tg", K)
+            tolist("px1", 0, "zt", 384, "tg", K); tolist("px1", 32, "zt", 0, "tg", K)
+        def steps():
+            if last: return
+            tt(T.ee[:, 0:32], T.px0[:, 0:32], T[df][:, :], ALU.subtract, ["px0", df], ["e0"])
+            tt(T.ee[:, 32:64], T.px1[:, 0:32], T[df][:, :], ALU.subtract, ["px1", df], ["e1"])
+
+        src = "b" if s else "bh"
+        act(T.nb[:, :], ind(src, D), AF.Copy, [src, dq], ["nb"], scale=-1.0)
+        if s or OPT["tb0"] == 0: tables()
+        if not s: act(T.b[:, 0:cb], T.bh[:, 0:cb], AF.Copy, ["bh"], ["b"])
+        act(ind("b", D), T.zero[:, :], AF.Silu, ["zero", dq, "b", "b1"], ["b"])
+        tt(T.dl[:, :], ind("rb", D), T.nb[:, :], ALU.mult, ["rb", dq, "nb"], ["dl"])
+        def uplist():
+            cp(T[xl][:, 96:128], T.pxu[:, 0:32], ["pxu"], [xl + "u"])
+            send(up, ul, T[ul][:, :], T[xl][:, 96:128], [xl + "u"])
+        if s: uplist()
+        if not s and OPT["tb0"] == 1: tables()
+        tt(T[h][:, :], ind("wb", D), T.dl[:, :], ALU.mult, ["wb", dq, "dl"], [h])
+        send(up, hu, T[hu][:, :], T[h][:, :], [h]); send(dn, "land%d" % s, T.land[s], T[h][:, :], [h])
+        if not s and OPT["tb0"] == 2: tables()
+        if not s: uplist()
+        cp(T[xl][:, 0:32], T.px0[:, 0:32], ["px0"], [xl + "a"])
+        grad(0)
+        if acts: act(T.nth[:, :], T.ths[:, :], AF.Copy, ["ths"], ["nth"], scale=-1.0)
+        old(0, True)
+        deep = ((0, H, "pc0", "0"), (H, K, "pl", "1")) if 0 in halves else ((0, K, "pc0", ""),)
+        for a, e, bank, p in deep: act(T.ab0[:, a:e], T.g0[:, a:e], AF.Abs, ["g0"], names("ab0h", p))
+        total(0)
+        for a, e, bank, p in deep:
+            ts(T.big0[:, a:e], T.ab0[:, a:e], T.ths[:, :], ALU.is_gt, names("ab0h", p) + ["ths"], names("big0h", p))
+            mm(T[bank][:, a:e], T.ones[:, :], T.big0[:, a:e], True, True, ["ones"] + names("big0h", p), [bank])
+        if OPT["lead"]: oldc()
+        for (a, e, bank, p), (_, _, to, _) in zip(deep, parts(0)):
+            act(T.rl[:, a:e], T[bank][:, a:e], AF.Relu, [bank], names("rlh", p), bias=-8.0)
+            mm(T[to][:, a:e], T.ones[:, :], T.rl[:, a:e], False, True, ["ones"] + names("rlh", p), [to])
+        cp(T[xl][:, 32:96], T.px1[:, 0:64], ["px1"], [xl + "b"])
+        send(dn, nl, T[nl][:, :], T[xl][:, 64:96], [xl + "b"])
+        if not s:
+            iota(T.c[:, :], [[0, W]], 0, 0, ["c"], **fl); iota(T.m1[:, :], [[0, W]], 63, 0, ["m1"], **fl)
+        arrives(dn, hu); arrives(dn, ul); arrives(up, "land%d" % s); arrives(up, nl)
+        dma("s", T[hd][16:128, :], T.land[s, 0:112, :], hd, r=["land%d" % s], w=[hd])
+        dma("s", T[hd][0:16, :], T.land[s, 112:128, :], hd, r=["land%d" % s], w=[hd])
+        m1, m2 = OPT["m1"], OPT["m2"]
+        grad(1); steps()
+        if OPT["s1"]: size(1); accept(0)
+        else: accept(0); size(1)
+        if not OPT["lead"]: oldc()
+        if OPT["s1"]: over(1); put(0)
+        else: put(0, lambda: over(1))
+        for k in (1, 2):
+            mark((0, m1)[k - 1], (m1, m2)[k - 1]); many(k)
+            old(k); grad(k + 1)
+            if k + 1 in acts: total(k); accept(k); size(k + 1); put(k); over(k + 1)
+            else: size(k + 1); total(k); accept(k); over(k + 1); put(k)
+            if last and OPT["c3"] == k: putc()
+        mark(m2, 64); many(3)
+        old(3); total(3)
+        if not s: late_constants()
+        if last and OPT["c3"] == 3: putc()
+        accept(3); put(3)
+        if last:
+            store("s", "b", "yb", 0, W // 2); store("a", "b", "yb", W // 2, W)
+            break
+        act(T.mg[:, :], ind(m, T[xl][:, 0:64]), AF.Copy, [m, xl + "a", xl + "b"], ["mg"])
+        tolist("pl", 0, "zb", 0, "mg", 2 * K)
+        act(T.ab0[:, :], ind("b", lst(0)), AF.Abs, ["b", X[0][2]], ["ab0"])
+        cp(T.ab1[:, :], ind("b", lst(1)), ["b", X[1][2]], ["ab1"])
+        sm = [T.sm[:, 32 * i:32 * i + 32] for i in range(8)]
+        pp = ((0, H, "pc0", "ps", "0"), (H, K, "pc1", "pa", "1")) if OPT["p4"] else ((0, K, "pc0", "ps", ""),)
+        for a, e, u, v, p in pp: act(T[u][:, a:e], T.ab1[:, a:e], AF.Abs, ["ab1"], [u])
+        ts(T.lk[:, :], T.pl[:, 32:64], -544.0, ALU.add, ["pl"], ["lk"])
+        ts(sm[0], T.pl[:, 0:32], 1080.0, ALU.is_lt, ["pl"], ["s0"])
+        for a, e, u, v, p in pp: tt(T.tt[:, a:e], T[u][:, a:e], T.ab0[:, a:e], ALU.subtract, [u, "ab0"], names("tt", p))
+        for a, e, u, v, p in pp:
+            act(T.sg[:, a:e], T.tt[:, a:e], AF.Sign, names("tt", p), names("sg", p))
+            mm(T[v][:, a:e], T.ones[:, :], T.sg[:, a:e], True, True, ["ones"] + names("sg", p), [v])
+        for a, e, u, v, p in pp: act(T.wv[:, a:e], T[v][:, a:e], AF.Sign, [v], names("wvh", p), bias=-0.5)
+        tolist("px0", 0, "zc", 0, "wv", K, True); ops[-1]["r"] += ["wvh0", "wvh1"]
+        act(T.wg[:, :], ind("wv", T.lk[:, :]), AF.Copy, ["wvh0", "wvh1", "wv1", "wv2", "lk"], ["wg"])
+        tolist("px1", 0, "zc", 0, "wg", K, True)
+        putc()
+        tt(sm[1], sm[0], T.ee[:, 0:32], ALU.mult, ["s0", "e0"], ["s1"])
+        tt(sm[5], T.px0[:, 0:32], T.ee[:, 32:64], ALU.mult, ["px0", "e1"], ["s5"])
+        tt(sm[2], sm[1], T[df][:, :], ALU.add, ["s1", df], ["s2"])
+        tt(sm[4], T.px0[:, 0:32], sm[1], ALU.mult, ["px0", "s1"], ["s4"])
+        tt(sm[6], sm[2], sm[4], ALU.subtract, ["s2", "s4"], ["s6"])
+        tt(sm[0], T.px1[:, 0:32], sm[5], ALU.mult, ["px1", "s5"], ["s0"])
+        nx = "%d" % (s + 1)
+        tt(T["df" + nx][:, :], sm[0], sm[6], ALU.add, ["s0", "s6"], ["df" + nx])
+        cp(T["dq" + nx][:, :], T["df" + nx][:, :], ["df" + nx], ["dq" + nx])
+    emit(g, T, ops)

@@ -1,39 +1,42 @@
+from concourse.bass import DstId, RemoteDMATransfer
 from concourse.mybir import AluOpType as ALU, ActivationFunctionType as AF
 
 W, K, RO = 2048, 512, 3
+U = 2.0 ** -30
 F32, BF, F16, I32, U16 = "float32", "bfloat16", "float16", "int32", "uint16"
 SCRATCH = {
-    "b": ("sbuf", [128, W], F32), "c": ("sbuf", [128, W], F32), "m0": ("sbuf", [128, W], F32), "m1": ("sbuf", [128, W], F32),
+    "b": ("sbuf", [128, 10 * W], F32), "c": ("sbuf", [128, W], F32), "m0": ("sbuf", [128, W], F32), "m1": ("sbuf", [128, W], F32),
     "tw": ("sbuf", [128, W], I32), "bh": ("sbuf", [128, W], BF), "wb": ("sbuf", [128, W], BF), "rb": ("sbuf", [128, W], BF),
     "nth": ("sbuf", [128, 1], F32), "ths": ("sbuf", [128, 1], F32), "wki": ("sbuf", [128, 32], I32),
     "zero": ("sbuf", [128, K], F32), "held": ("sbuf", [128, K], F32), "jc": ("sbuf", [128, K], F32), "jlo": ("sbuf", [128, 32], F32),
-    "zc": ("sbuf", [128, 176], BF),
-    "zi": ("sbuf", [128, 32], I32), "zj": ("sbuf", [128, 32], I32), "za": ("sbuf", [128, 16], F32),
-    "bi": ("sbuf", [128, 128], I32), "bj": ("sbuf", [128, 128], I32),
-    "zt": ("sbuf", [128, 528], F16), "zb": ("sbuf", [128, 144], BF), "ones": ("sbuf", [128, 128], BF),
+    "zi": ("sbuf", [128, 32], I32), "idn": ("sbuf", [128, 128], F32),
+    "zt": ("sbuf", [128, 528], F16), "zz": ("sbuf", [128, 432], BF), "nine": ("sbuf", [128, 32], F32),
     "nb": ("sbuf", [128, K], F32), "dl": ("sbuf", [128, K], F32), "cd": ("sbuf", [128, K], F32), "tg": ("sbuf", [128, K], F16),
     "ab0": ("sbuf", [128, K], F32), "ab1": ("sbuf", [128, K], F32), "big0": ("sbuf", [128, K], BF), "big1": ("sbuf", [128, K], BF),
-    "rl": ("sbuf", [128, K], BF), "ao": ("sbuf", [128, K], BF), "acc": ("sbuf", [128, K], F32), "tt": ("sbuf", [128, K], F32),
-    "mg": ("sbuf", [128, 2 * K], BF), "wv": ("sbuf", [128, 560], BF), "wg": ("sbuf", [128, K], BF), "sg": ("sbuf", [128, K], BF),
+    "ao": ("sbuf", [128, K], BF), "bo": ("sbuf", [128, K], F32), "aim": ("sbuf", [128, 32], F32), "to": ("sbuf", [128, 32], U16),
+    "mg": ("sbuf", [128, 2 * K], BF), "dd": ("sbuf", [128, 560], BF), "sg": ("sbuf", [128, 2 * K], BF),
     "ee": ("sbuf", [128, 64], F32), "sm": ("sbuf", [128, 256], F32), "lk": ("sbuf", [128, 32], U16),
-    "land": ("dram", [RO, 128, K], F32),
-    "pc0": ("psum", [128, K], F32), "pc1": ("psum", [128, K], F32), "ps": ("psum", [128, K], F32), "px0": ("psum", [128, K], F32),
-    "px1": ("psum", [128, K], F32), "pxu": ("psum", [128, K], F32), "pl": ("psum", [128, K], F32), "pa": ("psum", [128, K], F32),
+    "land": ("dram", [RO, 128, K + 32], F32),
 }
+PSUM = ("pc0", "pc1", "pd0", "pd1", "px0", "px1", "pl", "pv")
+for _n in PSUM:
+    SCRATCH[_n] = ("psum", [128, K], F32)
 for _k in range(4):
     SCRATCH["g%d" % _k] = ("sbuf", [128, K], F32)
 for _s in range(RO):
-    for _n in ("h", "hu", "hd"):
-        SCRATCH["%s%d" % (_n, _s)] = ("sbuf", [128, K], F32)
+    SCRATCH["h%d" % _s] = ("sbuf", [128, K + 64], F32)
+    SCRATCH["hu%d" % _s] = ("sbuf", [128, K + 32], F32)
+    SCRATCH["hd%d" % _s] = ("sbuf", [128, K + 32], F32)
     SCRATCH["xl%d" % _s] = ("sbuf", [128, 128], U16)
+    SCRATCH["xs%d" % _s] = ("sbuf", [128, 64], F32)
     SCRATCH["df%d" % _s] = ("sbuf", [128, 32], F32)
-    for _n in ("dq", "ul", "nl"):
-        SCRATCH["%s%d" % (_n, _s)] = ("sbuf", [128, 32], U16)
+    SCRATCH["dq%d" % _s] = ("sbuf", [128, 32], U16)
 LOADS = ["wki", "bh", "rb", "wb", "tw", "ths", "jc", "yb", "yc"]
 SEMAPHORES = (["qv", "qa", "qp", "qg", "sent"] + ["d_" + n for n in LOADS] + ["d_hd%d" % s for s in range(RO)]
-              + ["r_%s%d" % (n, s) for n in ("hu", "ul", "land", "nl") for s in range(RO)])
-OPT = dict(ld=1, cw=1408, cb=1152, half=(0, 3), half3=(0, 3), act=(), act3=(), tb0=1, m1=22, m2=44, lead=1, s1=0, c3=2, p4=1)
-PSUM = ("pc0", "pc1", "ps", "px0", "px1", "pxu", "pl", "pa")
+              + ["r_%s%d" % (n, s) for n in ("hu", "land") for s in range(RO)])
+OPT = dict(cw=1408, cb=1152, mf=1024, kv=160, oc=0,
+           act=((), (), ()), late=((), (), ()), marks=((0, 14, 40, 64, 64), (0, 14, 40, 64, 64), None),
+           pc=((0, 0, 128, 256, 128), (0, 0, 128, 256, 128), (0, 128, 128, 256)), split=((), (), ()))
 
 
 def emit(g, T, ops):
@@ -91,9 +94,10 @@ def rank_program(g, core, T, topo):
     n = len(T.cores); up = T.cores[(rank + 1) % n]; dn = T.cores[(rank - 1) % n]
     V, A, P = g.vector, g.scalar, g.tensor
     ops = []
+    H = K // 2
 
     def op(q, f, r=(), w=(), sem=None, cnt=16, inc=True):
-        r, w = ([y for x in z for y in ([x + "h0", x + "h1"] if x in ("ab0", "big0", "rl") else [x])] for z in (r, w))
+        r, w = ([y for x in z for y in ([x + "h0", x + "h1"] if x in ("g0", "ab0", "big0", "dd", "ao") else [x])] for z in (r, w))
         ops.append({"q": q, "f": f, "r": r, "w": w, "sem": sem, "n": cnt, "inc": inc})
 
     def engines(src, dst):
@@ -122,201 +126,193 @@ def rank_program(g, core, T, topo):
         dma(q, T[dst][128 - cut:128, a:e], T[name][0:cut, a:e], dst, r=[name])
         if rank: dma(q, T[dst][0:128 - cut, a:e], T[name][cut:128, a:e], dst, r=[name])
 
-    def ind(win, lst):
-        return T[win][:, :].indirect(lst)
+    def ind(win, lst, wide=W):
+        return T[win][:, 0:wide].indirect(lst)
 
     def tt(out, a, b, o, r, w): op("v", lambda: V.tensor_tensor(out, a, b, o), r, w)
     def ts(out, a, s, o, r, w): op("v", lambda: V.tensor_scalar(out, a, s, None, o), r, w)
+    def ts2(out, a, s, o, s2, o2, r, w): op("v", lambda: V.tensor_scalar(out, a, s, s2, o, o2), r, w)
     def cp(out, a, r, w): op("v", lambda: V.tensor_copy(out, a), r, w)
     def ms(out, v, w): op("v", lambda: V.memset(out, v), (), w)
     def act(out, a, f, r, w, **kw): op("a", lambda: A.activation(out, a, f, **kw), r, w)
     def iota(out, pat, base, cm, w, **kw): op("g", lambda: g.iota(out, pat, base, cm, **kw), (), w)
+    def keep(out, pat, o, fill, base, cm, w): op("g", lambda: g.affine_select(out, out, pat, o, fill, base, cm), w, w)
     def mm(out, l, x, st, sp, r, w): op("p", lambda: P.matmul(out, l, x, st, sp), r, w)
 
-    def tolist(bank, col, z, zoff, src, cols, lift=False):
+    def tolist(bank, col, z, zoff, src, cols, st=True, sp=True, r=None):
         def f():
             for i in range(16):
                 o = zoff + 15 - i
-                ins = P.matmul(T[bank][:, col:col + cols // 16], T[z][:, o:o + 128], T[src][:, i:cols:16], i == 0 and not lift, i == 15)
+                ins = P.matmul(T[bank][:, col:col + cols // 16], T[z][:, o:o + 128], T[src][:, i:cols:16], st and i == 0, sp and i == 15)
             return ins
-        if lift: mm(T[bank][:, col:col + 32], T.ones[:, :], T.zc[:, 144:176], True, False, ["ones", "zc1"], [bank])
-        op("p", f, [z, src], [bank])
+        op("p", f, [z] + (r or [src]), [bank])
 
     fl = {"allow_small_or_imprecise_dtypes": True}
-    cw = OPT["cw"]
+    ZB, ZC, ZO = 0, 144, 288
+    cw, cb, mf = OPT["cw"], OPT["cb"], OPT["mf"]
     ms(T.tw[:, 0:cw], 0, ["tw"])
-    iota(T.zi[:, :], [[-4, 4], [-16, 8]], 132, 1, ["zi"])
+    iota(T.zi[:, :], [[-4, 4], [-16, 8]], 0, 1, ["zi"])
     if cw < W: iota(T.tw[:, cw:W], [[0, W - cw]], 0, 0, ["tw1"])
     load("a", "wki", T.wk); load("s", "bh", T.b0); load("s", "rb", T.rec)
-    if not OPT["ld"]: load("s", "wb", T.w)
     load("a", "ths", T.th)
     for lo, hi, a, e in ((0, cut, rank, 8), (cut, 128, 0, rank)):
         if a < e:
             dma("a", T.tw[lo:hi:8, :], T.hop[a:e, :], "tw", w=["tw", "tw1"])
             dma("s", T.tw[lo + 4:hi:16, :], T.up[a:e, :], "tw", w=["tw", "tw1"])
             dma("s", T.tw[lo + 12:hi:16, :], T.dn[a:e, :], "tw", w=["tw", "tw1"])
-    if OPT["ld"]: load("s", "wb", T.w)
-    iota(T.bi[:, :], [[-16, 8], [0, 16]], 128, 1, ["bi"])
+    load("s", "wb", T.w)
+    iota(T.idn[:, :], [[0, 128]], 1, 0, ["idn"], **fl); keep(T.idn[:, :], [[-1, 128]], ALU.is_equal, 0.0, 0, 1, ["idn"])
+    iota(T.zz[:, :], [[0, 432]], 0, 0, ["zz"], **fl)
+    for off, wt in ((ZC, -W * U), (ZO, -2.0 ** 11)):
+        keep(T.zz[:, off + 15:off + 128:16], [[16, 8]], ALU.is_gt, wt, 0, -1, ["zz"])
+        keep(T.zz[:, off + 15:off + 128:16], [[16, 8]], ALU.is_ge, 0.0, 15, -1, ["zz"])
+    for row, wt in ((0, 16.0), (1, 1.0)): keep(T.zz[:, ZB + 15:ZB + 128:16], [[-16, 8]], ALU.not_equal, wt, -row, 1, ["zz"])
     iota(T.jlo[:, :], [[0, 2], [1, 16]], 32, 0, ["jlo"], **fl); iota(T.jc[:, :], [[1, 32], [0, 16]], 32, 0, ["jc"], **fl)
     dma("s", T.jc[1:128:16, :], T.jlo[:, :], "jc", r=["jlo"], w=["jc"])
-    iota(T.m0[:, K:W], [[0, W - K]], 63, 0, ["m0"], **fl)
+    if mf > K: iota(T.m0[:, K:mf], [[0, mf - K]], 63, 0, ["m0"], **fl)
     ms(T.zero[:, :], 0.0, ["zero"]); ms(T.m0[:, 0:K], 63.0, ["m0v"])
     act(T.held[:, :], T.zero[:, :], AF.Silu, ["zero"], ["held"], bias=64.0)
     cp(T.zt[:, 0:K], T.zero[:, :], ["zero"], ["zt"]); cp(T.zt[:, K:528], T.zero[:, 0:16], ["zero"], ["zt1"])
-    ts(T.zj[:, :], T.zi[:, :], 127, ALU.bitwise_and, ["zi"], ["zj"])
     cp(T.dq0[:, :], T.wki[:, :], ["wki"], ["dq0"])
-    ts(T.zt[:, 15:K:16], T.zj[:, :], 0.0, ALU.is_equal, ["zj", "zt", "zt1"], ["zt"])
-    ts(T.bj[:, :], T.bi[:, :], 4, ALU.arith_shift_right, ["bi"], ["bj"])
-    cp(T.df0[:, :], T.wki[:, :], ["wki"], ["df0"])
-    ts(T.ones[:, :], T.bj[:, :], 8.0, ALU.is_equal, ["bj"], ["ones"])
-    cb = OPT["cb"]
+    ts(T.zt[:, 15:K:16], T.zi[:, :], 0.0, ALU.is_equal, ["zi", "zt", "zt1"], ["zt"])
+    ts(T.df0[:, :], T.wki[:, :], U, ALU.mult, ["wki"], ["df0"])
     cp(T.b[:, cb:W], T.bh[:, cb:W], ["bh"], ["b1"])
 
-    def late_constants():
-        ms(T.zb[:, :], 0.0, ["zb"]); ms(T.wv[:, K:544], 1.0, ["wv1"]); ms(T.wv[:, 544:560], -1.0, ["wv2"])
-        ms(T.zc[:, 0:144], 0.0, ["zc"]); ms(T.zc[:, 144:176], 1.0 / 32, ["zc1"])
-        op("v", lambda: V.tensor_scalar(T.zc[:, 15:128:16], T.zi[:, 8:16], 128.0, 0.5, ALU.is_equal, ALU.mult), ["zi", "zc"], ["zc"])
-        op("v", lambda: V.tensor_scalar(T.za[:, 0:8], T.zi[:, 8:16], 128.0, 16.0, ALU.is_equal, ALU.mult), ["zi"], ["za0"])
-        ts(T.za[:, 8:16], T.zi[:, 8:16], 129.0, ALU.is_equal, ["zi"], ["za1"])
-        tt(T.zb[:, 15:128:16], T.za[:, 0:8], T.za[:, 8:16], ALU.add, ["za0", "za1", "zb"], ["zb"])
-
-    H = K // 2
     for s in range(RO):
         last = s == RO - 1
-        dq, xl, h, hu, hd, ul, nl, df, m = ("%s%d" % (x, s) for x in ("dq", "xl", "h", "hu", "hd", "ul", "nl", "df", "m"))
+        dq, xl, xs, h, hu, hd, df, m = ("%s%d" % (x, s) for x in ("dq", "xl", "xs", "h", "hu", "hd", "df", "m"))
         D = T[dq][:, :]
-        X = [(xl, 0, xl + "a", h), (xl, 32, xl + "b", h), (ul, 0, ul, hu), (nl, 0, nl, hd)]
-        halves = OPT["half3" if last else "half"]; acts = OPT["act3"] if last else OPT["act"]
+        X = [(xl + "a", T[xs][:, 0:32], xs + "a", h, 32), (xl + "b", T[xs][:, 32:64], xs + "b", h, 32),
+             (xl + "c", T[hu][:, 0:32], hu, hu, 32), (xl + "d", T[hd][:, K:K + 32], hd, hd, 0)]
+        acts, late, mk, pcs, split = (OPT[x][s] for x in ("act", "late", "marks", "pc", "split")); cdone = [0]
 
-        def lst(k, a=0, e=K): return T[X[k][0]][:, X[k][1] + a // 16:X[k][1] + e // 16]
-        def parts(k): return ((0, H, "ps", "0"), (H, K, "pa", "1")) if k in halves else ((0, K, "ps", ""),)
-        def names(x, p): return [x + p] if p else [x + "0", x + "1"]
-        def grad(k):
-            tt(T["g%d" % k][:, :], ind("wb", lst(k)), T[X[k][3]][:, :], ALU.mult, ["wb", X[k][2], X[k][3]], ["g%d" % k])
-        def size(k):
-            j = k % 2; ab = "ab%d" % j
-            act(T[ab][:, :], T["g%d" % k][:, :], AF.Abs, ["g%d" % k], [ab])
-        def over(k):
-            j = k % 2; ab = "ab%d" % j; big = "big%d" % j
+        def lst(k, a=0, e=K): return T[xl][:, 32 * k + a // 16:32 * k + e // 16]
+        def grad(k, a=0, e=K, p=""):
+            tt(T["g%d" % k][:, a:e], ind("wb", lst(k, a, e)), T[X[k][3]][:, X[k][4] + a:X[k][4] + e], ALU.mult, ["wb", X[k][0], X[k][3]], ["g%d" % k + p])
+        def size(k, a=0, e=K, p=""):
+            ab = "ab%d" % (k % 2)
+            act(T[ab][:, a:e], T["g%d" % k][:, a:e], AF.Abs, ["g%d" % k + p], [ab + p])
+        def over(k, a=0, e=K, p=""):
+            ab = "ab%d" % (k % 2); big = "big%d" % (k % 2)
             if k in acts:
-                act(T[ab][:, :], T[ab][:, :], AF.Relu, [ab, "nth"], [ab], bias=T.nth[:, :])
-                act(T[big][:, :], T[ab][:, :], AF.Sign, [ab], [big])
-            else: ts(T[big][:, :], T[ab][:, :], T.ths[:, :], ALU.is_gt, [ab, "ths"], [big])
-            mm(T["pc%d" % j][:, :], T.ones[:, :], T[big][:, :], True, True, ["ones", big], ["pc%d" % j])
-        def many(k, first=True):
-            act(T.rl[:, :], T["pc%d" % (k % 2)][:, :], AF.Relu, ["pc%d" % (k % 2)], ["rl"], bias=-8.0)
-            for a, e, bank, p in parts(k): mm(T[bank][:, a:e], T.ones[:, :], T.rl[:, a:e], first, not first, ["ones", "rl"], [bank])
-        def old(k, first=False):
-            act(T.ao[:, :], ind("b", lst(k)), AF.Abs, ["b", X[k][2]], ["ao"])
-            for a, e, bank, p in parts(k): mm(T[bank][:, a:e], T.ones[:, :], T.ao[:, a:e], first, not first, ["ones", "ao"], [bank])
-        def accept(k):
-            for a, e, bank, p in parts(k): act(T.acc[:, a:e], T[bank][:, a:e], AF.Sign, [bank], names("acc", p))
-        def total(k): tt(T.tt[:, :], ind("b", lst(k)), T["g%d" % k][:, :], ALU.add, ["b", X[k][2], "g%d" % k], ["tt0", "tt1"])
-        def put(k, between=None):
-            for a, e, bank, p in parts(k):
-                tt(ind("b", lst(k, a, e)), T.tt[:, a:e], T.acc[:, a:e], ALU.mult, names("tt", p) + names("acc", p) + [X[k][2]], ["b"])
-                if between and not a: between()
-        def mark(a, e):
-            if last: return
-            if a < 32: z = min(e, 32); act(ind(m, T[xl][:, a:z]), T.jc[:, 16 * a:16 * z], AF.Silu, [xl + "a", "jc", m, "m0v"], [m])
+                act(T[ab][:, a:e], T[ab][:, a:e], AF.Relu, [ab + p, "nth"], [ab + p], bias=T.nth[:, :])
+                act(T[big][:, a:e], T[ab][:, a:e], AF.Sign, [ab + p], [big + p])
+            else: ts2(T[big][:, a:e], T[ab][:, a:e], T.ths[:, :], ALU.is_gt, -9.0 / 16, ALU.add, [ab + p, "ths"], [big + p])
+        def place(k):
+            bank = "pd%d" % (k % 2)
+            mm(T[bank][:, 0:32], T.idn[:, :], X[k][1], True, False, ["idn", X[k][2]], [bank])
+            if k in acts: mm(T[bank][:, 0:32], T.idn[:, :], T.nine[:, :], False, False, ["idn", "nine"], [bank])
+        def count(k, sp=False): tolist("pd%d" % (k % 2), 0, "zz", ZC, "big%d" % (k % 2), K, False, sp)
+        def old(k, sp=True):
+            e = H if k in split else K
+            act(T.ao[:, 0:e], ind("b", lst(k, 0, e)), AF.Abs, ["b", X[k][0]], ["aoh0"] if e < K else ["ao"], scale=2.0 ** 99)
+            if e < K: ts(T.ao[:, e:K], ind("b", lst(k, e, K)), 0.0, ALU.not_equal, ["b", X[k][0]], ["aoh1"])
+            tolist("pd%d" % (k % 2), 0, "zz", ZO, "ao", K, False, sp)
+        def base(k): act(T.bo[:, :], ind("b", lst(k)), AF.Copy, ["b", X[k][0]], ["bo"])
+        def aim(k):
+            tt(T.aim[:, :], T["pd%d" % (k % 2)][:, 0:32], X[k][1], ALU.max, ["pd%d" % (k % 2), X[k][2]], ["aim"])
+            ts(T.to[:, :], T.aim[:, :], 1 / U, ALU.mult, ["aim"], ["to"])
+        def put(k): tt(ind("b", T.to[:, :], 10 * W), T.bo[:, :], T["g%d" % k][:, :], ALU.add, ["bo", "g%d" % k, "to"], ["b"])
+        def mark(i):
+            if last or mk[i] == mk[i + 1]: return
+            a, e = mk[i], mk[i + 1]
+            if a < 32: z = min(e, 32); act(ind(m, T[xl][:, a:z]), T.jc[:, 16 * a:16 * z], AF.Silu, [xl + "a", "jc", m, "m0v", "m0w"], [m])
             if e > 32: z = max(a, 32) - 32; act(ind(m, T[dq][:, z:e - 32]), T.held[:, 16 * z:16 * (e - 32)], AF.Silu, [dq, "held", m], [m])
+        def marked():
+            act(T.mg[:, :], ind(m, T[xl][:, 0:64]), AF.Copy, [m, xl + "a", xl + "b"], ["mg"]); tolist("pl", 0, "zz", ZB, "mg", 2 * K)
         def oldc():
             if s: act(T.cd[:, :], ind("c", D), AF.Copy, ["c", dq], ["cd"])
-        def putc():
-            if s: tt(ind("c", D), T.cd[:, :], T.dl[:, :], ALU.add, ["cd", "dl", dq], ["c"])
-            else: cp(ind("c", D), T.dl[:, :], ["dl", dq, "c"], ["c"])
-            if last: store("s", "c", "yc")
+        def putc(i):
+            a = cdone[0]; e = a + pcs[i]; cdone[0] = e
+            if a == e: return
+            o = ind("c", T[dq][:, a // 16:e // 16])
+            if s: tt(o, T.cd[:, a:e], T.dl[:, a:e], ALU.add, ["cd", "dl", dq], ["c"])
+            else: cp(o, T.dl[:, a:e], ["dl", dq, "c"], ["c"])
+            if last and e == K: store("s", "c", "yc")
         def tables():
             cp(T.tg[:, :], ind("tw", D), ["tw", dq], ["tg"])
-            tolist("pxu", 0, "zt", 256, "tg", K); tolist("px0", 0, "zt", 128, "tg", K)
-            tolist("px1", 0, "zt", 384, "tg", K); tolist("px1", 32, "zt", 0, "tg", K)
-        def steps():
-            if last: return
-            tt(T.ee[:, 0:32], T.px0[:, 0:32], T[df][:, :], ALU.subtract, ["px0", df], ["e0"])
-            tt(T.ee[:, 32:64], T.px1[:, 0:32], T[df][:, :], ALU.subtract, ["px1", df], ["e1"])
+            for bank, row in (("pl", 1), ("px0", 0), ("pv", 3), ("px1", 2)): tolist(bank, 0, "zt", 128 * row, "tg", K)
+        def uplist(): ts(T[h][:, 0:32], T.pl[:, 0:32], U, ALU.mult, ["pl"], [h + "u"])
+        def far(k): ts(lst(k), X[k][1], 1 / U, ALU.mult, [X[k][2]], [X[k][0]]); grad(k)
 
         src = "b" if s else "bh"
         act(T.nb[:, :], ind(src, D), AF.Copy, [src, dq], ["nb"], scale=-1.0)
-        if s or OPT["tb0"] == 0: tables()
+        if s: tables()
         if not s: act(T.b[:, 0:cb], T.bh[:, 0:cb], AF.Copy, ["bh"], ["b"])
         act(ind("b", D), T.zero[:, :], AF.Silu, ["zero", dq, "b", "b1"], ["b"])
         tt(T.dl[:, :], ind("rb", D), T.nb[:, :], ALU.mult, ["rb", dq, "nb"], ["dl"])
-        def uplist():
-            cp(T[xl][:, 96:128], T.pxu[:, 0:32], ["pxu"], [xl + "u"])
-            send(up, ul, T[ul][:, :], T[xl][:, 96:128], [xl + "u"])
+        if not s: tables()
         if s: uplist()
-        if not s and OPT["tb0"] == 1: tables()
-        tt(T[h][:, :], ind("wb", D), T.dl[:, :], ALU.mult, ["wb", dq, "dl"], [h])
-        send(up, hu, T[hu][:, :], T[h][:, :], [h]); send(dn, "land%d" % s, T.land[s], T[h][:, :], [h])
-        if not s and OPT["tb0"] == 2: tables()
+        tt(T[h][:, 32:32 + K], ind("wb", D), T.dl[:, :], ALU.mult, ["wb", dq, "dl"], [h])
         if not s: uplist()
+        send(up, hu, T[hu][:, :], T[h][:, 0:32 + K], [h, h + "u"])
         cp(T[xl][:, 0:32], T.px0[:, 0:32], ["px0"], [xl + "a"])
-        grad(0)
-        if acts: act(T.nth[:, :], T.ths[:, :], AF.Copy, ["ths"], ["nth"], scale=-1.0)
-        old(0, True)
-        deep = ((0, H, "pc0", "0"), (H, K, "pl", "1")) if 0 in halves else ((0, K, "pc0", ""),)
-        for a, e, bank, p in deep: act(T.ab0[:, a:e], T.g0[:, a:e], AF.Abs, ["g0"], names("ab0h", p))
-        total(0)
-        for a, e, bank, p in deep:
-            ts(T.big0[:, a:e], T.ab0[:, a:e], T.ths[:, :], ALU.is_gt, names("ab0h", p) + ["ths"], names("big0h", p))
-            mm(T[bank][:, a:e], T.ones[:, :], T.big0[:, a:e], True, True, ["ones"] + names("big0h", p), [bank])
-        if OPT["lead"]: oldc()
-        for (a, e, bank, p), (_, _, to, _) in zip(deep, parts(0)):
-            act(T.rl[:, a:e], T[bank][:, a:e], AF.Relu, [bank], names("rlh", p), bias=-8.0)
-            mm(T[to][:, a:e], T.ones[:, :], T.rl[:, a:e], False, True, ["ones"] + names("rlh", p), [to])
-        cp(T[xl][:, 32:96], T.px1[:, 0:64], ["px1"], [xl + "b"])
-        send(dn, nl, T[nl][:, :], T[xl][:, 64:96], [xl + "b"])
+        grad(0, 0, H, "h0")
+        ts(T[h][:, 32 + K:64 + K], T.pv[:, 0:32], U, ALU.mult, ["pv"], [h + "d"])
+        send(dn, "land%d" % s, T.land[s], T[h][:, 32:64 + K], [h, h + "d"])
+        act(T[xs][:, 0:32], T.px0[:, 0:32], AF.Copy, ["px0"], [xs + "a"], scale=U)
+        place(0); old(0, False)
+        grad(0, H, K, "h1")
+        cp(T[xl][:, 32:64], T.px1[:, 0:32], ["px1"], [xl + "b"])
+        if acts and not any(OPT["act"][:s]): act(T.nth[:, :], T.ths[:, :], AF.Copy, ["ths"], ["nth"], scale=-1.0)
+        size(0, 0, H, "h0"); size(0, H, K, "h1")
+        over(0, 0, H, "h0"); over(0, H, K, "h1"); count(0, True)
+        base(0)
+        act(T[xs][:, 32:64], T.px1[:, 0:32], AF.Copy, ["px1"], [xs + "b"], scale=U)
         if not s:
-            iota(T.c[:, :], [[0, W]], 0, 0, ["c"], **fl); iota(T.m1[:, :], [[0, W]], 63, 0, ["m1"], **fl)
-        arrives(dn, hu); arrives(dn, ul); arrives(up, "land%d" % s); arrives(up, nl)
+            if mf < W: iota(T.m0[:, mf:W], [[0, W - mf]], 63, 0, ["m0w"], **fl)
+            iota(T.nine[:, :], [[0, 32]], 0, 0, ["nine"], **fl); keep(T.nine[:, :], [[0, 32]], ALU.is_gt, 9 * W * U, 0, 0, ["nine"])
+            iota(T.c[:, :], [[0, W]], 0, 0, ["c"], **fl)
+            iota(T.dd[:, K:544], [[0, 32]], 1, 0, ["dd1"], **fl); iota(T.dd[:, 544:560], [[0, 16]], -1, 0, ["dd2"], **fl)
+            iota(T.m1[:, :], [[0, W]], 63, 0, ["m1"], **fl)
+        arrives(dn, hu); arrives(up, "land%d" % s)
         dma("s", T[hd][16:128, :], T.land[s, 0:112, :], hd, r=["land%d" % s], w=[hd])
         dma("s", T[hd][0:16, :], T.land[s, 112:128, :], hd, r=["land%d" % s], w=[hd])
-        m1, m2 = OPT["m1"], OPT["m2"]
-        grad(1); steps()
-        if OPT["s1"]: size(1); accept(0)
-        else: accept(0); size(1)
-        if not OPT["lead"]: oldc()
-        if OPT["s1"]: over(1); put(0)
-        else: put(0, lambda: over(1))
-        for k in (1, 2):
-            mark((0, m1)[k - 1], (m1, m2)[k - 1]); many(k)
-            old(k); grad(k + 1)
-            if k + 1 in acts: total(k); accept(k); size(k + 1); put(k); over(k + 1)
-            else: size(k + 1); total(k); accept(k); over(k + 1); put(k)
-            if last and OPT["c3"] == k: putc()
-        mark(m2, 64); many(3)
-        old(3); total(3)
-        if not s: late_constants()
-        if last and OPT["c3"] == 3: putc()
-        accept(3); put(3)
+        sm = [T.sm[:, 32 * i:32 * i + 32] for i in range(8)]
+        grad(1); putc(0)
+        for k in range(4):
+            aim(k)
+            if k == 3:
+                put(k)
+                if not last: mark(3); marked()
+                break
+            if k + 1 in late:
+                put(k)
+                if k == OPT["oc"]: oldc()
+                mark(k); far(k + 1); place(k + 1); old(k + 1, False); size(k + 1); base(k + 1); over(k + 1); count(k + 1, True)
+            else:
+                size(k + 1); put(k); over(k + 1); place(k + 1); count(k + 1)
+                if k == OPT["oc"]: oldc()
+                mark(k); old(k + 1); base(k + 1)
+            putc(k + 1)
+            if k < 2 and k + 2 not in late: far(k + 2)
+            if k == 2 and not last:
+                tt(T.ee[:, 0:32], T[df][:, :], T[xs][:, 0:32], ALU.subtract, [xs + "a", df], ["e0"])
+                tt(T.ee[:, 32:64], T[xs][:, 32:64], T[df][:, :], ALU.subtract, [xs + "b", df], ["e1"])
         if last:
             store("s", "b", "yb", 0, W // 2); store("a", "b", "yb", W // 2, W)
             break
-        act(T.mg[:, :], ind(m, T[xl][:, 0:64]), AF.Copy, [m, xl + "a", xl + "b"], ["mg"])
-        tolist("pl", 0, "zb", 0, "mg", 2 * K)
-        act(T.ab0[:, :], ind("b", lst(0)), AF.Abs, ["b", X[0][2]], ["ab0"])
-        cp(T.ab1[:, :], ind("b", lst(1)), ["b", X[1][2]], ["ab1"])
-        sm = [T.sm[:, 32 * i:32 * i + 32] for i in range(8)]
-        pp = ((0, H, "pc0", "ps", "0"), (H, K, "pc1", "pa", "1")) if OPT["p4"] else ((0, K, "pc0", "ps", ""),)
-        for a, e, u, v, p in pp: act(T[u][:, a:e], T.ab1[:, a:e], AF.Abs, ["ab1"], [u])
+        act(T.ab0[:, :], ind("b", lst(0)), AF.Abs, ["b", X[0][0]], ["ab0"])
+        cp(T.ab1[:, :], ind("b", lst(1)), ["b", X[1][0]], ["ab1"])
+        pp = ((0, H, "pc0", "h0"), (H, K, "pc1", "h1"))
+        for a, e, u, p in pp: act(T[u][:, a:e], T.ab1[:, a:e], AF.Abs, ["ab1"], [u])
         ts(T.lk[:, :], T.pl[:, 32:64], -544.0, ALU.add, ["pl"], ["lk"])
         ts(sm[0], T.pl[:, 0:32], 1080.0, ALU.is_lt, ["pl"], ["s0"])
-        for a, e, u, v, p in pp: tt(T.tt[:, a:e], T[u][:, a:e], T.ab0[:, a:e], ALU.subtract, [u, "ab0"], names("tt", p))
-        for a, e, u, v, p in pp:
-            act(T.sg[:, a:e], T.tt[:, a:e], AF.Sign, names("tt", p), names("sg", p))
-            mm(T[v][:, a:e], T.ones[:, :], T.sg[:, a:e], True, True, ["ones"] + names("sg", p), [v])
-        for a, e, u, v, p in pp: act(T.wv[:, a:e], T[v][:, a:e], AF.Sign, [v], names("wvh", p), bias=-0.5)
-        tolist("px0", 0, "zc", 0, "wv", K, True); ops[-1]["r"] += ["wvh0", "wvh1"]
-        act(T.wg[:, :], ind("wv", T.lk[:, :]), AF.Copy, ["wvh0", "wvh1", "wv1", "wv2", "lk"], ["wg"])
-        tolist("px1", 0, "zc", 0, "wg", K, True)
-        putc()
-        tt(sm[1], sm[0], T.ee[:, 0:32], ALU.mult, ["s0", "e0"], ["s1"])
-        tt(sm[5], T.px0[:, 0:32], T.ee[:, 32:64], ALU.mult, ["px0", "e1"], ["s5"])
-        tt(sm[2], sm[1], T[df][:, :], ALU.add, ["s1", df], ["s2"])
-        tt(sm[4], T.px0[:, 0:32], sm[1], ALU.mult, ["px0", "s1"], ["s4"])
-        tt(sm[6], sm[2], sm[4], ALU.subtract, ["s2", "s4"], ["s6"])
-        tt(sm[0], T.px1[:, 0:32], sm[5], ALU.mult, ["px1", "s5"], ["s0"])
+        for a, e, u, p in pp: tt(T.dd[:, a:e], T[u][:, a:e], T.ab0[:, a:e], ALU.subtract, [u, "ab0"], ["dd" + p])
+        kv = OPT["kv"]; eps = 2.0 ** -116
+        act(T.sg[:, K + kv:2 * K], ind("dd", T.lk[:, kv // 16:32], 560), AF.Sign, ["dd", "dd1", "dd2", "lk"], ["sga"])
+        ts2(T.sg[:, 0:K], T.dd[:, 0:K], eps, ALU.min, -eps, ALU.max, ["dd"], ["sgo"])
+        if kv: ts2(T.sg[:, K:K + kv], ind("dd", T.lk[:, 0:kv // 16], 560), eps, ALU.min, -eps, ALU.max, ["dd", "dd1", "dd2", "lk"], ["sgv"])
+        tolist("pv", 0, "zz", ZO, "sg", 2 * K, r=["sga", "sgo", "sgv"])
+        tt(T.ee[:, 0:32], T.ee[:, 0:32], sm[0], ALU.mult, ["s0", "e0"], ["e0"])
+        tt(sm[1], T[df][:, :], T.ee[:, 0:32], ALU.subtract, ["e0", df], ["s1"])
+        putc(4)
+        assert cdone[0] == K
+        ts(T.sm[:, 64:128], T.pv[:, 0:64], 0.0, ALU.is_lt, ["pv"], ["s2"])
+        tt(T.sm[:, 128:192], T.sm[:, 64:128], T.ee[:, :], ALU.mult, ["s2", "e0", "e1"], ["s4"])
+        tt(sm[6], sm[5], sm[2], ALU.mult, ["s2", "s4"], ["s6"])
+        tt(sm[7], sm[4], sm[1], ALU.add, ["s1", "s4"], ["s7"])
         nx = "%d" % (s + 1)
-        tt(T["df" + nx][:, :], sm[0], sm[6], ALU.add, ["s0", "s6"], ["df" + nx])
-        cp(T["dq" + nx][:, :], T["df" + nx][:, :], ["df" + nx], ["dq" + nx])
+        tt(T["df" + nx][:, :], sm[6], sm[7], ALU.add, ["s6", "s7"], ["df" + nx])
+        ts(T["dq" + nx][:, :], T["df" + nx][:, :], 1 / U, ALU.mult, ["df" + nx], ["dq" + nx])
     emit(g, T, ops)

@@ -1,4 +1,3 @@
-from concourse.bass import DstId, RemoteDMATransfer
 from concourse.mybir import AluOpType as ALU, ActivationFunctionType as AF
 
 W, K, RO = 2048, 512, 3
@@ -6,37 +5,40 @@ U = 2.0 ** -30
 F32, BF, F16, I32, U16 = "float32", "bfloat16", "float16", "int32", "uint16"
 SCRATCH = {
     "b": ("sbuf", [128, 10 * W], F32), "c": ("sbuf", [128, W], F32), "m0": ("sbuf", [128, W], F32), "m1": ("sbuf", [128, W], F32),
-    "tw": ("sbuf", [128, W], I32), "bh": ("sbuf", [128, W], BF), "wb": ("sbuf", [128, W], BF), "rb": ("sbuf", [128, W], BF),
-    "nth": ("sbuf", [128, 1], F32), "ths": ("sbuf", [128, 1], F32), "wki": ("sbuf", [128, 32], I32),
-    "zero": ("sbuf", [128, K], F32), "held": ("sbuf", [128, K], F32), "jc": ("sbuf", [128, K], F32), "jlo": ("sbuf", [128, 32], F32),
-    "zi": ("sbuf", [128, 32], I32), "idn": ("sbuf", [128, 128], F32),
-    "zt": ("sbuf", [128, 528], F16), "zz": ("sbuf", [128, 432], BF), "nine": ("sbuf", [128, 32], F32),
-    "nb": ("sbuf", [128, K], F32), "dl": ("sbuf", [128, K], F32), "cd": ("sbuf", [128, K], F32), "tg": ("sbuf", [128, K], F16),
+    "tw": ("sbuf", [128, W], I32), "bh": ("sbuf", [128, W], BF), "wb": ("sbuf", [128, W], BF), "wu": ("sbuf", [128, W], BF),
+    "rb": ("sbuf", [128, W], BF), "nth": ("sbuf", [128, 2], F32), "ths": ("sbuf", [128, 2], F32), "wki": ("sbuf", [128, 32], I32),
+    "zero": ("sbuf", [128, K], F32), "jc": ("sbuf", [128, K], F32), "jlo": ("sbuf", [128, 32], F32),
+    "zi": ("sbuf", [128, 40], I32), "idn": ("sbuf", [128, 128], F32), "gu": ("sbuf", [128, K], F32),
+    "zt": ("sbuf", [128, 656], F16), "zz": ("sbuf", [128, 656], BF), "nine": ("sbuf", [128, 32], F32),
+    "nb": ("sbuf", [128, K], F32), "cd": ("sbuf", [128, K], F32), "tg": ("sbuf", [128, K], F16),
     "ab0": ("sbuf", [128, K], F32), "ab1": ("sbuf", [128, K], F32), "big0": ("sbuf", [128, K], BF), "big1": ("sbuf", [128, K], BF),
     "ao": ("sbuf", [128, K], BF), "bo": ("sbuf", [128, K], F32), "aim": ("sbuf", [128, 32], F32), "to": ("sbuf", [128, 32], U16),
     "mg": ("sbuf", [128, 2 * K], BF), "dd": ("sbuf", [128, 560], BF), "sg": ("sbuf", [128, 2 * K], BF),
     "ee": ("sbuf", [128, 64], F32), "sm": ("sbuf", [128, 256], F32), "lk": ("sbuf", [128, 32], U16),
-    "land": ("dram", [RO, 128, K + 32], F32),
 }
-PSUM = ("pc0", "pc1", "pd0", "pd1", "px0", "px1", "pl", "pv")
+HALVED = ("g0", "ab0", "big0", "dd")
+PSUM = ("pc0", "pc1", "pd0", "pd1", "px", "pl", "pv")
 for _n in PSUM:
     SCRATCH[_n] = ("psum", [128, K], F32)
 for _k in range(4):
     SCRATCH["g%d" % _k] = ("sbuf", [128, K], F32)
 for _s in range(RO):
-    SCRATCH["h%d" % _s] = ("sbuf", [128, K + 64], F32)
-    SCRATCH["hu%d" % _s] = ("sbuf", [128, K + 32], F32)
+    SCRATCH["h%d" % _s] = ("sbuf", [128, K + 96], F32)
+    SCRATCH["hu%d" % _s] = ("sbuf", [128, K + 64], F32)
     SCRATCH["hd%d" % _s] = ("sbuf", [128, K + 32], F32)
-    SCRATCH["xl%d" % _s] = ("sbuf", [128, 128], U16)
+    SCRATCH["xl%d" % _s] = ("sbuf", [128, 160], U16)
     SCRATCH["xs%d" % _s] = ("sbuf", [128, 64], F32)
+    SCRATCH["dl%d" % _s] = ("sbuf", [128, K], F32)
     SCRATCH["df%d" % _s] = ("sbuf", [128, 32], F32)
     SCRATCH["dq%d" % _s] = ("sbuf", [128, 32], U16)
-LOADS = ["wki", "bh", "rb", "wb", "tw", "ths", "jc", "yb", "yc"]
-SEMAPHORES = (["qv", "qa", "qp", "qg", "sent"] + ["d_" + n for n in LOADS] + ["d_hd%d" % s for s in range(RO)]
-              + ["r_%s%d" % (n, s) for n in ("hu", "land") for s in range(RO)])
-OPT = dict(cw=1408, cb=1152, mf=1024, kv=160, oc=0,
-           act=((), (), ()), late=((), (), ()), marks=((0, 14, 40, 64, 64), (0, 14, 40, 64, 64), None),
-           pc=((0, 0, 128, 256, 128), (0, 0, 128, 256, 128), (0, 128, 128, 256)), split=((), (), ()))
+LOADS = ["wki", "bh", "rb", "wb", "wu", "m0", "tw", "ths", "jc", "yb", "yc"]
+SEMAPHORES = (["qv", "qa", "qp", "qg", "sent"] + ["d_" + n for n in LOADS] + ["d_gu%d" % s for s in range(RO)]
+              + ["r_%s%d" % (n, s) for n in ("hu", "hd") for s in range(RO)])
+OPT = dict(cw=1408, cb=1280, kv=96, oc={(1, 2): 1, (2, 0): 2}, act=((), (), (2, 3)),
+           marks=((0, 22, 44, 64, 64), (0, 26, 52, 56, 64), None),
+           pc=({3: [(0, 0, 256)], 4: [(0, 256, 384)]}, {"p": [(0, 384, K)], 3: [(1, 0, 256)], 4: [(1, 256, 384)]},
+               {"p": [(1, 384, K)], 2: [(2, 0, 128)], 3: [(2, 128, K)]}))
+SHIFT = ((0, 112, 16), (112, 128, 0))
 
 
 def emit(g, T, ops):
@@ -97,7 +99,7 @@ def rank_program(g, core, T, topo):
     H = K // 2
 
     def op(q, f, r=(), w=(), sem=None, cnt=16, inc=True):
-        r, w = ([y for x in z for y in ([x + "h0", x + "h1"] if x in ("g0", "ab0", "big0", "dd", "ao") else [x])] for z in (r, w))
+        r, w = ([y for x in z for y in ([x + "h0", x + "h1"] if x in HALVED else [x])] for z in (r, w))
         ops.append({"q": q, "f": f, "r": r, "w": w, "sem": sem, "n": cnt, "inc": inc})
 
     def engines(src, dst):
@@ -106,29 +108,19 @@ def rank_program(g, core, T, topo):
         e = topo.engines(src, dst)
         return e if topo.chip(src) != topo.chip(dst) else [x for x in e if x not in far]
 
-    def send(dst, name, out, src, r):
+    def send(dst, name, src, r):
         e = engines(core, dst); rid, pid = topo.addr(dst)[:2]; m = sum(1 << x for x in e)
-        op("g", lambda: g.remote_dma(out, src, T.sem["r_" + name], T.sem.sent, pid, rid, m), r=r, sem="sent", cnt=len(e), inc=False)
+        op("g", lambda: g.remote_dma(T[name][:, :], src, T.sem["r_" + name], T.sem.sent, pid, rid, m), r=r, sem="sent", cnt=len(e), inc=False)
 
     def arrives(src, name):
         op("r", None, w=[name], sem="r_" + name, cnt=len(engines(src, core)))
 
-    cut = 128 - 16 * rank
-
     def dma(q, out, in_, sem, r=(), w=()):
         op(q, lambda: (g.sync if q == "s" else g.scalar).dma_start(out, in_), r=r, w=w, sem="d_" + sem)
 
-    def load(q, name, src):
-        dma(q, T[name][0:cut, :], src[128 - cut:128, :], name, w=[name])
-        if rank: dma(q, T[name][cut:128, :], src[0:128 - cut, :], name, w=[name])
-
-    def store(q, name, dst, a=0, e=W):
-        dma(q, T[dst][128 - cut:128, a:e], T[name][0:cut, a:e], dst, r=[name])
-        if rank: dma(q, T[dst][0:128 - cut, a:e], T[name][cut:128, a:e], dst, r=[name])
-
-    def ind(win, lst, wide=W):
-        return T[win][:, 0:wide].indirect(lst)
-
+    def load(q, name, src): dma(q, T[name][:, :], src[:, :], name, w=[name])
+    def store(q, name, dst, a=0, e=W): dma(q, T[dst][:, a:e], T[name][:, a:e], dst, r=[name])
+    def ind(win, lst, wide=W): return T[win][:, 0:wide].indirect(lst)
     def tt(out, a, b, o, r, w): op("v", lambda: V.tensor_tensor(out, a, b, o), r, w)
     def ts(out, a, s, o, r, w): op("v", lambda: V.tensor_scalar(out, a, s, None, o), r, w)
     def ts2(out, a, s, o, s2, o2, r, w): op("v", lambda: V.tensor_scalar(out, a, s, s2, o, o2), r, w)
@@ -147,167 +139,168 @@ def rank_program(g, core, T, topo):
             return ins
         op("p", f, [z] + (r or [src]), [bank])
 
+    def band(off, q0, q1, wt, w):
+        o = T.zz[:, off + 15 + 16 * q0:off + 16 * q1:16]
+        keep(o, [[16, q1 - q0]], ALU.is_gt, wt, 0, -1, w); keep(o, [[16, q1 - q0]], ALU.is_ge, 0.0, 15, -1, w)
+
     fl = {"allow_small_or_imprecise_dtypes": True}
-    ZB, ZC, ZO = 0, 144, 288
-    cw, cb, mf = OPT["cw"], OPT["cb"], OPT["mf"]
-    ms(T.tw[:, 0:cw], 0, ["tw"])
-    iota(T.zi[:, :], [[-4, 4], [-16, 8]], 0, 1, ["zi"])
-    if cw < W: iota(T.tw[:, cw:W], [[0, W - cw]], 0, 0, ["tw1"])
+    ZB, ZC, ZO, ZU = 0, 144, 288, 432
+    cw, cb = OPT["cw"], OPT["cb"]
+    ms(T.sm[:, 0:32], 1.0, ["s0"]); ms(T.tw[:, 0:cw], 0, ["tw"])
+    iota(T.tw[:, cw:W], [[0, W - cw]], 0, 0, ["tw1"]); iota(T.zi[:, :], [[-4, 5], [-16, 8]], 132, 1, ["zi"])
     load("a", "wki", T.wk); load("s", "bh", T.b0); load("s", "rb", T.rec)
-    load("a", "ths", T.th)
-    for lo, hi, a, e in ((0, cut, rank, 8), (cut, 128, 0, rank)):
-        if a < e:
-            dma("a", T.tw[lo:hi:8, :], T.hop[a:e, :], "tw", w=["tw", "tw1"])
-            dma("s", T.tw[lo + 4:hi:16, :], T.up[a:e, :], "tw", w=["tw", "tw1"])
-            dma("s", T.tw[lo + 12:hi:16, :], T.dn[a:e, :], "tw", w=["tw", "tw1"])
+    act(T.dd[:, 528:560], T.sm[:, 0:32], AF.Silu, ["s0"], ["dd1"])
+    for rows, src in ((T.tw[0:128:8, :], T.hop), (T.tw[4:128:16, :], T.dn), (T.tw[12:128:16, :], T.up)):
+        dma("s", rows, src[:, :], "tw", w=["tw", "tw1"])
     load("s", "wb", T.w)
+    dma("s", T.ths[:, 0:1], T.th[:, :], "ths", w=["ths"])
+    for lo, hi, a in SHIFT: dma("s", T.ths[lo:hi, 1:2], T.th[a:a + hi - lo, :], "ths", w=["ths"])
+    for lo, hi, a in SHIFT: dma("s", T.wu[lo:hi, :], T.w[a:a + hi - lo, :], "wu", w=["wu"])
+    ms(T.zz[:, :], 0.0, ["zz"]); cp(T.zt[:, :], T.zz[:, :], ["zz"], ["zt"])
+    act(T.zero[:, :], T.zz[:, 0:K], AF.Copy, ["zz"], ["zero"])
+    cp(T.dq0[:, :], T.wki[:, :], ["wki"], ["dq0"])
+    ts(T.zi[:, :], T.zi[:, :], 127, ALU.bitwise_and, ["zi"], ["zi"])
+    ts(T.zt[:, 15:640:16], T.zi[:, :], 0.0, ALU.is_equal, ["zi", "zt"], ["zt"])
     iota(T.idn[:, :], [[0, 128]], 1, 0, ["idn"], **fl); keep(T.idn[:, :], [[-1, 128]], ALU.is_equal, 0.0, 0, 1, ["idn"])
-    iota(T.zz[:, :], [[0, 432]], 0, 0, ["zz"], **fl)
-    for off, wt in ((ZC, -W * U), (ZO, -2.0 ** 11)):
-        keep(T.zz[:, off + 15:off + 128:16], [[16, 8]], ALU.is_gt, wt, 0, -1, ["zz"])
-        keep(T.zz[:, off + 15:off + 128:16], [[16, 8]], ALU.is_ge, 0.0, 15, -1, ["zz"])
-    for row, wt in ((0, 16.0), (1, 1.0)): keep(T.zz[:, ZB + 15:ZB + 128:16], [[-16, 8]], ALU.not_equal, wt, -row, 1, ["zz"])
+    band(ZO, 0, 8, -2.0 ** 11, ["zz"]); band(ZC, 0, 8, -W * U, ["zz"])
+    iota(T.m0[:, 0:K], [[0, K]], 63, 0, ["m0"], **fl)
+    for a in range(K, W, K): dma("s", T.m0[:, a:a + K], T.m0[:, 0:K], "m0", r=["m0"], w=["m0w"])
     iota(T.jlo[:, :], [[0, 2], [1, 16]], 32, 0, ["jlo"], **fl); iota(T.jc[:, :], [[1, 32], [0, 16]], 32, 0, ["jc"], **fl)
     dma("s", T.jc[1:128:16, :], T.jlo[:, :], "jc", r=["jlo"], w=["jc"])
-    if mf > K: iota(T.m0[:, K:mf], [[0, mf - K]], 63, 0, ["m0"], **fl)
-    ms(T.zero[:, :], 0.0, ["zero"]); ms(T.m0[:, 0:K], 63.0, ["m0v"])
-    act(T.held[:, :], T.zero[:, :], AF.Silu, ["zero"], ["held"], bias=64.0)
-    cp(T.zt[:, 0:K], T.zero[:, :], ["zero"], ["zt"]); cp(T.zt[:, K:528], T.zero[:, 0:16], ["zero"], ["zt1"])
-    cp(T.dq0[:, :], T.wki[:, :], ["wki"], ["dq0"])
-    ts(T.zt[:, 15:K:16], T.zi[:, :], 0.0, ALU.is_equal, ["zi", "zt", "zt1"], ["zt"])
-    ts(T.df0[:, :], T.wki[:, :], U, ALU.mult, ["wki"], ["df0"])
     cp(T.b[:, cb:W], T.bh[:, cb:W], ["bh"], ["b1"])
 
     for s in range(RO):
         last = s == RO - 1
-        dq, xl, xs, h, hu, hd, df, m = ("%s%d" % (x, s) for x in ("dq", "xl", "xs", "h", "hu", "hd", "df", "m"))
+        dq, xl, xs, h, hu, hd, df, m, dl = ("%s%d" % (x, s) for x in ("dq", "xl", "xs", "h", "hu", "hd", "df", "m", "dl"))
         D = T[dq][:, :]
-        X = [(xl + "a", T[xs][:, 0:32], xs + "a", h, 32), (xl + "b", T[xs][:, 32:64], xs + "b", h, 32),
-             (xl + "c", T[hu][:, 0:32], hu, hu, 32), (xl + "d", T[hd][:, K:K + 32], hd, hd, 0)]
-        acts, late, mk, pcs, split = (OPT[x][s] for x in ("act", "late", "marks", "pc", "split")); cdone = [0]
+        X = [(xl + "a", T[xs][:, 0:32], xs, h, 32), (xl + "b", T[xs][:, 32:64], xs, h, 32),
+             (xl + "c", T[hu][:, K:K + 32], hu, hu, 0), (xl + "d", T[hd][:, 0:32], hd, hd, 32)]
+        acts, mk, pcs = (OPT[x][s] for x in ("act", "marks", "pc"))
 
-        def lst(k, a=0, e=K): return T[xl][:, 32 * k + a // 16:32 * k + e // 16]
+        def lst(k, a=0, e=K): o = (0, 32, 64, 128, 96)[k]; return T[xl][:, o + a // 16:o + e // 16]
         def grad(k, a=0, e=K, p=""):
-            tt(T["g%d" % k][:, a:e], ind("wb", lst(k, a, e)), T[X[k][3]][:, X[k][4] + a:X[k][4] + e], ALU.mult, ["wb", X[k][0], X[k][3]], ["g%d" % k + p])
+            wt, l = ("wu", lst(4)) if k == 2 else ("wb", lst(k, a, e))
+            tt(T["g%d" % k][:, a:e], ind(wt, l), T[X[k][3]][:, X[k][4] + a:X[k][4] + e], ALU.mult, [wt, X[k][0], X[k][3]], ["g%d" % k + p])
+            if k == 2:
+                for lo, hi, a in SHIFT: dma("s", T.gu[a:a + hi - lo, :], T.g2[lo:hi, :], "gu%d" % s, r=["g2"], w=["gu"])
         def size(k, a=0, e=K, p=""):
             ab = "ab%d" % (k % 2)
             act(T[ab][:, a:e], T["g%d" % k][:, a:e], AF.Abs, ["g%d" % k + p], [ab + p])
         def over(k, a=0, e=K, p=""):
-            ab = "ab%d" % (k % 2); big = "big%d" % (k % 2)
+            ab = "ab%d" % (k % 2); big = "big%d" % (k % 2); j = int(k == 2)
             if k in acts:
-                act(T[ab][:, a:e], T[ab][:, a:e], AF.Relu, [ab + p, "nth"], [ab + p], bias=T.nth[:, :])
+                act(T[ab][:, a:e], T[ab][:, a:e], AF.Relu, [ab + p, "nth"], [ab + p], bias=T.nth[:, j:j + 1])
                 act(T[big][:, a:e], T[ab][:, a:e], AF.Sign, [ab + p], [big + p])
-            else: ts2(T[big][:, a:e], T[ab][:, a:e], T.ths[:, :], ALU.is_gt, -9.0 / 16, ALU.add, [ab + p, "ths"], [big + p])
-        def place(k):
+            else: ts2(T[big][:, a:e], T[ab][:, a:e], T.ths[:, j:j + 1], ALU.is_gt, -9.0 / 16, ALU.add, [ab + p, "ths"], [big + p])
+        def place(k, st=True):
             bank = "pd%d" % (k % 2)
-            mm(T[bank][:, 0:32], T.idn[:, :], X[k][1], True, False, ["idn", X[k][2]], [bank])
+            mm(T[bank][:, 0:32], T.idn[:, :], X[k][1], st, False, ["idn", X[k][2]], [bank])
             if k in acts: mm(T[bank][:, 0:32], T.idn[:, :], T.nine[:, :], False, False, ["idn", "nine"], [bank])
-        def count(k, sp=False): tolist("pd%d" % (k % 2), 0, "zz", ZC, "big%d" % (k % 2), K, False, sp)
-        def old(k, sp=True):
-            e = H if k in split else K
-            act(T.ao[:, 0:e], ind("b", lst(k, 0, e)), AF.Abs, ["b", X[k][0]], ["aoh0"] if e < K else ["ao"], scale=2.0 ** 99)
-            if e < K: ts(T.ao[:, e:K], ind("b", lst(k, e, K)), 0.0, ALU.not_equal, ["b", X[k][0]], ["aoh1"])
-            tolist("pd%d" % (k % 2), 0, "zz", ZO, "ao", K, False, sp)
+        def count(k, sp=False):
+            big = "big%d" % (k % 2)
+            tolist("pd%d" % (k % 2), 0, "zz", ZU if k == 2 else ZC, big, K, False, sp, [big] + ["zu"] * (k == 2))
+        def old(k, sp=True, st=False):
+            act(T.ao[:, :], ind("b", lst(k)), AF.Abs, ["b", X[k][0]], ["ao"], scale=2.0 ** 99)
+            tolist("pd%d" % (k % 2), 0, "zz", ZO, "ao", K, st, sp)
         def base(k): act(T.bo[:, :], ind("b", lst(k)), AF.Copy, ["b", X[k][0]], ["bo"])
         def aim(k):
             tt(T.aim[:, :], T["pd%d" % (k % 2)][:, 0:32], X[k][1], ALU.max, ["pd%d" % (k % 2), X[k][2]], ["aim"])
             ts(T.to[:, :], T.aim[:, :], 1 / U, ALU.mult, ["aim"], ["to"])
-        def put(k): tt(ind("b", T.to[:, :], 10 * W), T.bo[:, :], T["g%d" % k][:, :], ALU.add, ["bo", "g%d" % k, "to"], ["b"])
+        def put(k):
+            gk = "gu" if k == 2 else "g%d" % k
+            tt(ind("b", T.to[:, :], 10 * W), T.bo[:, :], T[gk][:, :], ALU.add, ["bo", gk, "to"], ["b"])
         def mark(i):
             if last or mk[i] == mk[i + 1]: return
             a, e = mk[i], mk[i + 1]
-            if a < 32: z = min(e, 32); act(ind(m, T[xl][:, a:z]), T.jc[:, 16 * a:16 * z], AF.Silu, [xl + "a", "jc", m, "m0v", "m0w"], [m])
-            if e > 32: z = max(a, 32) - 32; act(ind(m, T[dq][:, z:e - 32]), T.held[:, 16 * z:16 * (e - 32)], AF.Silu, [dq, "held", m], [m])
+            if a < 32: z = min(e, 32); act(ind(m, T[xl][:, a:z]), T.jc[:, 16 * a:16 * z], AF.Silu, [xl + "a", "jc", m, "m0w"], [m])
+            if e > 32: z = max(a, 32) - 32; act(ind(m, T[dq][:, z:e - 32]), T.zero[:, 16 * z:16 * (e - 32)], AF.Silu, [dq, "zero", m], [m])
         def marked():
-            act(T.mg[:, :], ind(m, T[xl][:, 0:64]), AF.Copy, [m, xl + "a", xl + "b"], ["mg"]); tolist("pl", 0, "zz", ZB, "mg", 2 * K)
-        def oldc():
-            if s: act(T.cd[:, :], ind("c", D), AF.Copy, ["c", dq], ["cd"])
+            act(T.mg[:, :], ind(m, T[xl][:, 0:64]), AF.Copy, [m, xl + "a", xl + "b"], ["mg"])
+            tolist("pl", 0, "zz", ZB, "mg", 2 * K, r=["mg", "zb"])
+        def oldc(t): act(T.cd[:, :], ind("c", T["dq%d" % t][:, :]), AF.Copy, ["c", "dq%d" % t], ["cd"])
         def putc(i):
-            a = cdone[0]; e = a + pcs[i]; cdone[0] = e
-            if a == e: return
-            o = ind("c", T[dq][:, a // 16:e // 16])
-            if s: tt(o, T.cd[:, a:e], T.dl[:, a:e], ALU.add, ["cd", "dl", dq], ["c"])
-            else: cp(o, T.dl[:, a:e], ["dl", dq, "c"], ["c"])
-            if last and e == K: store("s", "c", "yc")
+            for t, a, e in pcs.get(i, ()):
+                d = "dl%d" % t; o = ind("c", T["dq%d" % t][:, a // 16:e // 16])
+                if t: tt(o, T.cd[:, a:e], T[d][:, a:e], ALU.add, ["cd", d, "dq%d" % t], ["c"])
+                else: cp(o, T[d][:, a:e], [d, "dq%d" % t, "c"], ["c"])
+                if t == RO - 1 and e == K: store("s", "c", "yc")
         def tables():
             cp(T.tg[:, :], ind("tw", D), ["tw", dq], ["tg"])
-            for bank, row in (("pl", 1), ("px0", 0), ("pv", 3), ("px1", 2)): tolist(bank, 0, "zt", 128 * row, "tg", K)
-        def uplist(): ts(T[h][:, 0:32], T.pl[:, 0:32], U, ALU.mult, ["pl"], [h + "u"])
-        def far(k): ts(lst(k), X[k][1], 1 / U, ALU.mult, [X[k][2]], [X[k][0]]); grad(k)
+            if s: tolist("px", 0, "zt", 128, "tg", K)
+            tolist("pl", 0, "zt", 0, "tg", K); tolist("pl", 32, "zt", 512, "tg", K)
+            if not s: tolist("px", 0, "zt", 128, "tg", K)
+        def first():
+            cp(T[xl][:, 0:32], T.px[:, 0:32], ["px"], [xl + "a"])
+            tolist("px", 32, "zt", 384, "tg", K); tolist("pv", 0, "zt", 256, "tg", K)
+        def far(k):
+            if k == 2: ts(T[xl][:, 64:128], T[hu][:, K:K + 64], 1 / U, ALU.mult, [hu], [X[k][0]])
+            else: ts(lst(k), X[k][1], 1 / U, ALU.mult, [X[k][2]], [X[k][0]])
+            grad(k)
 
         src = "b" if s else "bh"
         act(T.nb[:, :], ind(src, D), AF.Copy, [src, dq], ["nb"], scale=-1.0)
         if s: tables()
-        if not s: act(T.b[:, 0:cb], T.bh[:, 0:cb], AF.Copy, ["bh"], ["b"])
+        else: act(T.b[:, 0:cb], T.bh[:, 0:cb], AF.Copy, ["bh"], ["b"])
         act(ind("b", D), T.zero[:, :], AF.Silu, ["zero", dq, "b", "b1"], ["b"])
-        tt(T.dl[:, :], ind("rb", D), T.nb[:, :], ALU.mult, ["rb", dq, "nb"], ["dl"])
-        if not s: tables()
-        if s: uplist()
-        tt(T[h][:, 32:32 + K], ind("wb", D), T.dl[:, :], ALU.mult, ["wb", dq, "dl"], [h])
-        if not s: uplist()
-        send(up, hu, T[hu][:, :], T[h][:, 0:32 + K], [h, h + "u"])
-        cp(T[xl][:, 0:32], T.px0[:, 0:32], ["px0"], [xl + "a"])
-        grad(0, 0, H, "h0")
-        ts(T[h][:, 32 + K:64 + K], T.pv[:, 0:32], U, ALU.mult, ["pv"], [h + "d"])
-        send(dn, "land%d" % s, T.land[s], T[h][:, 32:64 + K], [h, h + "d"])
-        act(T[xs][:, 0:32], T.px0[:, 0:32], AF.Copy, ["px0"], [xs + "a"], scale=U)
-        place(0); old(0, False)
-        grad(0, H, K, "h1")
-        cp(T[xl][:, 32:64], T.px1[:, 0:32], ["px1"], [xl + "b"])
-        if acts and not any(OPT["act"][:s]): act(T.nth[:, :], T.ths[:, :], AF.Copy, ["ths"], ["nth"], scale=-1.0)
+        tt(T[dl][:, :], ind("rb", D), T.nb[:, :], ALU.mult, ["rb", dq, "nb"], [dl])
+        if s: first()
+        else: tables()
+        tt(T[h][:, 32:32 + K], ind("wb", D), T[dl][:, :], ALU.mult, ["wb", dq, dl], [h])
+        if s: act(T[h][:, 32 + K:96 + K], T.pl[:, 0:64], AF.Copy, ["pl"], [h + "u"], scale=U)
+        else: ts(T[h][:, 32 + K:96 + K], T.pl[:, 0:64], U, ALU.mult, ["pl"], [h + "u"]); first()
+        send(up, hu, T[h][:, 32:96 + K], [h, h + "u"])
+        grad(0, 0, H, "h0"); grad(0, H, K, "h1")
+        old(0, False, True)
+        cp(T[xl][:, 32:64], T.px[:, 32:64], ["px"], [xl + "b"])
+        putc("p")
         size(0, 0, H, "h0"); size(0, H, K, "h1")
-        over(0, 0, H, "h0"); over(0, H, K, "h1"); count(0, True)
+        act(T[xs][:, :], T.px[:, 0:64], AF.Copy, ["px"], [xs], scale=U)
+        act(T[h][:, 0:32], T.pv[:, 0:32], AF.Copy, ["pv"], [h + "d"], scale=U)
+        send(dn, hd, T[h][:, 0:32 + K], [h, h + "d"])
+        over(0, 0, H, "h0"); over(0, H, K, "h1"); place(0, False); count(0, True)
         base(0)
-        act(T[xs][:, 32:64], T.px1[:, 0:32], AF.Copy, ["px1"], [xs + "b"], scale=U)
         if not s:
-            if mf < W: iota(T.m0[:, mf:W], [[0, W - mf]], 63, 0, ["m0w"], **fl)
-            iota(T.nine[:, :], [[0, 32]], 0, 0, ["nine"], **fl); keep(T.nine[:, :], [[0, 32]], ALU.is_gt, 9 * W * U, 0, 0, ["nine"])
+            band(ZU, 1, 8, -W * U, ["zu"]); keep(T.zz[:, ZU + 15:ZU + 16], [[1, 1]], ALU.is_gt, -W * U, 112, -1, ["zu"])
             iota(T.c[:, :], [[0, W]], 0, 0, ["c"], **fl)
-            iota(T.dd[:, K:544], [[0, 32]], 1, 0, ["dd1"], **fl); iota(T.dd[:, 544:560], [[0, 16]], -1, 0, ["dd2"], **fl)
+            for row, wt in ((0, 16.0), (1, 1.0)): keep(T.zz[:, ZB + 15:ZB + 128:16], [[-16, 8]], ALU.not_equal, wt, -row, 1, ["zb"])
+            iota(T.dd[:, 0:16], [[0, 16]], -1, 0, ["dd2"], **fl)
+            iota(T.nine[:, :], [[0, 32]], 0, 0, ["nine"], **fl); keep(T.nine[:, :], [[0, 32]], ALU.is_gt, 9 * W * U, 0, 0, ["nine"])
             iota(T.m1[:, :], [[0, W]], 63, 0, ["m1"], **fl)
-        arrives(dn, hu); arrives(up, "land%d" % s)
-        dma("s", T[hd][16:128, :], T.land[s, 0:112, :], hd, r=["land%d" % s], w=[hd])
-        dma("s", T[hd][0:16, :], T.land[s, 112:128, :], hd, r=["land%d" % s], w=[hd])
+        arrives(dn, hu); arrives(up, hd)
         sm = [T.sm[:, 32 * i:32 * i + 32] for i in range(8)]
-        grad(1); putc(0)
-        for k in range(4):
-            aim(k)
-            if k == 3:
-                put(k)
-                if not last: mark(3); marked()
-                break
-            if k + 1 in late:
-                put(k)
-                if k == OPT["oc"]: oldc()
-                mark(k); far(k + 1); place(k + 1); old(k + 1, False); size(k + 1); base(k + 1); over(k + 1); count(k + 1, True)
-            else:
-                size(k + 1); put(k); over(k + 1); place(k + 1); count(k + 1)
-                if k == OPT["oc"]: oldc()
-                mark(k); old(k + 1); base(k + 1)
-            putc(k + 1)
-            if k < 2 and k + 2 not in late: far(k + 2)
-            if k == 2 and not last:
-                tt(T.ee[:, 0:32], T[df][:, :], T[xs][:, 0:32], ALU.subtract, [xs + "a", df], ["e0"])
-                tt(T.ee[:, 32:64], T[xs][:, 32:64], T[df][:, :], ALU.subtract, [xs + "b", df], ["e1"])
+        grad(1)
+        for k in range(3):
+            aim(k); size(k + 1); put(k); over(k + 1); place(k + 1); count(k + 1)
+            if (s, k) in OPT["oc"]: oldc(OPT["oc"][s, k])
+            mark(k); old(k + 1); base(k + 1)
+            if k == 0: putc(1)
+            if k < 2: far(k + 2)
+            if k: putc(k + 1)
+        if not last:
+            if not s: ts(T.df0[:, :], T.wki[:, :], U, ALU.mult, ["wki"], ["df0"])
+            tt(T.ee[:, 0:32], T[df][:, :], T[xs][:, 0:32], ALU.subtract, [xs, df], ["e0"])
+            tt(T.ee[:, 32:64], T[xs][:, 32:64], T[df][:, :], ALU.subtract, [xs, df], ["e1"])
+        aim(3); put(3)
         if last:
             store("s", "b", "yb", 0, W // 2); store("a", "b", "yb", W // 2, W)
             break
+        mark(3); marked()
         act(T.ab0[:, :], ind("b", lst(0)), AF.Abs, ["b", X[0][0]], ["ab0"])
         cp(T.ab1[:, :], ind("b", lst(1)), ["b", X[1][0]], ["ab1"])
         pp = ((0, H, "pc0", "h0"), (H, K, "pc1", "h1"))
         for a, e, u, p in pp: act(T[u][:, a:e], T.ab1[:, a:e], AF.Abs, ["ab1"], [u])
-        ts(T.lk[:, :], T.pl[:, 32:64], -544.0, ALU.add, ["pl"], ["lk"])
-        ts(sm[0], T.pl[:, 0:32], 1080.0, ALU.is_lt, ["pl"], ["s0"])
-        for a, e, u, p in pp: tt(T.dd[:, a:e], T[u][:, a:e], T.ab0[:, a:e], ALU.subtract, [u, "ab0"], ["dd" + p])
+        ts(T.lk[:, :], T.pl[:, 32:64], -528.0, ALU.add, ["pl"], ["lk"])
+        ts(sm[0], T.pl[:, 0:32], 64.0, ALU.is_gt, ["pl"], ["s0"])
+        for a, e, u, p in pp: tt(T.dd[:, 16 + a:16 + e], T[u][:, a:e], T.ab0[:, a:e], ALU.subtract, [u, "ab0"], ["dd" + p])
         kv = OPT["kv"]; eps = 2.0 ** -116
         act(T.sg[:, K + kv:2 * K], ind("dd", T.lk[:, kv // 16:32], 560), AF.Sign, ["dd", "dd1", "dd2", "lk"], ["sga"])
-        ts2(T.sg[:, 0:K], T.dd[:, 0:K], eps, ALU.min, -eps, ALU.max, ["dd"], ["sgo"])
+        ts2(T.sg[:, 0:K], T.dd[:, 16:16 + K], eps, ALU.min, -eps, ALU.max, ["dd"], ["sgo"])
         if kv: ts2(T.sg[:, K:K + kv], ind("dd", T.lk[:, 0:kv // 16], 560), eps, ALU.min, -eps, ALU.max, ["dd", "dd1", "dd2", "lk"], ["sgv"])
         tolist("pv", 0, "zz", ZO, "sg", 2 * K, r=["sga", "sgo", "sgv"])
         tt(T.ee[:, 0:32], T.ee[:, 0:32], sm[0], ALU.mult, ["s0", "e0"], ["e0"])
         tt(sm[1], T[df][:, :], T.ee[:, 0:32], ALU.subtract, ["e0", df], ["s1"])
         putc(4)
-        assert cdone[0] == K
+        if s == RO - 2: act(T.nth[:, :], T.ths[:, :], AF.Copy, ["ths"], ["nth"], scale=-1.0)
         ts(T.sm[:, 64:128], T.pv[:, 0:64], 0.0, ALU.is_lt, ["pv"], ["s2"])
         tt(T.sm[:, 128:192], T.sm[:, 64:128], T.ee[:, :], ALU.mult, ["s2", "e0", "e1"], ["s4"])
         tt(sm[6], sm[5], sm[2], ALU.mult, ["s2", "s4"], ["s6"])

@@ -9,12 +9,12 @@ SCRATCH = {
     "rb": ("sbuf", [128, W], BF), "nth": ("sbuf", [128, 2], F32), "ths": ("sbuf", [128, 2], F32), "wki": ("sbuf", [128, 32], I32),
     "zero": ("sbuf", [128, K], F32), "jc": ("sbuf", [128, K], F32), "jlo": ("sbuf", [128, 32], F32),
     "zi": ("sbuf", [128, 40], I32), "idn": ("sbuf", [128, 128], F32), "gu": ("sbuf", [128, K], F32),
-    "zt": ("sbuf", [128, 656], F16), "zz": ("sbuf", [128, 656], BF), "nine": ("sbuf", [128, 32], F32),
+    "zt": ("sbuf", [128, 656], F16), "zz": ("sbuf", [128, 864], BF), "nine": ("sbuf", [128, 32], F32),
     "nb": ("sbuf", [128, K], F32), "cd": ("sbuf", [128, K], F32), "tg": ("sbuf", [128, K], F16),
     "ab0": ("sbuf", [128, K], F32), "ab1": ("sbuf", [128, K], F32), "big0": ("sbuf", [128, K], BF), "big1": ("sbuf", [128, K], BF),
     "ao": ("sbuf", [128, K], BF), "bo": ("sbuf", [128, K], F32), "aim": ("sbuf", [128, 32], F32), "to": ("sbuf", [128, 32], U16),
     "mg": ("sbuf", [128, 2 * K], BF), "dd": ("sbuf", [128, 560], BF), "sg": ("sbuf", [128, 2 * K], BF),
-    "ee": ("sbuf", [128, 64], F32), "sm": ("sbuf", [128, 256], F32), "lk": ("sbuf", [128, 32], U16),
+    "ee": ("sbuf", [128, 96], F32), "pick": ("sbuf", [128, 96], F32), "sm": ("sbuf", [128, 256], F32), "lk": ("sbuf", [128, 32], U16),
 }
 HALVED = ("g0", "ab0", "big0", "dd")
 PSUM = ("pc0", "pc1", "pd0", "pd1", "px", "pl", "pv")
@@ -34,8 +34,9 @@ for _s in range(RO):
 LOADS = ["wki", "bh", "rb", "wb", "wu", "m0", "tw", "ths", "jc", "yb", "yc"]
 SEMAPHORES = (["qv", "qa", "qp", "qg", "sent"] + ["d_" + n for n in LOADS] + ["d_gu%d" % s for s in range(RO)]
               + ["r_%s%d" % (n, s) for n in ("hu", "hd") for s in range(RO)])
-OPT = dict(cw=1408, cb=1280, kv=96, oc={(1, 2): 1, (2, 0): 2}, act=((), (), (2, 3)),
-           marks=((0, 22, 44, 64, 64), (0, 26, 52, 56, 64), None),
+OPT = dict(cw=1280, cb=1152, kv=160, oc={(1, 2): 1, (2, 0): 2}, act=({}, {}, {2: 448, 3: K}),
+           bv=((0, 0, 32, 96), (0, 32, 64, 128), (0, 0, 0, 0)),
+           marks=((0, 22, 44, 64, 64), (0, 24, 48, 56, 64), None),
            pc=({3: [(0, 0, 256)], 4: [(0, 256, 384)]}, {"p": [(0, 384, K)], 3: [(1, 0, 256)], 4: [(1, 256, 384)]},
                {"p": [(1, 384, K)], 2: [(2, 0, 128)], 3: [(2, 128, K)]}))
 SHIFT = ((0, 112, 16), (112, 128, 0))
@@ -108,9 +109,9 @@ def rank_program(g, core, T, topo):
         e = topo.engines(src, dst)
         return e if topo.chip(src) != topo.chip(dst) else [x for x in e if x not in far]
 
-    def send(dst, name, src, r):
+    def send(dst, name, src, r, a=0, z=None):
         e = engines(core, dst); rid, pid = topo.addr(dst)[:2]; m = sum(1 << x for x in e)
-        op("g", lambda: g.remote_dma(T[name][:, :], src, T.sem["r_" + name], T.sem.sent, pid, rid, m), r=r, sem="sent", cnt=len(e), inc=False)
+        op("g", lambda: g.remote_dma(T[name][:, a:z], src, T.sem["r_" + name], T.sem.sent, pid, rid, m), r=r, sem="sent", cnt=len(e), inc=False)
 
     def arrives(src, name):
         op("r", None, w=[name], sem="r_" + name, cnt=len(engines(src, core)))
@@ -144,9 +145,10 @@ def rank_program(g, core, T, topo):
         keep(o, [[16, q1 - q0]], ALU.is_gt, wt, 0, -1, w); keep(o, [[16, q1 - q0]], ALU.is_ge, 0.0, 15, -1, w)
 
     fl = {"allow_small_or_imprecise_dtypes": True}
-    ZB, ZC, ZO, ZU = 0, 144, 288, 432
+    ZB, ZO, ZC, ZU = 0, 144, 288, 432
+    FINE = 288
     cw, cb = OPT["cw"], OPT["cb"]
-    ms(T.sm[:, 0:32], 1.0, ["s0"]); ms(T.tw[:, 0:cw], 0, ["tw"])
+    ms(T.sm[:, 0:32], 1.0, ["s0"]); ms(T.zz[:, 0:656], 0.0, ["zz"]); ms(T.tw[:, 0:cw], 0, ["tw"])
     iota(T.tw[:, cw:W], [[0, W - cw]], 0, 0, ["tw1"]); iota(T.zi[:, :], [[-4, 5], [-16, 8]], 132, 1, ["zi"])
     load("a", "wki", T.wk); load("s", "bh", T.b0); load("s", "rb", T.rec)
     act(T.dd[:, 528:560], T.sm[:, 0:32], AF.Silu, ["s0"], ["dd1"])
@@ -156,14 +158,13 @@ def rank_program(g, core, T, topo):
     dma("s", T.ths[:, 0:1], T.th[:, :], "ths", w=["ths"])
     for lo, hi, a in SHIFT: dma("s", T.ths[lo:hi, 1:2], T.th[a:a + hi - lo, :], "ths", w=["ths"])
     for lo, hi, a in SHIFT: dma("s", T.wu[lo:hi, :], T.w[a:a + hi - lo, :], "wu", w=["wu"])
-    ms(T.zz[:, :], 0.0, ["zz"]); cp(T.zt[:, :], T.zz[:, :], ["zz"], ["zt"])
     act(T.zero[:, :], T.zz[:, 0:K], AF.Copy, ["zz"], ["zero"])
-    cp(T.dq0[:, :], T.wki[:, :], ["wki"], ["dq0"])
+    cp(T.dq0[:, :], T.wki[:, :], ["wki"], ["dq0"]); cp(T.zt[:, :], T.zz[:, 0:656], ["zz"], ["zt"])
     ts(T.zi[:, :], T.zi[:, :], 127, ALU.bitwise_and, ["zi"], ["zi"])
     ts(T.zt[:, 15:640:16], T.zi[:, :], 0.0, ALU.is_equal, ["zi", "zt"], ["zt"])
     iota(T.idn[:, :], [[0, 128]], 1, 0, ["idn"], **fl); keep(T.idn[:, :], [[-1, 128]], ALU.is_equal, 0.0, 0, 1, ["idn"])
-    band(ZO, 0, 8, -2.0 ** 11, ["zz"]); band(ZC, 0, 8, -W * U, ["zz"])
     iota(T.m0[:, 0:K], [[0, K]], 63, 0, ["m0"], **fl)
+    band(ZO, 0, 8, -2.0 ** 15, ["zz"]); band(ZC, 0, 8, -1.0 * W, ["zz"])
     for a in range(K, W, K): dma("s", T.m0[:, a:a + K], T.m0[:, 0:K], "m0", r=["m0"], w=["m0w"])
     iota(T.jlo[:, :], [[0, 2], [1, 16]], 32, 0, ["jlo"], **fl); iota(T.jc[:, :], [[1, 32], [0, 16]], 32, 0, ["jc"], **fl)
     dma("s", T.jc[1:128:16, :], T.jlo[:, :], "jc", r=["jlo"], w=["jc"])
@@ -173,8 +174,10 @@ def rank_program(g, core, T, topo):
         last = s == RO - 1
         dq, xl, xs, h, hu, hd, df, m, dl = ("%s%d" % (x, s) for x in ("dq", "xl", "xs", "h", "hu", "hd", "df", "m", "dl"))
         D = T[dq][:, :]
-        X = [(xl + "a", T[xs][:, 0:32], xs, h, 32), (xl + "b", T[xs][:, 32:64], xs, h, 32),
+        X = [(xl + "a", T[xs][:, 0:32], xs, h, 32), (xl + "b", T[xs][:, 32:64], xs + "b" * last, h, 32),
              (xl + "c", T[hu][:, K:K + 32], hu, hu, 0), (xl + "d", T[hd][:, 0:32], hd, hd, 32)]
+        u = U if last else 1.0; zf = FINE if last else 0
+        if not s: df = "wki"
         acts, mk, pcs = (OPT[x][s] for x in ("act", "marks", "pc"))
 
         def lst(k, a=0, e=K): o = (0, 32, 64, 128, 96)[k]; return T[xl][:, o + a // 16:o + e // 16]
@@ -188,27 +191,32 @@ def rank_program(g, core, T, topo):
             act(T[ab][:, a:e], T["g%d" % k][:, a:e], AF.Abs, ["g%d" % k + p], [ab + p])
         def over(k, a=0, e=K, p=""):
             ab = "ab%d" % (k % 2); big = "big%d" % (k % 2); j = int(k == 2)
-            if k in acts:
-                act(T[ab][:, a:e], T[ab][:, a:e], AF.Relu, [ab + p, "nth"], [ab + p], bias=T.nth[:, j:j + 1])
-                act(T[big][:, a:e], T[ab][:, a:e], AF.Sign, [ab + p], [big + p])
-            else: ts2(T[big][:, a:e], T[ab][:, a:e], T.ths[:, j:j + 1], ALU.is_gt, -9.0 / 16, ALU.add, [ab + p, "ths"], [big + p])
+            z = acts.get(k, a)
+            if z > a:
+                act(T[ab][:, a:z], T[ab][:, a:z], AF.Relu, [ab + p, "nth"], [ab + p], bias=T.nth[:, j:j + 1])
+                act(T[big][:, a:z], T[ab][:, a:z], AF.Sign, [ab + p], [big + "a"])
+            if z < e: ts2(T[big][:, z:e], T[ab][:, z:e], T.ths[:, j:j + 1], ALU.is_gt, -9.0 / 16, ALU.add, [ab + p, "ths"], [big + p])
         def place(k, st=True):
             bank = "pd%d" % (k % 2)
             mm(T[bank][:, 0:32], T.idn[:, :], X[k][1], st, False, ["idn", X[k][2]], [bank])
-            if k in acts: mm(T[bank][:, 0:32], T.idn[:, :], T.nine[:, :], False, False, ["idn", "nine"], [bank])
+            if k in acts: mm(T[bank][:, 0:acts[k] // 16], T.idn[:, :], T.nine[:, 0:acts[k] // 16], False, False, ["idn", "nine"], [bank])
         def count(k, sp=False):
             big = "big%d" % (k % 2)
-            tolist("pd%d" % (k % 2), 0, "zz", ZU if k == 2 else ZC, big, K, False, sp, [big] + ["zu"] * (k == 2))
+            tolist("pd%d" % (k % 2), 0, "zz", (zf if k else 0) + (ZU if k == 2 else ZC), big, K, False, sp, [big, big + "a"] + ["zu"] * (k == 2 or last))
         def old(k, sp=True, st=False):
-            act(T.ao[:, :], ind("b", lst(k)), AF.Abs, ["b", X[k][0]], ["ao"], scale=2.0 ** 99)
+            act(T.ao[:, :], ind("b", lst(k)), AF.Abs, ["b", X[k][0]], ["ao"], scale=2.0 ** (95 if last and k else 90))
             tolist("pd%d" % (k % 2), 0, "zz", ZO, "ao", K, st, sp)
-        def base(k): act(T.bo[:, :], ind("b", lst(k)), AF.Copy, ["b", X[k][0]], ["bo"])
+        def base(k): e = K - OPT["bv"][s][k]; act(T.bo[:, 0:e], ind("b", lst(k, 0, e)), AF.Copy, ["b", X[k][0]], ["bo"])
+        def rest(k):
+            e = K - OPT["bv"][s][k]
+            if e < K: cp(T.bo[:, e:K], ind("b", lst(k, e, K)), ["b", X[k][0]], ["bov"])
         def aim(k):
-            tt(T.aim[:, :], T["pd%d" % (k % 2)][:, 0:32], X[k][1], ALU.max, ["pd%d" % (k % 2), X[k][2]], ["aim"])
-            ts(T.to[:, :], T.aim[:, :], 1 / U, ALU.mult, ["aim"], ["to"])
+            o = "aim" if last and k else "to"
+            tt(T[o][:, :], T["pd%d" % (k % 2)][:, 0:32], X[k][1], ALU.max, ["pd%d" % (k % 2), X[k][2]], [o])
+            if last and k: ts(T.to[:, :], T.aim[:, :], 1 / U, ALU.mult, ["aim"], ["to"])
         def put(k):
             gk = "gu" if k == 2 else "g%d" % k
-            tt(ind("b", T.to[:, :], 10 * W), T.bo[:, :], T[gk][:, :], ALU.add, ["bo", gk, "to"], ["b"])
+            tt(ind("b", T.to[:, :], 10 * W), T.bo[:, :], T[gk][:, :], ALU.add, ["bo", "bov", gk, "to"], ["b"])
         def mark(i):
             if last or mk[i] == mk[i + 1]: return
             a, e = mk[i], mk[i + 1]
@@ -226,15 +234,19 @@ def rank_program(g, core, T, topo):
                 if t == RO - 1 and e == K: store("s", "c", "yc")
         def tables():
             cp(T.tg[:, :], ind("tw", D), ["tw", dq], ["tg"])
-            if s: tolist("px", 0, "zt", 128, "tg", K)
-            tolist("pl", 0, "zt", 0, "tg", K); tolist("pl", 32, "zt", 512, "tg", K)
-            if not s: tolist("px", 0, "zt", 128, "tg", K)
+            tolist("px", 0, "zt", 128, "tg", K); tolist("pl", 0, "zt", 0, "tg", K)
+            if s: tolist("pl", 32, "zt", 512, "tg", K)
         def first():
             cp(T[xl][:, 0:32], T.px[:, 0:32], ["px"], [xl + "a"])
-            tolist("px", 32, "zt", 384, "tg", K); tolist("pv", 0, "zt", 256, "tg", K)
+            tolist("px", 32, "zt", 384, "tg", K)
+            if not s: tolist("pl", 32, "zt", 512, "tg", K)
+            tolist("pv", 0, "zt", 256, "tg", K)
+        def uplists(): act(T[h][:, 32 + K:96 + K], T.pl[:, 0:64], AF.Copy, ["pl"], [h + "u"], scale=u)
         def far(k):
-            if k == 2: ts(T[xl][:, 64:128], T[hu][:, K:K + 64], 1 / U, ALU.mult, [hu], [X[k][0]])
-            else: ts(lst(k), X[k][1], 1 / U, ALU.mult, [X[k][2]], [X[k][0]])
+            if k == 2: ts(T[xl][:, 64:128], T[hu][:, K:K + 64], 1 / u, ALU.mult, [hu], [X[k][0]])
+            else: ts(lst(k), X[k][1], 1 / u, ALU.mult, [X[k][2]], [X[k][0]])
+            if k == 2 and not last: tt(T.ee[:, 1:96:3], T[df][:, :], T[xs][:, 0:32], ALU.subtract, [xs, df], ["e0"])
+            if k == 3 and not last: tt(T.ee[:, 0:96:3], T[xs][:, 32:64], T[df][:, :], ALU.subtract, [xs, df], ["e1"])
             grad(k)
 
         src = "b" if s else "bh"
@@ -246,26 +258,34 @@ def rank_program(g, core, T, topo):
         if s: first()
         else: tables()
         tt(T[h][:, 32:32 + K], ind("wb", D), T[dl][:, :], ALU.mult, ["wb", dq, dl], [h])
-        if s: act(T[h][:, 32 + K:96 + K], T.pl[:, 0:64], AF.Copy, ["pl"], [h + "u"], scale=U)
-        else: ts(T[h][:, 32 + K:96 + K], T.pl[:, 0:64], U, ALU.mult, ["pl"], [h + "u"]); first()
-        send(up, hu, T[h][:, 32:96 + K], [h, h + "u"])
-        grad(0, 0, H, "h0"); grad(0, H, K, "h1")
+        if s: uplists(); send(up, hu, T[h][:, 32:96 + K], [h, h + "u"])
+        else: send(up, hu, T[h][:, 32:32 + K], [h], 0, K); first()
+        grad(0)
         old(0, False, True)
         cp(T[xl][:, 32:64], T.px[:, 32:64], ["px"], [xl + "b"])
         putc("p")
         size(0, 0, H, "h0"); size(0, H, K, "h1")
-        act(T[xs][:, :], T.px[:, 0:64], AF.Copy, ["px"], [xs], scale=U)
-        act(T[h][:, 0:32], T.pv[:, 0:32], AF.Copy, ["pv"], [h + "d"], scale=U)
+        e = 32 if last else 64
+        act(T[xs][:, 0:e], T.px[:, 0:e], AF.Copy, ["px"], [xs])
+        if not s: uplists(); send(up, hu, T[h][:, 32 + K:96 + K], [h + "u"], K, K + 64)
+        act(T[h][:, 0:32], T.pv[:, 0:32], AF.Copy, ["pv"], [h + "d"], scale=u)
         send(dn, hd, T[h][:, 0:32 + K], [h, h + "d"])
         over(0, 0, H, "h0"); over(0, H, K, "h1"); place(0, False); count(0, True)
         base(0)
+        if last: act(T[xs][:, 32:64], T.px[:, 32:64], AF.Copy, ["px"], [xs + "b"], scale=u)
         if not s:
-            band(ZU, 1, 8, -W * U, ["zu"]); keep(T.zz[:, ZU + 15:ZU + 16], [[1, 1]], ALU.is_gt, -W * U, 112, -1, ["zu"])
+            band(ZU, 1, 8, -1.0 * W, ["zu"]); keep(T.zz[:, ZU + 15:ZU + 16], [[1, 1]], ALU.is_gt, -1.0 * W, 112, -1, ["zu"])
             iota(T.c[:, :], [[0, W]], 0, 0, ["c"], **fl)
             for row, wt in ((0, 16.0), (1, 1.0)): keep(T.zz[:, ZB + 15:ZB + 128:16], [[-16, 8]], ALU.not_equal, wt, -row, 1, ["zb"])
             iota(T.dd[:, 0:16], [[0, 16]], -1, 0, ["dd2"], **fl)
             iota(T.nine[:, :], [[0, 32]], 0, 0, ["nine"], **fl); keep(T.nine[:, :], [[0, 32]], ALU.is_gt, 9 * W * U, 0, 0, ["nine"])
+            iota(T.pick[:, :], [[0, 96]], 0, 0, ["pick"], **fl)
             iota(T.m1[:, :], [[0, W]], 63, 0, ["m1"], **fl)
+        if s == 1:
+            iota(T.zz[:, 656:864], [[0, 208]], 0, 0, ["zu"], **fl)
+            band(FINE + ZC, 0, 8, -W * U, ["zu"]); band(FINE + ZU, 1, 8, -W * U, ["zu"])
+            keep(T.zz[:, FINE + ZU + 15:FINE + ZU + 16], [[1, 1]], ALU.is_gt, -W * U, 112, -1, ["zu"])
+        if not s: arrives(dn, hu)
         arrives(dn, hu); arrives(up, hd)
         sm = [T.sm[:, 32 * i:32 * i + 32] for i in range(8)]
         grad(1)
@@ -273,13 +293,11 @@ def rank_program(g, core, T, topo):
             aim(k); size(k + 1); put(k); over(k + 1); place(k + 1); count(k + 1)
             if (s, k) in OPT["oc"]: oldc(OPT["oc"][s, k])
             mark(k); old(k + 1); base(k + 1)
-            if k == 0: putc(1)
+            if k == 0:
+                rest(1)
+                if s and not last: cp(T[df][:, :], D, [dq], [df])
             if k < 2: far(k + 2)
-            if k: putc(k + 1)
-        if not last:
-            if not s: ts(T.df0[:, :], T.wki[:, :], U, ALU.mult, ["wki"], ["df0"])
-            tt(T.ee[:, 0:32], T[df][:, :], T[xs][:, 0:32], ALU.subtract, [xs, df], ["e0"])
-            tt(T.ee[:, 32:64], T[xs][:, 32:64], T[df][:, :], ALU.subtract, [xs, df], ["e1"])
+            if k: putc(k + 1); rest(k + 1)
         aim(3); put(3)
         if last:
             store("s", "b", "yb", 0, W // 2); store("a", "b", "yb", W // 2, W)
@@ -291,21 +309,19 @@ def rank_program(g, core, T, topo):
         for a, e, u, p in pp: act(T[u][:, a:e], T.ab1[:, a:e], AF.Abs, ["ab1"], [u])
         ts(T.lk[:, :], T.pl[:, 32:64], -528.0, ALU.add, ["pl"], ["lk"])
         ts(sm[0], T.pl[:, 0:32], 64.0, ALU.is_gt, ["pl"], ["s0"])
+        tt(T.ee[:, 1:96:3], T.ee[:, 1:96:3], sm[0], ALU.mult, ["s0", "e0"], ["e0"])
         for a, e, u, p in pp: tt(T.dd[:, 16 + a:16 + e], T[u][:, a:e], T.ab0[:, a:e], ALU.subtract, [u, "ab0"], ["dd" + p])
+        act(T.sg[:, 0:H], T.dd[:, 16:16 + H], AF.Sign, ["ddh0"], ["sgh"])
         kv = OPT["kv"]; eps = 2.0 ** -116
         act(T.sg[:, K + kv:2 * K], ind("dd", T.lk[:, kv // 16:32], 560), AF.Sign, ["dd", "dd1", "dd2", "lk"], ["sga"])
-        ts2(T.sg[:, 0:K], T.dd[:, 16:16 + K], eps, ALU.min, -eps, ALU.max, ["dd"], ["sgo"])
+        ts2(T.sg[:, H:K], T.dd[:, 16 + H:16 + K], eps, ALU.min, -eps, ALU.max, ["dd"], ["sgo"])
         if kv: ts2(T.sg[:, K:K + kv], ind("dd", T.lk[:, 0:kv // 16], 560), eps, ALU.min, -eps, ALU.max, ["dd", "dd1", "dd2", "lk"], ["sgv"])
-        tolist("pv", 0, "zz", ZO, "sg", 2 * K, r=["sga", "sgo", "sgv"])
-        tt(T.ee[:, 0:32], T.ee[:, 0:32], sm[0], ALU.mult, ["s0", "e0"], ["e0"])
-        tt(sm[1], T[df][:, :], T.ee[:, 0:32], ALU.subtract, ["e0", df], ["s1"])
+        tolist("pv", 0, "zz", ZO, "sg", 2 * K, r=["sga", "sgo", "sgv", "sgh"])
+        tt(T.ee[:, 2:96:3], T[df][:, :], T.ee[:, 1:96:3], ALU.subtract, ["e0", df], ["s1"])
         putc(4)
         if s == RO - 2: act(T.nth[:, :], T.ths[:, :], AF.Copy, ["ths"], ["nth"], scale=-1.0)
-        ts(T.sm[:, 64:128], T.pv[:, 0:64], 0.0, ALU.is_lt, ["pv"], ["s2"])
-        tt(T.sm[:, 128:192], T.sm[:, 64:128], T.ee[:, :], ALU.mult, ["s2", "e0", "e1"], ["s4"])
-        tt(sm[6], sm[5], sm[2], ALU.mult, ["s2", "s4"], ["s6"])
-        tt(sm[7], sm[4], sm[1], ALU.add, ["s1", "s4"], ["s7"])
-        nx = "%d" % (s + 1)
-        tt(T["df" + nx][:, :], sm[6], sm[7], ALU.add, ["s6", "s7"], ["df" + nx])
-        ts(T["dq" + nx][:, :], T["df" + nx][:, :], 1 / U, ALU.mult, ["df" + nx], ["dq" + nx])
+        ts(T.pick[:, 1:96:3], T.pv[:, 32:64], 0.0, ALU.is_lt, ["pv", "pick"], ["s2"])
+        ts(T.pick[:, 2:96:3], T.pv[:, 0:32], 0.0, ALU.is_lt, ["pv", "pick"], ["s3"])
+        op("v", lambda: V.tensor_tensor_scan(T.sm[:, 64:160], T.pick[:, :], T.ee[:, :], 0.0, ALU.mult, ALU.add), ["s2", "s3", "e0", "e1", "s1"], ["s4"])
+        cp(T["dq%d" % (s + 1)][:, :], T.sm[:, 66:160:3], ["s4"], ["dq%d" % (s + 1)])
     emit(g, T, ops)

@@ -2,43 +2,45 @@ from concourse.mybir import AluOpType as ALU, ActivationFunctionType as AF
 
 W, K, RO = 2048, 512, 3
 U = 2.0 ** -30
+TAG = 2.0 ** -80
+EPS = 2.0 ** -62
+SP = W + K
 F32, BF, F16, I32, U16 = "float32", "bfloat16", "float16", "int32", "uint16"
 SCRATCH = {
-    "b": ("sbuf", [128, 10 * W], F32), "c": ("sbuf", [128, W], F32), "m0": ("sbuf", [128, W], F32), "m1": ("sbuf", [128, W], F32),
+    "b": ("sbuf", [128, 9 * SP], F32), "c0": ("sbuf", [128, W], F32), "c1": ("sbuf", [128, W], F32),
     "tw": ("sbuf", [128, W], I32), "bh": ("sbuf", [128, W], BF), "wb": ("sbuf", [128, W], BF), "wu": ("sbuf", [128, W], BF),
-    "rb": ("sbuf", [128, W], BF), "nth": ("sbuf", [128, 2], F32), "ths": ("sbuf", [128, 2], F32), "wki": ("sbuf", [128, 32], I32),
-    "zero": ("sbuf", [128, K], F32), "jc": ("sbuf", [128, K], F32), "jlo": ("sbuf", [128, 32], F32),
-    "zi": ("sbuf", [128, 40], I32), "idn": ("sbuf", [128, 128], F32), "gu": ("sbuf", [128, K], F32),
-    "zt": ("sbuf", [128, 656], F16), "zz": ("sbuf", [128, 864], BF), "nine": ("sbuf", [128, 32], F32),
+    "rb": ("sbuf", [128, W], BF), "ths": ("sbuf", [128, 2], F32), "tq": ("sbuf", [128, 16], F32), "wki": ("sbuf", [128, 32], I32),
+    "zero": ("sbuf", [128, K], F32), "jc": ("sbuf", [128, K], F32), "jlo": ("sbuf", [128, 32], F32), "eps": ("sbuf", [128, K], F32),
+    "zi": ("sbuf", [128, 72], I32), "idn": ("sbuf", [128, 384], F32), "gu": ("sbuf", [128, K], F32),
+    "zt": ("sbuf", [128, 656], F16), "zz": ("sbuf", [128, 864], BF), "cst": ("sbuf", [128, 64], F32),
     "nb": ("sbuf", [128, K], F32), "cd": ("sbuf", [128, K], F32), "tg": ("sbuf", [128, K], F16),
     "ab0": ("sbuf", [128, K], F32), "ab1": ("sbuf", [128, K], F32), "big0": ("sbuf", [128, K], BF), "big1": ("sbuf", [128, K], BF),
     "ao": ("sbuf", [128, K], BF), "bo": ("sbuf", [128, K], F32), "aim": ("sbuf", [128, 32], F32), "to": ("sbuf", [128, 32], U16),
     "mg": ("sbuf", [128, 2 * K], BF), "dd": ("sbuf", [128, 560], BF), "sg": ("sbuf", [128, 2 * K], BF),
-    "ee": ("sbuf", [128, 96], F32), "pick": ("sbuf", [128, 96], F32), "sm": ("sbuf", [128, 256], F32), "lk": ("sbuf", [128, 32], U16),
+    "pick": ("sbuf", [128, 96], F32), "one": ("sbuf", [128, 16], F32), "df": ("sbuf", [128, 32], F32),
+    "free": ("sbuf", [128, 32], BF), "lk": ("sbuf", [128, 32], U16),
 }
 HALVED = ("g0", "ab0", "big0", "dd")
-PSUM = ("pc0", "pc1", "pd0", "pd1", "px", "pl", "pv")
+PSUM = ("pc0", "pc1", "pd0", "pd1", "px", "pl", "pv", "pe")
 for _n in PSUM:
     SCRATCH[_n] = ("psum", [128, K], F32)
 for _k in range(4):
     SCRATCH["g%d" % _k] = ("sbuf", [128, K], F32)
 for _s in range(RO):
-    SCRATCH["h%d" % _s] = ("sbuf", [128, K + 96], F32)
-    SCRATCH["hu%d" % _s] = ("sbuf", [128, K + 64], F32)
-    SCRATCH["hd%d" % _s] = ("sbuf", [128, K + 32], F32)
+    for _n in ("h", "hu", "hd", "dl"):
+        SCRATCH["%s%d" % (_n, _s)] = ("sbuf", [128, K], F32)
     SCRATCH["xl%d" % _s] = ("sbuf", [128, 160], U16)
-    SCRATCH["xs%d" % _s] = ("sbuf", [128, 64], F32)
-    SCRATCH["dl%d" % _s] = ("sbuf", [128, K], F32)
-    SCRATCH["df%d" % _s] = ("sbuf", [128, 32], F32)
+    SCRATCH["xu%d" % _s] = ("sbuf", [128, 64], U16)
+    SCRATCH["xd%d" % _s] = ("sbuf", [128, 32], U16)
+    SCRATCH["sm%d" % _s] = ("sbuf", [128, 96], F32)
     SCRATCH["dq%d" % _s] = ("sbuf", [128, 32], U16)
-LOADS = ["wki", "bh", "rb", "wb", "wu", "m0", "tw", "ths", "jc", "yb", "yc"]
+LOADS = ["wki", "bh", "rb", "wb", "wu", "c0", "c1", "tw", "ths", "jc", "yb", "yc", "add"]
 SEMAPHORES = (["qv", "qa", "qp", "qg", "sent"] + ["d_" + n for n in LOADS] + ["d_gu%d" % s for s in range(RO)]
-              + ["r_%s%d" % (n, s) for n in ("hu", "hd") for s in range(RO)])
-OPT = dict(cw=1280, cb=1152, kv=160, oc={(1, 2): 1, (2, 0): 2}, act=({}, {}, {2: 448, 3: K}),
-           bv=((0, 0, 32, 96), (0, 32, 64, 128), (0, 0, 0, 0)),
-           marks=((0, 22, 44, 64, 64), (0, 24, 48, 56, 64), None),
-           pc=({3: [(0, 0, 256)], 4: [(0, 256, 384)]}, {"p": [(0, 384, K)], 3: [(1, 0, 256)], 4: [(1, 256, 384)]},
-               {"p": [(1, 384, K)], 2: [(2, 0, 128)], 3: [(2, 128, K)]}))
+              + ["r_%s%d" % (n, s) for n in ("hu", "xu", "hd") for s in range(RO)])
+OPT = dict(cw=1728, cb=416, cg=576, cz=384, join=1152, kv=224, sv=256, nv=(0, 64, 64), late=(2, 1, 1),
+           act=((0, K, K, K), (256, K, K, K), (256, K, 448, K)),
+           av=((0, 256, 256, 64), (224, 256, 256, 96), (256, 224, 160, 0)),
+           marks=(18, 16), pc=((0, 288, 352, K), (0, 288, 352, K), (0, 64, K)))
 SHIFT = ((0, 112, 16), (112, 128, 0))
 
 
@@ -98,6 +100,7 @@ def rank_program(g, core, T, topo):
     V, A, P = g.vector, g.scalar, g.tensor
     ops = []
     H = K // 2
+    halves = ((0, H, "h0"), (H, K, "h1"))
 
     def op(q, f, r=(), w=(), sem=None, cnt=16, inc=True):
         r, w = ([y for x in z for y in ([x + "h0", x + "h1"] if x in HALVED else [x])] for z in (r, w))
@@ -109,18 +112,18 @@ def rank_program(g, core, T, topo):
         e = topo.engines(src, dst)
         return e if topo.chip(src) != topo.chip(dst) else [x for x in e if x not in far]
 
-    def send(dst, name, src, r, a=0, z=None):
+    def send(dst, out, src, r, sem):
         e = engines(core, dst); rid, pid = topo.addr(dst)[:2]; m = sum(1 << x for x in e)
-        op("g", lambda: g.remote_dma(T[name][:, a:z], src, T.sem["r_" + name], T.sem.sent, pid, rid, m), r=r, sem="sent", cnt=len(e), inc=False)
+        op("g", lambda: g.remote_dma(out, src, T.sem["r_" + sem], T.sem.sent, pid, rid, m), r=r, sem="sent", cnt=len(e), inc=False)
 
-    def arrives(src, name):
-        op("r", None, w=[name], sem="r_" + name, cnt=len(engines(src, core)))
+    def arrives(src, name, sem):
+        op("r", None, w=[name], sem="r_" + sem, cnt=len(engines(src, core)))
 
     def dma(q, out, in_, sem, r=(), w=()):
         op(q, lambda: (g.sync if q == "s" else g.scalar).dma_start(out, in_), r=r, w=w, sem="d_" + sem)
 
     def load(q, name, src): dma(q, T[name][:, :], src[:, :], name, w=[name])
-    def store(q, name, dst, a=0, e=W): dma(q, T[dst][:, a:e], T[name][:, a:e], dst, r=[name])
+    def store(name, dst): dma("s", T[dst][:, :], T[name][:, 0:W], dst, r=[name])
     def ind(win, lst, wide=W): return T[win][:, 0:wide].indirect(lst)
     def tt(out, a, b, o, r, w): op("v", lambda: V.tensor_tensor(out, a, b, o), r, w)
     def ts(out, a, s, o, r, w): op("v", lambda: V.tensor_scalar(out, a, s, None, o), r, w)
@@ -129,14 +132,15 @@ def rank_program(g, core, T, topo):
     def ms(out, v, w): op("v", lambda: V.memset(out, v), (), w)
     def act(out, a, f, r, w, **kw): op("a", lambda: A.activation(out, a, f, **kw), r, w)
     def iota(out, pat, base, cm, w, **kw): op("g", lambda: g.iota(out, pat, base, cm, **kw), (), w)
+    def choose(out, a, pat, o, fill, cm, r, w): op("g", lambda: g.affine_select(out, a, pat, o, fill, 0, cm), r, w)
     def keep(out, pat, o, fill, base, cm, w): op("g", lambda: g.affine_select(out, out, pat, o, fill, base, cm), w, w)
     def mm(out, l, x, st, sp, r, w): op("p", lambda: P.matmul(out, l, x, st, sp), r, w)
 
-    def tolist(bank, col, z, zoff, src, cols, st=True, sp=True, r=None):
+    def tolist(bank, col, z, zoff, src, cols, st=True, sp=True, r=None, step=1):
         def f():
             for i in range(16):
                 o = zoff + 15 - i
-                ins = P.matmul(T[bank][:, col:col + cols // 16], T[z][:, o:o + 128], T[src][:, i:cols:16], st and i == 0, sp and i == 15)
+                ins = P.matmul(T[bank][:, col:col + step * cols // 16:step], T[z][:, o:o + 128], T[src][:, i:cols:16], st and i == 0, sp and i == 15)
             return ins
         op("p", f, [z] + (r or [src]), [bank])
 
@@ -144,184 +148,219 @@ def rank_program(g, core, T, topo):
         o = T.zz[:, off + 15 + 16 * q0:off + 16 * q1:16]
         keep(o, [[16, q1 - q0]], ALU.is_gt, wt, 0, -1, w); keep(o, [[16, q1 - q0]], ALU.is_ge, 0.0, 15, -1, w)
 
+    def onward(off, wt):
+        band(off, 1, 8, wt, ["zu"]); keep(T.zz[:, off + 15:off + 16], [[1, 1]], ALU.is_gt, wt, 112, -1, ["zu"])
+
+    def diagonal(i, v):
+        choose(T.idn[:, 128 * i:128 * i + 128], T.zero[:, 0:128], [[-1, 128]], ALU.not_equal, v, 1, ["zero"], ["idn%d" % i])
+
     fl = {"allow_small_or_imprecise_dtypes": True}
     ZB, ZO, ZC, ZU = 0, 144, 288, 432
     FINE = 288
-    cw, cb = OPT["cw"], OPT["cb"]
-    ms(T.sm[:, 0:32], 1.0, ["s0"]); ms(T.zz[:, 0:656], 0.0, ["zz"]); ms(T.tw[:, 0:cw], 0, ["tw"])
-    iota(T.tw[:, cw:W], [[0, W - cw]], 0, 0, ["tw1"]); iota(T.zi[:, :], [[-4, 5], [-16, 8]], 132, 1, ["zi"])
-    load("a", "wki", T.wk); load("s", "bh", T.b0); load("s", "rb", T.rec)
-    act(T.dd[:, 528:560], T.sm[:, 0:32], AF.Silu, ["s0"], ["dd1"])
+    ZX = (256, 0, 384, 128, 512)
+    cw, cb, cg, cz = (OPT[x] for x in ("cw", "cb", "cg", "cz"))
+    ms(T.one[:, :], 1.0, ["one"]); ms(T.tw[:, 0:cw], 0, ["tw"]); ms(T.zz[:, 0:656], 0.0, ["zz"])
+    iota(T.jc[:, :], [[1, 32], [0, 16]], 32, 0, ["jc"], **fl); iota(T.jlo[:, :], [[0, 2], [1, 16]], 32, 0, ["jlo"], **fl)
+    iota(T.tw[:, cw:W], [[0, W - cw]], 0, 0, ["tw1"])
+    load("a", "wki", T.wk); load("s", "bh", T.b0)
+    act(T.dd[:, 0:16], T.one[:, :], AF.Silu, ["one"], ["dd1"])
+    load("s", "rb", T.rec)
     for rows, src in ((T.tw[0:128:8, :], T.hop), (T.tw[4:128:16, :], T.dn), (T.tw[12:128:16, :], T.up)):
         dma("s", rows, src[:, :], "tw", w=["tw", "tw1"])
     load("s", "wb", T.w)
     dma("s", T.ths[:, 0:1], T.th[:, :], "ths", w=["ths"])
     for lo, hi, a in SHIFT: dma("s", T.ths[lo:hi, 1:2], T.th[a:a + hi - lo, :], "ths", w=["ths"])
     for lo, hi, a in SHIFT: dma("s", T.wu[lo:hi, :], T.w[a:a + hi - lo, :], "wu", w=["wu"])
-    act(T.zero[:, :], T.zz[:, 0:K], AF.Copy, ["zz"], ["zero"])
-    cp(T.dq0[:, :], T.wki[:, :], ["wki"], ["dq0"]); cp(T.zt[:, :], T.zz[:, 0:656], ["zz"], ["zt"])
-    ts(T.zi[:, :], T.zi[:, :], 127, ALU.bitwise_and, ["zi"], ["zi"])
-    ts(T.zt[:, 15:640:16], T.zi[:, :], 0.0, ALU.is_equal, ["zi", "zt"], ["zt"])
-    iota(T.idn[:, :], [[0, 128]], 1, 0, ["idn"], **fl); keep(T.idn[:, :], [[-1, 128]], ALU.is_equal, 0.0, 0, 1, ["idn"])
-    iota(T.m0[:, 0:K], [[0, K]], 63, 0, ["m0"], **fl)
-    band(ZO, 0, 8, -2.0 ** 15, ["zz"]); band(ZC, 0, 8, -1.0 * W, ["zz"])
-    for a in range(K, W, K): dma("s", T.m0[:, a:a + K], T.m0[:, 0:K], "m0", r=["m0"], w=["m0w"])
-    iota(T.jlo[:, :], [[0, 2], [1, 16]], 32, 0, ["jlo"], **fl); iota(T.jc[:, :], [[1, 32], [0, 16]], 32, 0, ["jc"], **fl)
+    iota(T.zi[:, 0:40], [[-16, 5], [-64, 8]], 528, 4, ["zi"]); iota(T.zi[:, 40:72], [[1, 32]], 0, 32, ["zj"])
+    act(T.zero[:, :], T.jc[:, :], AF.Copy, ["jc"], ["zero"], scale=0.0)
+    for x in ("jlo", "jc"): act(T[x][:, :], T[x][:, :], AF.Copy, [x], [x], scale=2 * TAG)
     dma("s", T.jc[1:128:16, :], T.jlo[:, :], "jc", r=["jlo"], w=["jc"])
-    cp(T.b[:, cb:W], T.bh[:, cb:W], ["bh"], ["b1"])
+    cp(T.dq0[:, :], T.wki[:, :], ["wki"], ["dq0"]); cp(T.zt[:, :], T.zz[:, 0:656], ["zz"], ["zt"])
+    choose(T.b[:, W - cg:W], T.bh[:, W - cg:W], [[0, cg]], ALU.is_ge, 0.0, 0, ["bh"], ["b2"])
+    cp(T.b[:, cb:W - cg], T.bh[:, cb:W - cg], ["bh"], ["b1"])
+    ts(T.zi[:, :], T.zi[:, :], 511, ALU.bitwise_and, ["zi", "zj"], ["zi", "zj"])
+    ts(T.zt[:, 15:640:16], T.zi[:, 0:40], 0.0, ALU.is_equal, ["zi", "zt"], ["zt"])
+    band(ZO, 0, 8, -2.0 ** 15, ["zz"]); band(ZC, 0, 8, -SP / 2, ["zz"])
+    diagonal(0, 1.0); iota(T.cst[:, 32:64], [[0, 32]], 8 * SP, 0, ["cs8"], **fl)
+    for a in range(cz, W, K): dma("s", T.c0[:, a:min(a + K, W)], T.zero[:, 0:min(K, W - a)], "c0", r=["zero"], w=["c0"])
+    iota(T.c0[:, 0:cz], [[0, cz]], 0, 0, ["c0g"], **fl)
+
+    def bounds():
+        for j in range(2): act(T.tq[:, 8 + j:9 + j], T.ths[:, j:j + 1], AF.Square, ["ths", "scale"], ["bound%d" % j], scale=T.tq[:, 2 + j:3 + j])
+        act(T.tq[:, 10:12], T.tq[:, 8:10], AF.Identity, ["bound0", "bound1"], ["nbound"], scale=-1.0, bias=-2.0 ** -24)
+
+    def later():
+        onward(ZU, -SP / 2)
+        choose(T.eps[:, :], T.zero[:, :], [[0, K]], ALU.is_gt, 2 * EPS, 0, ["zero"], ["eps"])
+        diagonal(1, -1.0)
+        for row, wt in ((0, 16.0), (1, 1.0)): keep(T.zz[:, ZB + 15:ZB + 128:16], [[-16, 8]], ALU.not_equal, wt, -row, 1, ["zb"])
+        iota(T.dd[:, 528:560], [[0, 32]], -1, 0, ["dd2"], **fl)
+        iota(T.pick[:, :], [[0, 96]], 0, 0, ["pick"], **fl)
+        op("g", lambda: g.dma_start(T.c1[:, 0:K], T.zero[:, :]), ["zero"], ["c1z"], "d_c1")
+        iota(T.c1[:, K:W], [[0, W - K]], 0, 0, ["c1"], **fl)
+
+    def join(a, e): op("g", lambda: g.dma_start(T.c1[:, a:e], T.c0[:, a:e], accum_op=ALU.add), ["c0", "c1"], ["c1"], "d_add")
 
     for s in range(RO):
         last = s == RO - 1
-        dq, xl, xs, h, hu, hd, df, m, dl = ("%s%d" % (x, s) for x in ("dq", "xl", "xs", "h", "hu", "hd", "df", "m", "dl"))
+        dq, xl, xu, xd, h, hu, hd, dl, sm = ("%s%d" % (x, s) for x in ("dq", "xl", "xu", "xd", "h", "hu", "hd", "dl", "sm"))
+        c = "c%d" % min(s, 1)
         D = T[dq][:, :]
-        X = [(xl + "a", T[xs][:, 0:32], xs, h, 32), (xl + "b", T[xs][:, 32:64], xs + "b" * last, h, 32),
-             (xl + "c", T[hu][:, K:K + 32], hu, hu, 0), (xl + "d", T[hd][:, 0:32], hd, hd, 32)]
-        u = U if last else 1.0; zf = FINE if last else 0
-        if not s: df = "wki"
-        acts, mk, pcs = (OPT[x][s] for x in ("act", "marks", "pc"))
+        DF, df = (T["sm%d" % (s - 1)][:, 2:96:3], "sm%d" % (s - 1)) if s else (T.df[:, :], "df")
+        X = [(xl + "a", h), (xl + "b", h), (xu, hu), (xd, hd)]
+        acts, pcs, late = (OPT[x][s] for x in ("act", "pc", "late"))
 
-        def lst(k, a=0, e=K): o = (0, 32, 64, 128, 96)[k]; return T[xl][:, o + a // 16:o + e // 16]
+        def lst(k, a=0, e=K):
+            t, o = ((xl, 96), (xl, 64), (xu, 0), (xd, 0), (xu, 32))[k]
+            return T[t][:, o + a // 16:o + e // 16]
+        def lists(bank, which):
+            for i in which: tolist(bank, 32 * i, "zt", ZX[i], "tg", K)
+        def cast(bank, a, e, w): cp(T[xl][:, 32 * a:32 * e], T[bank][:, 32 * a:32 * e], [bank], [xl + w])
+        def hand(a, e, w):
+            if a <= 1 < e: send(up, T[xu][:, 0:32], T[xl][:, 32:64], [xl + w], xu)
+            if a == 0: send(dn, T[xd][:, :], T[xl][:, 0:32], [xl + w], hd)
+        def uplist(): cast("pv", 4, 5, "u"); send(up, T[xu][:, 32:64], T[xl][:, 128:160], [xl + "u"], hu)
         def grad(k, a=0, e=K, p=""):
-            wt, l = ("wu", lst(4)) if k == 2 else ("wb", lst(k, a, e))
-            tt(T["g%d" % k][:, a:e], ind(wt, l), T[X[k][3]][:, X[k][4] + a:X[k][4] + e], ALU.mult, [wt, X[k][0], X[k][3]], ["g%d" % k + p])
+            wt, l = ("wu", 4) if k == 2 else ("wb", k)
+            tt(T["g%d" % k][:, a:e], ind(wt, lst(l, a, e)), T[X[k][1]][:, a:e], ALU.mult, [wt, X[k][0] + "w" * (k == 2), X[k][1]], ["g%d" % k + p])
             if k == 2:
                 for lo, hi, a in SHIFT: dma("s", T.gu[a:a + hi - lo, :], T.g2[lo:hi, :], "gu%d" % s, r=["g2"], w=["gu"])
         def size(k, a=0, e=K, p=""):
-            ab = "ab%d" % (k % 2)
-            act(T[ab][:, a:e], T["g%d" % k][:, a:e], AF.Abs, ["g%d" % k + p], [ab + p])
-        def over(k, a=0, e=K, p=""):
+            ab = "ab%d" % (k % 2); j = 2 + int(k == 2)
+            if s or k: act(T[ab][:, a:e], T["g%d" % k][:, a:e], AF.Square, ["g%d" % k + p, "scale"], [ab + p], scale=T.tq[:, j:j + 1])
+            else: act(T[ab][:, a:e], T.g0[:, a:e], AF.Abs, ["g0" + p], [ab + p])
+        def over(k, q, a=0, e=K, p=""):
             ab = "ab%d" % (k % 2); big = "big%d" % (k % 2); j = int(k == 2)
-            z = acts.get(k, a)
-            if z > a:
-                act(T[ab][:, a:z], T[ab][:, a:z], AF.Relu, [ab + p, "nth"], [ab + p], bias=T.nth[:, j:j + 1])
-                act(T[big][:, a:z], T[ab][:, a:z], AF.Sign, [ab + p], [big + "a"])
-            if z < e: ts2(T[big][:, z:e], T[ab][:, z:e], T.ths[:, j:j + 1], ALU.is_gt, -9.0 / 16, ALU.add, [ab + p, "ths"], [big + p])
-        def place(k, st=True):
-            bank = "pd%d" % (k % 2)
-            mm(T[bank][:, 0:32], T.idn[:, :], X[k][1], st, False, ["idn", X[k][2]], [bank])
-            if k in acts: mm(T[bank][:, 0:acts[k] // 16], T.idn[:, :], T.nine[:, 0:acts[k] // 16], False, False, ["idn", "nine"], [bank])
+            z = min(max(acts[k], a), e)
+            if z > a and q == "a": act(T[big][:, a:z], T[ab][:, a:z], AF.Sign, [ab + p, "nbound"], [big + "a"], bias=T.tq[:, 10 + j:11 + j])
+            bound, r = (T.tq[:, 8 + j:9 + j], "bound%d" % j) if s or k else (T.ths[:, 0:1], "ths")
+            if z < e and q == "v": ts2(T[big][:, z:e], T[ab][:, z:e], bound, ALU.is_gt, 2.0, ALU.mult, [ab + p, r], [big + p])
+        def place(k):
+            bank = "pd%d" % (k % 2); i = 2 * int(last and k > 0); z = acts[k] // 16
+            mm(T[bank][:, 0:32], T.idn[:, 128 * i:128 * i + 128], T.cst[:, 0:32], True, False, ["idn%d" % i, "cst"], [bank])
+            if z < 32: mm(T[bank][:, z:32], T.idn[:, 128 * i:128 * i + 128], T.cst[:, 32 + z:64], False, False, ["idn%d" % i, "cs8"], [bank])
         def count(k, sp=False):
             big = "big%d" % (k % 2)
-            tolist("pd%d" % (k % 2), 0, "zz", (zf if k else 0) + (ZU if k == 2 else ZC), big, K, False, sp, [big, big + "a"] + ["zu"] * (k == 2 or last))
-        def old(k, sp=True, st=False):
-            act(T.ao[:, :], ind("b", lst(k)), AF.Abs, ["b", X[k][0]], ["ao"], scale=2.0 ** (95 if last and k else 90))
-            tolist("pd%d" % (k % 2), 0, "zz", ZO, "ao", K, st, sp)
-        def base(k): e = K - OPT["bv"][s][k]; act(T.bo[:, 0:e], ind("b", lst(k, 0, e)), AF.Copy, ["b", X[k][0]], ["bo"])
-        def rest(k):
-            e = K - OPT["bv"][s][k]
-            if e < K: cp(T.bo[:, e:K], ind("b", lst(k, e, K)), ["b", X[k][0]], ["bov"])
+            tolist("pd%d" % (k % 2), 0, "zz", (FINE if last and k else 0) + (ZU if k == 2 else ZC), big, K, False, sp, [big, big + "a"] + ["zu"] * (k == 2 or last))
+        def old(k, q):
+            e = K - OPT["av"][s][k]
+            if q == "a": act(T.ao[:, 0:e], ind("b", lst(k, 0, e)), AF.Abs, ["b", X[k][0]], ["ao"], scale=2.0 ** (95 if last and k else 90))
+            elif e < K: ts(T.ao[:, e:K], ind("b", lst(k, e, K)), 0.0, ALU.not_equal, ["b", X[k][0]], ["aov"])
+        def empty(k, sp=True): tolist("pd%d" % (k % 2), 0, "zz", ZO, "ao", K, False, sp, ["ao", "aov"])
+        def base(k): act(T.bo[:, :], ind("b", lst(k)), AF.Copy, ["b", X[k][0]], ["bo"])
         def aim(k):
-            o = "aim" if last and k else "to"
-            tt(T[o][:, :], T["pd%d" % (k % 2)][:, 0:32], X[k][1], ALU.max, ["pd%d" % (k % 2), X[k][2]], [o])
-            if last and k: ts(T.to[:, :], T.aim[:, :], 1 / U, ALU.mult, ["aim"], ["to"])
+            bank = "pd%d" % (k % 2)
+            if last and k:
+                ts2(T.aim[:, :], T[bank][:, 0:32], 0.0, ALU.max, 1 / U, ALU.mult, [bank], ["aim"])
+                tt(T.to[:, :], T.aim[:, :], lst(k), ALU.max, ["aim", X[k][0]], ["to"])
+            else: tt(T.to[:, :], T[bank][:, 0:32], lst(k), ALU.max, [bank, X[k][0]], ["to"])
         def put(k):
             gk = "gu" if k == 2 else "g%d" % k
-            tt(ind("b", T.to[:, :], 10 * W), T.bo[:, :], T[gk][:, :], ALU.add, ["bo", "bov", gk, "to"], ["b"])
-        def mark(i):
-            if last or mk[i] == mk[i + 1]: return
-            a, e = mk[i], mk[i + 1]
-            if a < 32: z = min(e, 32); act(ind(m, T[xl][:, a:z]), T.jc[:, 16 * a:16 * z], AF.Silu, [xl + "a", "jc", m, "m0w"], [m])
-            if e > 32: z = max(a, 32) - 32; act(ind(m, T[dq][:, z:e - 32]), T.zero[:, 16 * z:16 * (e - 32)], AF.Silu, [dq, "zero", m], [m])
-        def marked():
-            act(T.mg[:, :], ind(m, T[xl][:, 0:64]), AF.Copy, [m, xl + "a", xl + "b"], ["mg"])
-            tolist("pl", 0, "zz", ZB, "mg", 2 * K, r=["mg", "zb"])
-        def oldc(t): act(T.cd[:, :], ind("c", T["dq%d" % t][:, :]), AF.Copy, ["c", "dq%d" % t], ["cd"])
+            tt(ind("b", T.to[:, :], 9 * SP), T.bo[:, :], T[gk][:, :], ALU.add, ["bo", gk, "to"], ["b"])
+        def beside(k):
+            if last:
+                if k == 1: act(T.cd[:, :], ind(c, D), AF.Copy, [c, dq], ["cd"])
+            elif k < 2:
+                a, e = (0, OPT["marks"][s], 32)[k:k + 2]
+                act(ind(c, T[xl][:, 96 + a:96 + e]), T.jc[:, 16 * a:16 * e], AF.Silu, [xl + "a", "jc", c, "c0g"] + ["c1z"] * s, [c])
+            else:
+                act(ind(c, T[dq][:, pcs[1] // 16:32]), T.eps[:, pcs[1]:K], AF.Silu, ["eps", dq, c], [c])
         def putc(i):
-            for t, a, e in pcs.get(i, ()):
-                d = "dl%d" % t; o = ind("c", T["dq%d" % t][:, a // 16:e // 16])
-                if t: tt(o, T.cd[:, a:e], T[d][:, a:e], ALU.add, ["cd", d, "dq%d" % t], ["c"])
-                else: cp(o, T[d][:, a:e], [d, "dq%d" % t, "c"], ["c"])
-                if t == RO - 1 and e == K: store("s", "c", "yc")
+            a, e = pcs[i:i + 2]; o = ind(c, T[dq][:, a // 16:e // 16])
+            if last: tt(o, T.cd[:, a:e], T[dl][:, a:e], ALU.add, ["cd", dl, dq], [c])
+            else: ts2(o, T[dl][:, a:e], 1.0, ALU.mult, EPS, ALU.add, [dl, dq, c], [c])
+            if e == K and s == 1: join(0, OPT["join"])
+            if e == K and last: store(c, "yc")
         def tables():
             cp(T.tg[:, :], ind("tw", D), ["tw", dq], ["tg"])
-            tolist("px", 0, "zt", 128, "tg", K); tolist("pl", 0, "zt", 0, "tg", K)
-            if s: tolist("pl", 32, "zt", 512, "tg", K)
-        def first():
-            cp(T[xl][:, 0:32], T.px[:, 0:32], ["px"], [xl + "a"])
-            tolist("px", 32, "zt", 384, "tg", K)
-            if not s: tolist("pl", 32, "zt", 512, "tg", K)
-            tolist("pv", 0, "zt", 256, "tg", K)
-        def uplists(): act(T[h][:, 32 + K:96 + K], T.pl[:, 0:64], AF.Copy, ["pl"], [h + "u"], scale=u)
-        def far(k):
-            if k == 2: ts(T[xl][:, 64:128], T[hu][:, K:K + 64], 1 / u, ALU.mult, [hu], [X[k][0]])
-            else: ts(lst(k), X[k][1], 1 / u, ALU.mult, [X[k][2]], [X[k][0]])
-            if k == 2 and not last: tt(T.ee[:, 1:96:3], T[df][:, :], T[xs][:, 0:32], ALU.subtract, [xs, df], ["e0"])
-            if k == 3 and not last: tt(T.ee[:, 0:96:3], T[xs][:, 32:64], T[df][:, :], ALU.subtract, [xs, df], ["e1"])
-            grad(k)
+            for bank, i in (("pv", 4), ("px", 3)) if last else (("px", 3), ("pv", 4)): lists(bank, [i])
+            lists("pl", range(2, late - 1, -1))
+        def moves():
+            for i, col, step in ((2, 0, 3), (3, 96, 1)):
+                tolist("pe", col, "zt", ZX[i], "tg", K, True, False, step=step)
+                mm(T.pe[:, col:col + 32 * step:step], T.idn[:, 128:256], DF, False, True, ["idn1", df], ["pe"])
 
         src = "b" if s else "bh"
-        act(T.nb[:, :], ind(src, D), AF.Copy, [src, dq], ["nb"], scale=-1.0)
+        e = K - OPT["nv"][s]
+        act(T.nb[:, 0:e], ind(src, T[dq][:, 0:e // 16]), AF.Copy, [src, dq], ["nb"], scale=-1.0)
+        if e < K: ts(T.nb[:, e:K], ind(src, T[dq][:, e // 16:32]), -1.0, ALU.mult, [src, dq], ["nbv"])
         if s: tables()
         else: act(T.b[:, 0:cb], T.bh[:, 0:cb], AF.Copy, ["bh"], ["b"])
-        act(ind("b", D), T.zero[:, :], AF.Silu, ["zero", dq, "b", "b1"], ["b"])
-        tt(T[dl][:, :], ind("rb", D), T.nb[:, :], ALU.mult, ["rb", dq, "nb"], [dl])
-        if s: first()
-        else: tables()
-        tt(T[h][:, 32:32 + K], ind("wb", D), T[dl][:, :], ALU.mult, ["wb", dq, dl], [h])
-        if s: uplists(); send(up, hu, T[h][:, 32:96 + K], [h, h + "u"])
-        else: send(up, hu, T[h][:, 32:32 + K], [h], 0, K); first()
-        grad(0)
-        old(0, False, True)
-        cp(T[xl][:, 32:64], T.px[:, 32:64], ["px"], [xl + "b"])
-        putc("p")
-        size(0, 0, H, "h0"); size(0, H, K, "h1")
-        e = 32 if last else 64
-        act(T[xs][:, 0:e], T.px[:, 0:e], AF.Copy, ["px"], [xs])
-        if not s: uplists(); send(up, hu, T[h][:, 32 + K:96 + K], [h + "u"], K, K + 64)
-        act(T[h][:, 0:32], T.pv[:, 0:32], AF.Copy, ["pv"], [h + "d"], scale=u)
-        send(dn, hd, T[h][:, 0:32 + K], [h, h + "d"])
-        over(0, 0, H, "h0"); over(0, H, K, "h1"); place(0, False); count(0, True)
-        base(0)
-        if last: act(T[xs][:, 32:64], T.px[:, 32:64], AF.Copy, ["px"], [xs + "b"], scale=u)
+        act(ind("b", D), T.zero[:, :], AF.Silu, ["zero", dq, "b", "b1", "b2"], ["b"])
+        tt(T[dl][:, :], ind("rb", D), T.nb[:, :], ALU.mult, ["rb", dq, "nb", "nbv"], [dl])
+        if not s: tables()
+        if s == 1: cast("px", 3, 4, "a")
+        if last: uplist()
+        tt(T[h][:, :], ind("wb", D), T[dl][:, :], ALU.mult, ["wb", dq, dl], [h])
+        if s != 1: cast("px", 3, 4, "a")
+        send(up, T[hu][:, :], T[h][:, :], [h], hu)
+        if s == 1: uplist()
+        if s: send(dn, T[hd][:, :], T[h][:, :], [h], hd)
+        old(0, "a")
+        grad(0, *halves[0])
+        if not s: uplist(); send(dn, T[hd][:, :], T[h][:, :], [h], hd)
+        grad(0, *halves[1])
         if not s:
-            band(ZU, 1, 8, -1.0 * W, ["zu"]); keep(T.zz[:, ZU + 15:ZU + 16], [[1, 1]], ALU.is_gt, -1.0 * W, 112, -1, ["zu"])
-            iota(T.c[:, :], [[0, W]], 0, 0, ["c"], **fl)
-            for row, wt in ((0, 16.0), (1, 1.0)): keep(T.zz[:, ZB + 15:ZB + 128:16], [[-16, 8]], ALU.not_equal, wt, -row, 1, ["zb"])
-            iota(T.dd[:, 0:16], [[0, 16]], -1, 0, ["dd2"], **fl)
-            iota(T.nine[:, :], [[0, 32]], 0, 0, ["nine"], **fl); keep(T.nine[:, :], [[0, 32]], ALU.is_gt, 9 * W * U, 0, 0, ["nine"])
-            iota(T.pick[:, :], [[0, 96]], 0, 0, ["pick"], **fl)
-            iota(T.m1[:, :], [[0, W]], 63, 0, ["m1"], **fl)
+            op("v", lambda: V.reciprocal(T.tq[:, 0:2], T.ths[:, :]), ["ths"], ["tq"])
+            ts(T.cst[:, 0:32], T.zi[:, 40:72], float(W), ALU.add, ["zj"], ["cst"])
+            ts(T.tq[:, 2:4], T.tq[:, 0:2], 1 - 2.0 ** -20, ALU.mult, ["tq"], ["scale"])
+        place(0)
+        cast("pl", late, 3, "b"); hand(late, 3, "b")
+        if last: join(OPT["join"], W)
+        old(0, "v"); empty(0, False)
+        for x in halves: size(0, *x)
+        over(0, "a", *halves[0])
+        if not s: bounds()
+        for x in halves: over(0, "v", *x)
+        count(0, True)
+        lists("pe", range(late - 1, -1, -1))
+        grad(1); base(0)
         if s == 1:
             iota(T.zz[:, 656:864], [[0, 208]], 0, 0, ["zu"], **fl)
-            band(FINE + ZC, 0, 8, -W * U, ["zu"]); band(FINE + ZU, 1, 8, -W * U, ["zu"])
-            keep(T.zz[:, FINE + ZU + 15:FINE + ZU + 16], [[1, 1]], ALU.is_gt, -W * U, 112, -1, ["zu"])
-        if not s: arrives(dn, hu)
-        arrives(dn, hu); arrives(up, hd)
-        sm = [T.sm[:, 32 * i:32 * i + 32] for i in range(8)]
-        grad(1)
+            band(FINE + ZC, 0, 8, -SP / 2 * U, ["zu"]); onward(FINE + ZU, -SP / 2 * U)
+            diagonal(2, U)
+        arrives(dn, hu, hu); arrives(dn, xu + "w", hu); arrives(dn, xu, xu); arrives(up, hd, hd); arrives(up, xd, hd)
+        aim(0)
         for k in range(3):
-            aim(k); size(k + 1); put(k); over(k + 1); place(k + 1); count(k + 1)
-            if (s, k) in OPT["oc"]: oldc(OPT["oc"][s, k])
-            mark(k); old(k + 1); base(k + 1)
-            if k == 0:
-                rest(1)
-                if s and not last: cp(T[df][:, :], D, [dq], [df])
-            if k < 2: far(k + 2)
-            if k: putc(k + 1); rest(k + 1)
-        aim(3); put(3)
+            size(k + 1); put(k)
+            if not k: cast("pe", 0, late, "c"); hand(0, late, "c")
+            if not k and not s: later()
+            place(k + 1); beside(k); over(k + 1, "a")
+            old(k + 1, "a")
+            over(k + 1, "v"); count(k + 1)
+            old(k + 1, "v"); empty(k + 1); base(k + 1)
+            if k < 2: grad(k + 2)
+            if last and k: putc(k - 1)
+            if not last and k == 2: putc(0)
+            aim(k + 1)
+        if not s: cp(T.df[:, :], T.wki[:, :], ["wki"], ["df"])
+        if not last: moves()
+        put(3)
         if last:
-            store("s", "b", "yb", 0, W // 2); store("a", "b", "yb", W // 2, W)
+            store("b", "yb")
             break
-        mark(3); marked()
+        act(T.mg[:, :], ind(c, T[xl][:, 64:128]), AF.Abs, [c, xl + "a", xl + "b"], ["mg"], scale=1 / TAG)
+        tolist("pl", 0, "zz", ZB, "mg", 2 * K, r=["mg", "zb"])
         act(T.ab0[:, :], ind("b", lst(0)), AF.Abs, ["b", X[0][0]], ["ab0"])
         cp(T.ab1[:, :], ind("b", lst(1)), ["b", X[1][0]], ["ab1"])
-        pp = ((0, H, "pc0", "h0"), (H, K, "pc1", "h1"))
-        for a, e, u, p in pp: act(T[u][:, a:e], T.ab1[:, a:e], AF.Abs, ["ab1"], [u])
-        ts(T.lk[:, :], T.pl[:, 32:64], -528.0, ALU.add, ["pl"], ["lk"])
-        ts(sm[0], T.pl[:, 0:32], 64.0, ALU.is_gt, ["pl"], ["s0"])
-        tt(T.ee[:, 1:96:3], T.ee[:, 1:96:3], sm[0], ALU.mult, ["s0", "e0"], ["e0"])
-        for a, e, u, p in pp: tt(T.dd[:, 16 + a:16 + e], T[u][:, a:e], T.ab0[:, a:e], ALU.subtract, [u, "ab0"], ["dd" + p])
-        act(T.sg[:, 0:H], T.dd[:, 16:16 + H], AF.Sign, ["ddh0"], ["sgh"])
-        kv = OPT["kv"]; eps = 2.0 ** -116
+        putc(1)
+        ts(T.free[:, :], T.pl[:, 32:64], 2.0 * W, ALU.is_lt, ["pl"], ["free"])
+        ts2(T.lk[:, :], T.pl[:, 0:32], -528.0, ALU.add, 559.0, ALU.min, ["pl"], ["lk"])
+        for (a, e, p), u in zip(halves, ("pc0", "pc1")): act(T[u][:, a:e], T.ab1[:, a:e], AF.Abs, ["ab1"], [u])
+        tt(T.pe[:, 1:96:3], T.free[:, :], T.pe[:, 96:128], ALU.mult, ["free", "pe"], ["pe"])
+        for (a, e, p), u in zip(halves, ("pc0", "pc1")):
+            tt(T.dd[:, 16 + a:16 + e], T[u][:, a:e], T.ab0[:, a:e], ALU.subtract, [u, "ab0" + p], ["dd" + p])
+        kv, sv = OPT["kv"], K - OPT["sv"]; eps = 2.0 ** -116
+        act(T.sg[:, 0:sv], T.dd[:, 16:16 + sv], AF.Sign, ["ddh0"], ["sgh"])
         act(T.sg[:, K + kv:2 * K], ind("dd", T.lk[:, kv // 16:32], 560), AF.Sign, ["dd", "dd1", "dd2", "lk"], ["sga"])
-        ts2(T.sg[:, H:K], T.dd[:, 16 + H:16 + K], eps, ALU.min, -eps, ALU.max, ["dd"], ["sgo"])
-        if kv: ts2(T.sg[:, K:K + kv], ind("dd", T.lk[:, 0:kv // 16], 560), eps, ALU.min, -eps, ALU.max, ["dd", "dd1", "dd2", "lk"], ["sgv"])
+        tt(T.pe[:, 2:96:3], DF, T.pe[:, 1:96:3], ALU.add, [df, "pe"], ["pe"])
+        ts2(T.sg[:, sv:K], T.dd[:, 16 + sv:16 + K], eps, ALU.min, -eps, ALU.max, ["dd"], ["sgo"])
+        ts2(T.sg[:, K:K + kv], ind("dd", T.lk[:, 0:kv // 16], 560), eps, ALU.min, -eps, ALU.max, ["dd", "dd1", "dd2", "lk"], ["sgv"])
         tolist("pv", 0, "zz", ZO, "sg", 2 * K, r=["sga", "sgo", "sgv", "sgh"])
-        tt(T.ee[:, 2:96:3], T[df][:, :], T.ee[:, 1:96:3], ALU.subtract, ["e0", df], ["s1"])
-        putc(4)
-        if s == RO - 2: act(T.nth[:, :], T.ths[:, :], AF.Copy, ["ths"], ["nth"], scale=-1.0)
-        ts(T.pick[:, 1:96:3], T.pv[:, 32:64], 0.0, ALU.is_lt, ["pv", "pick"], ["s2"])
-        ts(T.pick[:, 2:96:3], T.pv[:, 0:32], 0.0, ALU.is_lt, ["pv", "pick"], ["s3"])
-        op("v", lambda: V.tensor_tensor_scan(T.sm[:, 64:160], T.pick[:, :], T.ee[:, :], 0.0, ALU.mult, ALU.add), ["s2", "s3", "e0", "e1", "s1"], ["s4"])
-        cp(T["dq%d" % (s + 1)][:, :], T.sm[:, 66:160:3], ["s4"], ["dq%d" % (s + 1)])
+        putc(2)
+        ts2(T.pick[:, 1:96:3], T.pv[:, 32:64], 0.0, ALU.is_lt, -1.0, ALU.mult, ["pv", "pick"], ["s2"])
+        ts2(T.pick[:, 2:96:3], T.pv[:, 0:32], 0.0, ALU.is_lt, -1.0, ALU.mult, ["pv", "pick"], ["s3"])
+        def scan(o=T[sm][:, :]): op("v", lambda: V.tensor_tensor_scan(o, T.pick[:, :], T.pe[:, 0:96], 0.0, ALU.mult, ALU.add), ["s2", "s3", "pe"], [sm])
+        scan()
+        cp(T["dq%d" % (s + 1)][:, :], T[sm][:, 2:96:3], [sm], ["dq%d" % (s + 1)])
     emit(g, T, ops)

from concourse.mybir import AluOpType as ALU, ActivationFunctionType as AF

W, K, RO = 2048, 512, 3
U = 2.0 ** -30
TAG = 2.0 ** -80
EPS = 2.0 ** -62
SP = W + K
F32, BF, F16, I32, U16 = "float32", "bfloat16", "float16", "int32", "uint16"
SCRATCH = {
    "b": ("sbuf", [128, 9 * SP], F32), "c0": ("sbuf", [128, W], F32), "c1": ("sbuf", [128, W], F32),
    "tw": ("sbuf", [128, W], I32), "bh": ("sbuf", [128, W], BF), "wb": ("sbuf", [128, W], BF), "wu": ("sbuf", [128, W], BF),
    "rb": ("sbuf", [128, W], BF), "ths": ("sbuf", [128, 2], F32), "tq": ("sbuf", [128, 16], F32), "wki": ("sbuf", [128, 32], I32),
    "zero": ("sbuf", [128, K], F32), "jc": ("sbuf", [128, K], F32), "jlo": ("sbuf", [128, 32], F32), "eps": ("sbuf", [128, K], F32),
    "zi": ("sbuf", [128, 72], I32), "idn": ("sbuf", [128, 384], F32), "gu": ("sbuf", [128, K], F32),
    "zt": ("sbuf", [128, 656], F16), "zz": ("sbuf", [128, 864], BF), "cst": ("sbuf", [128, 64], F32),
    "nb": ("sbuf", [128, K], F32), "cd": ("sbuf", [128, K], F32), "tg": ("sbuf", [128, K], F16),
    "ab0": ("sbuf", [128, K], F32), "ab1": ("sbuf", [128, K], F32), "big0": ("sbuf", [128, K], BF), "big1": ("sbuf", [128, K], BF),
    "ao": ("sbuf", [128, K], BF), "bo": ("sbuf", [128, K], F32), "aim": ("sbuf", [128, 32], F32), "to": ("sbuf", [128, 32], U16),
    "mg": ("sbuf", [128, 2 * K], BF), "dd": ("sbuf", [128, 560], BF), "sg": ("sbuf", [128, 2 * K], BF),
    "pick": ("sbuf", [128, 96], F32), "one": ("sbuf", [128, 16], F32), "df": ("sbuf", [128, 32], F32),
    "free": ("sbuf", [128, 32], BF), "lk": ("sbuf", [128, 32], U16),
}
HALVED = ("g0", "ab0", "big0", "dd")
PSUM = ("pc0", "pc1", "pd0", "pd1", "px", "pl", "pv", "pe")
for _n in PSUM:
    SCRATCH[_n] = ("psum", [128, K], F32)
for _k in range(4):
    SCRATCH["g%d" % _k] = ("sbuf", [128, K], F32)
for _s in range(RO):
    for _n in ("h", "hu", "hd", "dl"):
        SCRATCH["%s%d" % (_n, _s)] = ("sbuf", [128, K], F32)
    SCRATCH["xl%d" % _s] = ("sbuf", [128, 160], U16)
    SCRATCH["xu%d" % _s] = ("sbuf", [128, 64], U16)
    SCRATCH["xd%d" % _s] = ("sbuf", [128, 32], U16)
    SCRATCH["sm%d" % _s] = ("sbuf", [128, 96], F32)
    SCRATCH["dq%d" % _s] = ("sbuf", [128, 32], U16)
LOADS = ["wki", "bh", "rb", "wb", "wu", "c0", "c1", "tw", "ths", "jc", "yb", "yc", "add"]
SEMAPHORES = (["qv", "qa", "qp", "qg", "sent"] + ["d_" + n for n in LOADS] + ["d_gu%d" % s for s in range(RO)]
              + ["r_%s%d" % (n, s) for n in ("hu", "xu", "hd") for s in range(RO)])
OPT = dict(cw=1728, cb=416, cg=576, cz=384, join=1152, kv=224, sv=256, nv=(0, 64, 64), late=(2, 1, 1),
           act=((0, K, K, K), (256, K, K, K), (256, K, 448, K)),
           av=((0, 256, 256, 64), (224, 256, 256, 96), (256, 224, 160, 0)),
           marks=(18, 16), pc=((0, 288, 352, K), (0, 288, 352, K), (0, 64, K)))
SHIFT = ((0, 112, 16), (112, 128, 0))


def emit(g, T, ops):
    Q = {"v": g.vector, "a": g.scalar, "p": g.tensor, "g": g, "s": g.sync}
    lastw = {}; readers = {}
    for i, o in enumerate(ops):
        dep = set()
        for r in o["r"]:
            if r in lastw: dep.add(lastw[r])
            if r in PSUM: dep.update(j for j in readers.get(r, ()) if ops[j]["q"] != o["q"])
        for r in o["w"]:
            for j in ([lastw[r]] if r in lastw else []) + list(readers.get(r, ())):
                if ops[j]["q"] != o["q"] or ops[j]["sem"] or o["q"] != "p": dep.add(j)
        twins = [j for j in dep if ops[j]["sem"] and ops[j]["sem"] == o["sem"]]
        o["dep"] = [j for j in dep if j not in twins] + [x for j in twins for x in ops[j]["dep"]]
        for r in o["r"]: readers.setdefault(r, []).append(i)
        for r in o["w"]:
            same = r in lastw and o["sem"] and ops[lastw[r]]["sem"] == o["sem"]
            lastw[r] = i
            if not same: readers[r] = []
    known = {}; need = set(); final = {}
    for i, o in enumerate(ops):
        if o["sem"]: final[o["sem"]] = i
    for i, o in enumerate(ops):
        kn = known.setdefault(o["q"], {}); o["wait"] = []
        for j in sorted(o["dep"], reverse=True):
            key = ops[j]["sem"] or "q" + ops[j]["q"]
            if kn.get(key, -1) >= j: continue
            o["wait"].append(j); need.add(j)
            for x, v in ops[j]["kn"].items(): kn[x] = max(kn.get(x, -1), v)
            kn[key] = max(kn.get(key, -1), final[key] if ops[j]["sem"] else j)
        o["kn"] = dict(kn)
    total = {}; count = {}
    for i, o in enumerate(ops):
        if o["sem"]: total[o["sem"]] = total.get(o["sem"], 0) + o["n"]
        elif i in need:
            count[o["q"]] = count.get(o["q"], 0) + 1; o["at"] = count[o["q"]]
    waited = {}
    for i, o in enumerate(ops):
        for j in o["wait"]:
            p = ops[j]; s, v = (p["sem"], total[p["sem"]]) if p["sem"] else ("q" + p["q"], p["at"])
            Q[o["q"]].wait_ge(T.sem[s], v); waited[s] = max(waited.get(s, 0), v)
        if not o["f"]: continue
        ins = o["f"]()
        if o["sem"] and o["inc"]: ins.then_inc(T.sem[o["sem"]], o["n"])
        elif "at" in o: ins.then_inc(T.sem["q" + o["q"]], 1)
    for s, v in sorted(total.items()):
        if waited.get(s, 0) < v: (g if s == "sent" else g.sync).wait_ge(T.sem[s], v)


def rank_program(g, core, T, topo):
    rank = T.rank_of(core)
    if rank is None:
        return
    n = len(T.cores); up = T.cores[(rank + 1) % n]; dn = T.cores[(rank - 1) % n]
    V, A, P = g.vector, g.scalar, g.tensor
    ops = []
    H = K // 2
    halves = ((0, H, "h0"), (H, K, "h1"))

    def op(q, f, r=(), w=(), sem=None, cnt=16, inc=True):
        r, w = ([y for x in z for y in ([x + "h0", x + "h1"] if x in HALVED else [x])] for z in (r, w))
        ops.append({"q": q, "f": f, "r": r, "w": w, "sem": sem, "n": cnt, "inc": inc})

    def engines(src, dst):
        rk = T.rank_of(src); both = [T.cores[(rk + 1) % n], T.cores[(rk - 1) % n]]
        far = [e for c in both if topo.chip(c) != topo.chip(src) for e in topo.engines(src, c)]
        e = topo.engines(src, dst)
        return e if topo.chip(src) != topo.chip(dst) else [x for x in e if x not in far]

    def send(dst, out, src, r, sem):
        e = engines(core, dst); rid, pid = topo.addr(dst)[:2]; m = sum(1 << x for x in e)
        op("g", lambda: g.remote_dma(out, src, T.sem["r_" + sem], T.sem.sent, pid, rid, m), r=r, sem="sent", cnt=len(e), inc=False)

    def arrives(src, name, sem):
        op("r", None, w=[name], sem="r_" + sem, cnt=len(engines(src, core)))

    def dma(q, out, in_, sem, r=(), w=()):
        op(q, lambda: (g.sync if q == "s" else g.scalar).dma_start(out, in_), r=r, w=w, sem="d_" + sem)

    def load(q, name, src): dma(q, T[name][:, :], src[:, :], name, w=[name])
    def store(name, dst): dma("s", T[dst][:, :], T[name][:, 0:W], dst, r=[name])
    def ind(win, lst, wide=W): return T[win][:, 0:wide].indirect(lst)
    def tt(out, a, b, o, r, w): op("v", lambda: V.tensor_tensor(out, a, b, o), r, w)
    def ts(out, a, s, o, r, w): op("v", lambda: V.tensor_scalar(out, a, s, None, o), r, w)
    def ts2(out, a, s, o, s2, o2, r, w): op("v", lambda: V.tensor_scalar(out, a, s, s2, o, o2), r, w)
    def cp(out, a, r, w): op("v", lambda: V.tensor_copy(out, a), r, w)
    def ms(out, v, w): op("v", lambda: V.memset(out, v), (), w)
    def act(out, a, f, r, w, **kw): op("a", lambda: A.activation(out, a, f, **kw), r, w)
    def iota(out, pat, base, cm, w, **kw): op("g", lambda: g.iota(out, pat, base, cm, **kw), (), w)
    def choose(out, a, pat, o, fill, cm, r, w): op("g", lambda: g.affine_select(out, a, pat, o, fill, 0, cm), r, w)
    def keep(out, pat, o, fill, base, cm, w): op("g", lambda: g.affine_select(out, out, pat, o, fill, base, cm), w, w)
    def mm(out, l, x, st, sp, r, w): op("p", lambda: P.matmul(out, l, x, st, sp), r, w)

    def tolist(bank, col, z, zoff, src, cols, st=True, sp=True, r=None, step=1):
        def f():
            for i in range(16):
                o = zoff + 15 - i
                ins = P.matmul(T[bank][:, col:col + step * cols // 16:step], T[z][:, o:o + 128], T[src][:, i:cols:16], st and i == 0, sp and i == 15)
            return ins
        op("p", f, [z] + (r or [src]), [bank])

    def band(off, q0, q1, wt, w):
        o = T.zz[:, off + 15 + 16 * q0:off + 16 * q1:16]
        keep(o, [[16, q1 - q0]], ALU.is_gt, wt, 0, -1, w); keep(o, [[16, q1 - q0]], ALU.is_ge, 0.0, 15, -1, w)

    def onward(off, wt):
        band(off, 1, 8, wt, ["zu"]); keep(T.zz[:, off + 15:off + 16], [[1, 1]], ALU.is_gt, wt, 112, -1, ["zu"])

    def diagonal(i, v):
        choose(T.idn[:, 128 * i:128 * i + 128], T.zero[:, 0:128], [[-1, 128]], ALU.not_equal, v, 1, ["zero"], ["idn%d" % i])

    fl = {"allow_small_or_imprecise_dtypes": True}
    ZB, ZO, ZC, ZU = 0, 144, 288, 432
    FINE = 288
    ZX = (256, 0, 384, 128, 512)
    cw, cb, cg, cz = (OPT[x] for x in ("cw", "cb", "cg", "cz"))
    ms(T.one[:, :], 1.0, ["one"]); ms(T.tw[:, 0:cw], 0, ["tw"]); ms(T.zz[:, 0:656], 0.0, ["zz"])
    iota(T.jc[:, :], [[1, 32], [0, 16]], 32, 0, ["jc"], **fl); iota(T.jlo[:, :], [[0, 2], [1, 16]], 32, 0, ["jlo"], **fl)
    iota(T.tw[:, cw:W], [[0, W - cw]], 0, 0, ["tw1"])
    load("a", "wki", T.wk); load("s", "bh", T.b0)
    act(T.dd[:, 0:16], T.one[:, :], AF.Silu, ["one"], ["dd1"])
    load("s", "rb", T.rec)
    for rows, src in ((T.tw[0:128:8, :], T.hop), (T.tw[4:128:16, :], T.dn), (T.tw[12:128:16, :], T.up)):
        dma("s", rows, src[:, :], "tw", w=["tw", "tw1"])
    load("s", "wb", T.w)
    dma("s", T.ths[:, 0:1], T.th[:, :], "ths", w=["ths"])
    for lo, hi, a in SHIFT: dma("s", T.ths[lo:hi, 1:2], T.th[a:a + hi - lo, :], "ths", w=["ths"])
    for lo, hi, a in SHIFT: dma("s", T.wu[lo:hi, :], T.w[a:a + hi - lo, :], "wu", w=["wu"])
    iota(T.zi[:, 0:40], [[-16, 5], [-64, 8]], 528, 4, ["zi"]); iota(T.zi[:, 40:72], [[1, 32]], 0, 32, ["zj"])
    act(T.zero[:, :], T.jc[:, :], AF.Copy, ["jc"], ["zero"], scale=0.0)
    for x in ("jlo", "jc"): act(T[x][:, :], T[x][:, :], AF.Copy, [x], [x], scale=2 * TAG)
    dma("s", T.jc[1:128:16, :], T.jlo[:, :], "jc", r=["jlo"], w=["jc"])
    cp(T.dq0[:, :], T.wki[:, :], ["wki"], ["dq0"]); cp(T.zt[:, :], T.zz[:, 0:656], ["zz"], ["zt"])
    choose(T.b[:, W - cg:W], T.bh[:, W - cg:W], [[0, cg]], ALU.is_ge, 0.0, 0, ["bh"], ["b2"])
    cp(T.b[:, cb:W - cg], T.bh[:, cb:W - cg], ["bh"], ["b1"])
    ts(T.zi[:, :], T.zi[:, :], 511, ALU.bitwise_and, ["zi", "zj"], ["zi", "zj"])
    ts(T.zt[:, 15:640:16], T.zi[:, 0:40], 0.0, ALU.is_equal, ["zi", "zt"], ["zt"])
    band(ZO, 0, 8, -2.0 ** 15, ["zz"]); band(ZC, 0, 8, -SP / 2, ["zz"])
    diagonal(0, 1.0); iota(T.cst[:, 32:64], [[0, 32]], 8 * SP, 0, ["cs8"], **fl)
    for a in range(cz, W, K): dma("s", T.c0[:, a:min(a + K, W)], T.zero[:, 0:min(K, W - a)], "c0", r=["zero"], w=["c0"])
    iota(T.c0[:, 0:cz], [[0, cz]], 0, 0, ["c0g"], **fl)

    def bounds():
        for j in range(2): act(T.tq[:, 8 + j:9 + j], T.ths[:, j:j + 1], AF.Square, ["ths", "scale"], ["bound%d" % j], scale=T.tq[:, 2 + j:3 + j])
        act(T.tq[:, 10:12], T.tq[:, 8:10], AF.Identity, ["bound0", "bound1"], ["nbound"], scale=-1.0, bias=-2.0 ** -24)

    def later():
        onward(ZU, -SP / 2)
        choose(T.eps[:, :], T.zero[:, :], [[0, K]], ALU.is_gt, 2 * EPS, 0, ["zero"], ["eps"])
        diagonal(1, -1.0)
        for row, wt in ((0, 16.0), (1, 1.0)): keep(T.zz[:, ZB + 15:ZB + 128:16], [[-16, 8]], ALU.not_equal, wt, -row, 1, ["zb"])
        iota(T.dd[:, 528:560], [[0, 32]], -1, 0, ["dd2"], **fl)
        iota(T.pick[:, :], [[0, 96]], 0, 0, ["pick"], **fl)
        op("g", lambda: g.dma_start(T.c1[:, 0:K], T.zero[:, :]), ["zero"], ["c1z"], "d_c1")
        iota(T.c1[:, K:W], [[0, W - K]], 0, 0, ["c1"], **fl)

    def join(a, e): op("g", lambda: g.dma_start(T.c1[:, a:e], T.c0[:, a:e], accum_op=ALU.add), ["c0", "c1"], ["c1"], "d_add")

    for s in range(RO):
        last = s == RO - 1
        dq, xl, xu, xd, h, hu, hd, dl, sm = ("%s%d" % (x, s) for x in ("dq", "xl", "xu", "xd", "h", "hu", "hd", "dl", "sm"))
        c = "c%d" % min(s, 1)
        D = T[dq][:, :]
        DF, df = (T["sm%d" % (s - 1)][:, 2:96:3], "sm%d" % (s - 1)) if s else (T.df[:, :], "df")
        X = [(xl + "a", h), (xl + "b", h), (xu, hu), (xd, hd)]
        acts, pcs, late = (OPT[x][s] for x in ("act", "pc", "late"))

        def lst(k, a=0, e=K):
            t, o = ((xl, 96), (xl, 64), (xu, 0), (xd, 0), (xu, 32))[k]
            return T[t][:, o + a // 16:o + e // 16]
        def lists(bank, which):
            for i in which: tolist(bank, 32 * i, "zt", ZX[i], "tg", K)
        def cast(bank, a, e, w): cp(T[xl][:, 32 * a:32 * e], T[bank][:, 32 * a:32 * e], [bank], [xl + w])
        def hand(a, e, w):
            if a <= 1 < e: send(up, T[xu][:, 0:32], T[xl][:, 32:64], [xl + w], xu)
            if a == 0: send(dn, T[xd][:, :], T[xl][:, 0:32], [xl + w], hd)
        def uplist(): cast("pv", 4, 5, "u"); send(up, T[xu][:, 32:64], T[xl][:, 128:160], [xl + "u"], hu)
        def grad(k, a=0, e=K, p=""):
            wt, l = ("wu", 4) if k == 2 else ("wb", k)
            tt(T["g%d" % k][:, a:e], ind(wt, lst(l, a, e)), T[X[k][1]][:, a:e], ALU.mult, [wt, X[k][0] + "w" * (k == 2), X[k][1]], ["g%d" % k + p])
            if k == 2:
                for lo, hi, a in SHIFT: dma("s", T.gu[a:a + hi - lo, :], T.g2[lo:hi, :], "gu%d" % s, r=["g2"], w=["gu"])
        def size(k, a=0, e=K, p=""):
            ab = "ab%d" % (k % 2); j = 2 + int(k == 2)
            if s or k: act(T[ab][:, a:e], T["g%d" % k][:, a:e], AF.Square, ["g%d" % k + p, "scale"], [ab + p], scale=T.tq[:, j:j + 1])
            else: act(T[ab][:, a:e], T.g0[:, a:e], AF.Abs, ["g0" + p], [ab + p])
        def over(k, q, a=0, e=K, p=""):
            ab = "ab%d" % (k % 2); big = "big%d" % (k % 2); j = int(k == 2)
            z = min(max(acts[k], a), e)
            if z > a and q == "a": act(T[big][:, a:z], T[ab][:, a:z], AF.Sign, [ab + p, "nbound"], [big + "a"], bias=T.tq[:, 10 + j:11 + j])
            bound, r = (T.tq[:, 8 + j:9 + j], "bound%d" % j) if s or k else (T.ths[:, 0:1], "ths")
            if z < e and q == "v": ts2(T[big][:, z:e], T[ab][:, z:e], bound, ALU.is_gt, 2.0, ALU.mult, [ab + p, r], [big + p])
        def place(k):
            bank = "pd%d" % (k % 2); i = 2 * int(last and k > 0); z = acts[k] // 16
            mm(T[bank][:, 0:32], T.idn[:, 128 * i:128 * i + 128], T.cst[:, 0:32], True, False, ["idn%d" % i, "cst"], [bank])
            if z < 32: mm(T[bank][:, z:32], T.idn[:, 128 * i:128 * i + 128], T.cst[:, 32 + z:64], False, False, ["idn%d" % i, "cs8"], [bank])
        def count(k, sp=False):
            big = "big%d" % (k % 2)
            tolist("pd%d" % (k % 2), 0, "zz", (FINE if last and k else 0) + (ZU if k == 2 else ZC), big, K, False, sp, [big, big + "a"] + ["zu"] * (k == 2 or last))
        def old(k, q):
            e = K - OPT["av"][s][k]
            if q == "a": act(T.ao[:, 0:e], ind("b", lst(k, 0, e)), AF.Abs, ["b", X[k][0]], ["ao"], scale=2.0 ** (95 if last and k else 90))
            elif e < K: ts(T.ao[:, e:K], ind("b", lst(k, e, K)), 0.0, ALU.not_equal, ["b", X[k][0]], ["aov"])
        def empty(k, sp=True): tolist("pd%d" % (k % 2), 0, "zz", ZO, "ao", K, False, sp, ["ao", "aov"])
        def base(k): act(T.bo[:, :], ind("b", lst(k)), AF.Copy, ["b", X[k][0]], ["bo"])
        def aim(k):
            bank = "pd%d" % (k % 2)
            if last and k:
                ts2(T.aim[:, :], T[bank][:, 0:32], 0.0, ALU.max, 1 / U, ALU.mult, [bank], ["aim"])
                tt(T.to[:, :], T.aim[:, :], lst(k), ALU.max, ["aim", X[k][0]], ["to"])
            else: tt(T.to[:, :], T[bank][:, 0:32], lst(k), ALU.max, [bank, X[k][0]], ["to"])
        def put(k):
            gk = "gu" if k == 2 else "g%d" % k
            tt(ind("b", T.to[:, :], 9 * SP), T.bo[:, :], T[gk][:, :], ALU.add, ["bo", gk, "to"], ["b"])
        def beside(k):
            if last:
                if k == 1: act(T.cd[:, :], ind(c, D), AF.Copy, [c, dq], ["cd"])
            elif k < 2:
                a, e = (0, OPT["marks"][s], 32)[k:k + 2]
                act(ind(c, T[xl][:, 96 + a:96 + e]), T.jc[:, 16 * a:16 * e], AF.Silu, [xl + "a", "jc", c, "c0g"] + ["c1z"] * s, [c])
            else:
                act(ind(c, T[dq][:, pcs[1] // 16:32]), T.eps[:, pcs[1]:K], AF.Silu, ["eps", dq, c], [c])
        def putc(i):
            a, e = pcs[i:i + 2]; o = ind(c, T[dq][:, a // 16:e // 16])
            if last: tt(o, T.cd[:, a:e], T[dl][:, a:e], ALU.add, ["cd", dl, dq], [c])
            else: ts2(o, T[dl][:, a:e], 1.0, ALU.mult, EPS, ALU.add, [dl, dq, c], [c])
            if e == K and s == 1: join(0, OPT["join"])
            if e == K and last: store(c, "yc")
        def tables():
            cp(T.tg[:, :], ind("tw", D), ["tw", dq], ["tg"])
            for bank, i in (("pv", 4), ("px", 3)) if last else (("px", 3), ("pv", 4)): lists(bank, [i])
            lists("pl", range(2, late - 1, -1))
        def moves():
            for i, col, step in ((2, 0, 3), (3, 96, 1)):
                tolist("pe", col, "zt", ZX[i], "tg", K, True, False, step=step)
                mm(T.pe[:, col:col + 32 * step:step], T.idn[:, 128:256], DF, False, True, ["idn1", df], ["pe"])

        src = "b" if s else "bh"
        e = K - OPT["nv"][s]
        act(T.nb[:, 0:e], ind(src, T[dq][:, 0:e // 16]), AF.Copy, [src, dq], ["nb"], scale=-1.0)
        if e < K: ts(T.nb[:, e:K], ind(src, T[dq][:, e // 16:32]), -1.0, ALU.mult, [src, dq], ["nbv"])
        if s: tables()
        else: act(T.b[:, 0:cb], T.bh[:, 0:cb], AF.Copy, ["bh"], ["b"])
        act(ind("b", D), T.zero[:, :], AF.Silu, ["zero", dq, "b", "b1", "b2"], ["b"])
        tt(T[dl][:, :], ind("rb", D), T.nb[:, :], ALU.mult, ["rb", dq, "nb", "nbv"], [dl])
        if not s: tables()
        if s == 1: cast("px", 3, 4, "a")
        if last: uplist()
        tt(T[h][:, :], ind("wb", D), T[dl][:, :], ALU.mult, ["wb", dq, dl], [h])
        if s != 1: cast("px", 3, 4, "a")
        send(up, T[hu][:, :], T[h][:, :], [h], hu)
        if s == 1: uplist()
        if s: send(dn, T[hd][:, :], T[h][:, :], [h], hd)
        old(0, "a")
        grad(0, *halves[0])
        if not s: uplist(); send(dn, T[hd][:, :], T[h][:, :], [h], hd)
        grad(0, *halves[1])
        if not s:
            op("v", lambda: V.reciprocal(T.tq[:, 0:2], T.ths[:, :]), ["ths"], ["tq"])
            ts(T.cst[:, 0:32], T.zi[:, 40:72], float(W), ALU.add, ["zj"], ["cst"])
            ts(T.tq[:, 2:4], T.tq[:, 0:2], 1 - 2.0 ** -20, ALU.mult, ["tq"], ["scale"])
        place(0)
        cast("pl", late, 3, "b"); hand(late, 3, "b")
        if last: join(OPT["join"], W)
        old(0, "v"); empty(0, False)
        for x in halves: size(0, *x)
        over(0, "a", *halves[0])
        if not s: bounds()
        for x in halves: over(0, "v", *x)
        count(0, True)
        lists("pe", range(late - 1, -1, -1))
        grad(1); base(0)
        if s == 1:
            iota(T.zz[:, 656:864], [[0, 208]], 0, 0, ["zu"], **fl)
            band(FINE + ZC, 0, 8, -SP / 2 * U, ["zu"]); onward(FINE + ZU, -SP / 2 * U)
            diagonal(2, U)
        arrives(dn, hu, hu); arrives(dn, xu + "w", hu); arrives(dn, xu, xu); arrives(up, hd, hd); arrives(up, xd, hd)
        aim(0)
        for k in range(3):
            size(k + 1); put(k)
            if not k: cast("pe", 0, late, "c"); hand(0, late, "c")
            if not k and not s: later()
            place(k + 1); beside(k); over(k + 1, "a")
            old(k + 1, "a")
            over(k + 1, "v"); count(k + 1)
            old(k + 1, "v"); empty(k + 1); base(k + 1)
            if k < 2: grad(k + 2)
            if last and k: putc(k - 1)
            if not last and k == 2: putc(0)
            aim(k + 1)
        if not s: cp(T.df[:, :], T.wki[:, :], ["wki"], ["df"])
        if not last: moves()
        put(3)
        if last:
            store("b", "yb")
            break
        act(T.mg[:, :], ind(c, T[xl][:, 64:128]), AF.Abs, [c, xl + "a", xl + "b"], ["mg"], scale=1 / TAG)
        tolist("pl", 0, "zz", ZB, "mg", 2 * K, r=["mg", "zb"])
        act(T.ab0[:, :], ind("b", lst(0)), AF.Abs, ["b", X[0][0]], ["ab0"])
        cp(T.ab1[:, :], ind("b", lst(1)), ["b", X[1][0]], ["ab1"])
        putc(1)
        ts(T.free[:, :], T.pl[:, 32:64], 2.0 * W, ALU.is_lt, ["pl"], ["free"])
        ts2(T.lk[:, :], T.pl[:, 0:32], -528.0, ALU.add, 559.0, ALU.min, ["pl"], ["lk"])
        for (a, e, p), u in zip(halves, ("pc0", "pc1")): act(T[u][:, a:e], T.ab1[:, a:e], AF.Abs, ["ab1"], [u])
        tt(T.pe[:, 1:96:3], T.free[:, :], T.pe[:, 96:128], ALU.mult, ["free", "pe"], ["pe"])
        for (a, e, p), u in zip(halves, ("pc0", "pc1")):
            tt(T.dd[:, 16 + a:16 + e], T[u][:, a:e], T.ab0[:, a:e], ALU.subtract, [u, "ab0" + p], ["dd" + p])
        kv, sv = OPT["kv"], K - OPT["sv"]; eps = 2.0 ** -116
        act(T.sg[:, 0:sv], T.dd[:, 16:16 + sv], AF.Sign, ["ddh0"], ["sgh"])
        act(T.sg[:, K + kv:2 * K], ind("dd", T.lk[:, kv // 16:32], 560), AF.Sign, ["dd", "dd1", "dd2", "lk"], ["sga"])
        tt(T.pe[:, 2:96:3], DF, T.pe[:, 1:96:3], ALU.add, [df, "pe"], ["pe"])
        ts2(T.sg[:, sv:K], T.dd[:, 16 + sv:16 + K], eps, ALU.min, -eps, ALU.max, ["dd"], ["sgo"])
        ts2(T.sg[:, K:K + kv], ind("dd", T.lk[:, 0:kv // 16], 560), eps, ALU.min, -eps, ALU.max, ["dd", "dd1", "dd2", "lk"], ["sgv"])
        tolist("pv", 0, "zz", ZO, "sg", 2 * K, r=["sga", "sgo", "sgv", "sgh"])
        putc(2)
        ts2(T.pick[:, 1:96:3], T.pv[:, 32:64], 0.0, ALU.is_lt, -1.0, ALU.mult, ["pv", "pick"], ["s2"])
        ts2(T.pick[:, 2:96:3], T.pv[:, 0:32], 0.0, ALU.is_lt, -1.0, ALU.mult, ["pv", "pick"], ["s3"])
        def scan(o=T[sm][:, :]): op("v", lambda: V.tensor_tensor_scan(o, T.pick[:, :], T.pe[:, 0:96], 0.0, ALU.mult, ALU.add), ["s2", "s3", "pe"], [sm])
        scan()
        cp(T["dq%d" % (s + 1)][:, :], T[sm][:, 2:96:3], [sm], ["dq%d" % (s + 1)])
    emit(g, T, ops)
